import numpy as np
import ml_dtypes


def mxq(x, axis, fmt="e4m3"):
    dtype, down = {"e4m3": (ml_dtypes.float8_e4m3fn, 7), "e5m2": (ml_dtypes.float8_e5m2, 14)}[fmt]
    v = np.moveaxis(np.asarray(x, np.float32).astype(ml_dtypes.bfloat16).astype(np.float64), axis, -1)
    blocks = v.reshape(v.shape[:-1] + (-1, 32))
    amax = np.abs(blocks).max(-1, keepdims=True)
    byte = np.maximum(np.where(amax > 0, np.frexp(amax)[1] - 1 + 127, 0) - down, 1)
    scale = np.exp2(byte - 127.0)
    codes = (blocks / scale).astype(np.float32).astype(dtype).astype(np.float64)
    return np.moveaxis((codes * scale).reshape(v.shape), -1, axis)


WIDE = False


def mx_kscale(k):
    if not WIDE:
        return np.ones(k)
    levels = np.array([24, -24, 12, -12, 0])
    if k % 512:
        return np.exp2(np.random.permutation(np.resize(levels, k // 32))).repeat(32)
    a = np.empty((k // 512, 16))
    for p in range(k // 512):
        a[p, :8] = np.random.permutation(np.resize(levels, 8))
        for g in range(8):
            far = levels[np.abs(levels - a[p, g]) >= 10]
            a[p, g + 8] = far[np.random.randint(len(far))]
    return np.exp2(a.ravel()).repeat(32)


def f64(x):
    return np.asarray(x).astype(np.float64)


def striped(idx):
    return np.tile(idx.reshape(-1, 16).T, (8, 1)).astype(np.uint16)


def unstriped(offs):
    return offs[:16].T.reshape(-1).astype(np.int64)


E2M1 = np.array([0.0, 0.5, 1.0, 1.5, 2.0, 3.0, 4.0, 6.0, -0.0, -0.5, -1.0, -1.5, -2.0, -3.0, -4.0, -6.0])


def pack_weight(w, fmt):
    k, n = w.shape
    w = f64(np.asarray(w, np.float32).astype(ml_dtypes.bfloat16)).reshape(k // 32, 32, n)
    amax = np.abs(w).max(1)
    if fmt == "e4m3":
        byte = np.frexp(amax)[1] - 1 + 127 - 7
    else:
        mant, ex = np.frexp(amax / 6.0)
        byte = np.where(mant > 0.5, ex, ex - 1) + 127
    byte = np.clip(np.where(amax > 0, byte, 1), 1, 254)
    scaled = (w * np.exp2(127.0 - byte)[:, None, :]).reshape(k, n).astype(np.float32)
    by_word = np.ascontiguousarray(scaled.reshape(k // 512, 128, 4, n).transpose(0, 1, 3, 2))
    if fmt == "e4m3":
        words = by_word.astype(ml_dtypes.float8_e4m3fn).view(np.uint8)
    else:
        c = by_word.astype(ml_dtypes.float4_e2m1fn).view(np.uint8) & 0xF
        words = (c[..., 0::2] | (c[..., 1::2] << 4)).reshape(k // 512, 128, 2 * n)
    return np.ascontiguousarray(words), np.ascontiguousarray(byte.astype(np.uint8).reshape(k // 512, 16, n))


def unpack_weight(words, scales, fmt):
    g, _, n = scales.shape
    words = np.ascontiguousarray(words).reshape(g, 128, n, -1)
    if fmt == "e4m3":
        vals = words.view(ml_dtypes.float8_e4m3fn).astype(np.float64)
    else:
        nib = np.empty((g, 128, n, 4), np.uint8)
        nib[..., 0::2] = words & 0xF
        nib[..., 1::2] = words >> 4
        vals = E2M1[nib]
    vals = vals * np.repeat(np.exp2(scales.astype(np.float64) - 127.0), 8, axis=1)[..., None]
    return vals.transpose(0, 1, 3, 2).reshape(g * 512, n)


def pack_table4(v):
    words, scales = pack_weight(v, "e2m1")
    g, t = words.shape[0] // 2, v.shape[1]
    return np.ascontiguousarray(words.reshape(g, 2, 128, t, 2).transpose(0, 2, 3, 1, 4).reshape(g, 128, t, 4)), scales


def unpack_table4(words, scales):
    g, _, t, _ = words.shape
    return unpack_weight(words.reshape(g, 128, t, 2, 2).transpose(0, 3, 1, 2, 4).reshape(2 * g, 128, 2 * t), scales, "e2m1")


def planes(y):
    n, m = y.shape
    v = y.astype(np.float32).astype(ml_dtypes.bfloat16).astype(np.float64).reshape(n // 32, 32, m)
    top = np.abs(v).max(1)
    byte = np.clip(np.where(top > 0, np.frexp(top)[1] - 1 + 127 - 7, 1), 1, 254)
    codes = (v * np.exp2(127.0 - byte)[:, None, :]).reshape(n, m).astype(np.float32).astype(ml_dtypes.float8_e4m3fn).view(np.uint8)
    words = codes.reshape(n // 512, 128, 4, m).transpose(0, 1, 3, 2)
    return np.ascontiguousarray(words), np.ascontiguousarray(byte.astype(np.uint8).reshape(n // 512, 16, m))


K, R, N, T, J = 1024, 1024, 512, 2048, 1024


def setup_inputs():
    n = np.random.standard_normal
    s = mx_kscale(K)[:, None]
    u = mx_kscale(R)[:, None]
    p_tab = pack_table4(n((K, T)) * s)
    p_ws = pack_weight(n((K, R)) / np.sqrt(2 * K) / s, "e2m1")
    p_wt = pack_weight(n((K, R)) / np.sqrt(2 * K) / s, "e4m3")
    p_wd = pack_weight(n((R, N)) / np.sqrt(R) / u, "e2m1")
    return {
        "tab_words": p_tab[0],
        "tab_scales": p_tab[1],
        "ws_words": p_ws[0],
        "ws_scales": p_ws[1],
        "wt_words": p_wt[0],
        "wt_scales": p_wt[1],
        "sm": (np.random.uniform(0.5, 2.0, R) * u[:, 0]).astype(np.float32),
        "wd_words": p_wd[0],
        "wd_scales": p_wd[1],
        "gT": (n((N, T))).astype(np.float32),
        "wgo": np.tile(np.random.uniform(0.5, 2.0, J), (128, 1)).astype(np.float32),
        "offs": striped(np.random.permutation(T)[:J]),
        "offs2": striped(np.random.permutation(T)[:J]),
    }


def reference(tab_words, tab_scales, ws_words, ws_scales, wt_words, wt_scales, sm, wd_words, wd_scales, gT, wgo, offs, offs2):
    idx = unstriped(offs)
    idx2 = unstriped(offs2)
    tab_ = unpack_table4(tab_words, tab_scales)[:, idx]
    tabb_ = unpack_table4(tab_words, tab_scales)[:, idx2]
    ws_ = unpack_weight(ws_words, ws_scales, "e2m1")
    wt_ = unpack_weight(wt_words, wt_scales, "e4m3")
    a = ws_.T @ tab_ + wt_.T @ tabb_
    h = f64(sm)[:, None] * np.tanh(a)
    h_ = mxq(h, 0, "e4m3")
    wd_ = unpack_weight(wd_words, wd_scales, "e2m1")
    y = wd_.T @ h_
    out = np.zeros((N, T))
    out[:, idx2] = f64(wgo)[0] * (y * f64(gT)[:, idx])
    return (out,) + planes(out)

@@ -1,0 +1,259 @@
+from contextlib import ExitStack
+
+import concourse.mybir as mybir
+from concourse.masks import make_identity
+
+K, R, N, T, J = 1024, 1024, 512, 2048, 1024
+FLOPS = 2 * J * (2 * K * R + R * N)
+
+F32 = mybir.dt.float32
+BF16 = mybir.dt.bfloat16
+I32 = mybir.dt.int32
+U32 = mybir.dt.uint32
+U16 = mybir.dt.uint16
+U8 = mybir.dt.uint8
+FP8X4 = mybir.dt.float8_e4m3fn_x4
+FP4X4 = mybir.dt.float4_e2m1fn_x4
+ACT = mybir.ActivationFunctionType
+MULT = mybir.AluOpType.mult
+
+P = 128
+PACK = 4
+BANK = 512
+CH = 256
+NCH = J // CH
+JT = CH // P
+OC = CH // 16
+PIECE = 512
+VCOLS = 256
+LIVE = 24
+
+
+def tile_list_msg_tanh_gateP_kernel(
+    tc, tab_words, tab_scales, ws_words, ws_scales, wt_words, wt_scales, sm,
+    wd_words, wd_scales, gT, wgo, offs, offs2, out_0, out_1, out_2,
+):
+    nc = tc.nc
+    with ExitStack() as ctx:
+        keep = ctx.enter_context(tc.tile_pool(name="keep", bufs=1))
+        ring = ctx.enter_context(tc.tile_pool(name="ring", bufs=2))
+        psum = ctx.enter_context(tc.psum_pool(name="psum", bufs=1))
+
+        src_list = keep.tile([P, J // 16], U16, name="src_list")
+        dst_list = keep.tile([P, J // 16], U16, name="dst_list")
+        lists = (src_list, dst_list)
+
+        tab_sc = keep.tile([P, T // 4], I32, name="tab_sc", tag="big", align_bytes=64)
+        for q in range(4):
+            nc.vector.memset(tab_sc[32 * q : 32 * q + LIVE, :], 0)
+        ws_sc = keep.tile([P, 2, R], U8, name="ws_sc", align_bytes=64)
+        wt_sc = keep.tile([P, 2, R], U8, name="wt_sc", align_bytes=64)
+        nc.gpsimd.memset(ws_sc[:].rearrange("p a r -> p (a r)").bitcast(I32), 0)
+        nc.gpsimd.memset(wt_sc[:].rearrange("p a r -> p (a r)").bitcast(I32), 0)
+        nc.sync.dma_start(src_list[:], offs)
+        nc.sync.dma_start(dst_list[:], offs2)
+        for q in range(4):
+            nc.sync.dma_start(
+                tab_sc[32 * q + LIVE : 32 * q + 32, :],
+                tab_scales[:, 4 * q : 4 * q + 4, :].bitcast(I32),
+            )
+        tab_w = keep.tile([P, T], I32, name="tab_w", align_bytes=64)
+        nc.sync.dma_start(tab_w[:], tab_words[0].rearrange("p t i -> p (t i)").bitcast(I32))
+        ws_w = keep.tile([P, 2, 2 * R], U8, name="ws_w", align_bytes=64)
+        nc.sync.dma_start(ws_w[:].bitcast(I32), ws_words.rearrange("a p c -> p a c").bitcast(I32))
+        for plane, scales, queue in ((ws_sc, ws_scales, nc.sync), (wt_sc, wt_scales, nc.sync)):
+            for q in range(4):
+                queue.dma_start(
+                    plane[32 * q : 32 * q + 4].bitcast(I32),
+                    scales[:, 4 * q : 4 * q + 4, :].rearrange("a q r -> q a r").bitcast(I32),
+                )
+        w_sc = (ws_sc, wt_sc)
+        wt_w = keep.tile([P, 2, R], I32, name="wt_w", align_bytes=64)
+        nc.sync.dma_start(wt_w[:], wt_words.rearrange("a p r i -> p a (r i)").bitcast(I32))
+
+        HALF = J // 2
+        v_sc = [keep.tile([P, 2, 2, HALF], U8, name="v_sc_%d" % h, align_bytes=64) for h in range(2)]
+        for h in range(2):
+            nc.vector.memset(v_sc[h][:].rearrange("p a l j -> p (a l j)").bitcast(I32), 0)
+        ident = keep.tile([P, P], F32, name="ident")
+        make_identity(nc, ident[:])
+        sm_t = keep.tile([P, 2, PACK], F32, name="sm_t")
+        nc.gpsimd.dma_start(sm_t[:], sm.rearrange("(b p t) -> p b t", b=2, t=PACK))
+        pages = [keep.tile([P, T], F32, name="page%d" % t) for t in range(PACK)]
+        wd_sc = keep.tile([P, 2, N], U8, name="wd_sc", align_bytes=64)
+        for t in range(PACK):
+            nc.gpsimd.memset(pages[t][:], 0.0)
+            if t == 1:
+                nc.gpsimd.memset(wd_sc[:].rearrange("p a n -> p (a n)").bitcast(I32), 0)
+
+        v_w = []
+
+        def gather_scales(h, tag):
+            got = keep.tile([P, 2, HALF], U8, name="v_sc0", tag=tag, align_bytes=64)
+            for l in range(2):
+                nc.vector.tensor_copy(got[:, l, :], tab_sc[:].bitcast(U8).indirect(lists[l][:, h * 2 * OC : (h + 1) * 2 * OC]))
+            for a in range(2):
+                shift = LIVE + 4 * a
+                (nc.scalar if h == 0 else nc.sync).dma_start(
+                    v_sc[h][: P - shift, a].rearrange("p l j -> p (l j)").bitcast(I32),
+                    got[shift:].rearrange("p l j -> p (l j)").bitcast(I32),
+                )
+
+        def gather_words(c):
+            both = keep.tile([P, 2, CH], U32, name="both", tag="both%d" % c, align_bytes=64)
+            for l in range(2):
+                nc.vector.tensor_copy(
+                    both[:, l, :], tab_w[:].bitcast(U32).indirect(lists[l][:, c * OC : (c + 1) * OC])
+                )
+            parted = keep.tile([P, 2, 2, 2 * CH], U8, name="parted%d" % c, align_bytes=64)
+            nc.vector.tensor_copy(
+                parted[:].bitcast(U16),
+                both[:].bitcast(U16).rearrange("p l (j d) -> p l d j", d=2),
+            )
+            v_w.append(parted)
+
+        gather_scales(0, "v_sc0")
+        gather_words(0)
+        gather_words(1)
+        gather_scales(1, "both0")
+        gather_words(2)
+        gather_words(3)
+
+        gates = keep.tile([P, PACK * T], F32, name="gates", tag="big", align_bytes=64)
+        gT_rows = gT.rearrange("(p t) c -> p t c", t=PACK)
+        wd_w = keep.tile([P, 2, 2 * N], U8, name="wd_w", tag="both1", align_bytes=64)
+        nc.sync.dma_start(wd_w[:].bitcast(I32), wd_words.rearrange("a p c -> p a c").bitcast(I32))
+        for q in range(4):
+            nc.sync.dma_start(
+                wd_sc[32 * q : 32 * q + 4].bitcast(I32),
+                wd_scales[:, 4 * q : 4 * q + 4, :].rearrange("a q n -> q a n").bitcast(I32),
+            )
+        wg = keep.tile([P, J // P], F32, name="wg", tag="both2", align_bytes=64)
+        with nc.allow_non_contiguous_dma(reason="one edge weight a partition"):
+            nc.sync.dma_start(wg[:], wgo[0].rearrange("(c p) -> p c", p=P))
+        for t in range(PACK):
+            nc.sync.dma_start(gates[:, t * T : (t + 1) * T], gT_rows[:, t, :])
+
+        h_q = {}
+        picked = {}
+        msgs = {}
+
+        def first_stage(c):
+            th = []
+            for jt in range(JT):
+                th_t = ring.tile([P, 2, PACK, P], F32, name="th", bufs=3)
+                h = c // 2
+                jc = slice((c % 2) * CH + jt * P, (c % 2) * CH + (jt + 1) * P)
+                jw = slice(2 * jt * P, 2 * (jt + 1) * P)
+                for b in range(2):
+                    acc = psum.tile([P, BANK], F32, name="acc", bufs=3)
+                    rc = slice(b * BANK, (b + 1) * BANK)
+                    for a in range(2):
+                        nc.tensor.matmul_mx(
+                            acc[:], lhsT=v_w[c][:, 0, a, jw].bitcast(FP4X4), lhsT_scale=v_sc[h][:, a, 0, jc],
+                            rhs=ws_w[:, a, 2 * b * BANK : 2 * (b + 1) * BANK].bitcast(FP4X4),
+                            rhs_scale=w_sc[0][:, a, rc], start=(a == 0), stop=False,
+                        )
+                        nc.tensor.matmul_mx(
+                            acc[:], lhsT=v_w[c][:, 1, a, jw].bitcast(FP4X4), lhsT_scale=v_sc[h][:, a, 1, jc],
+                            rhs=wt_w[:, a, rc].bitcast(FP8X4),
+                            rhs_scale=w_sc[1][:, a, rc], start=False, stop=(a == 1),
+                        )
+                    nc.scalar.activation(th_t[:, b], acc[:].rearrange("p (m t) -> p t m", t=PACK), ACT.Tanh)
+                th.append(th_t)
+            h_rows = ring.tile([P, 2, PACK, CH], BF16, name="h_rows", align_bytes=64)
+            for b in range(2):
+                for u in range(2):
+                    turned = psum.tile([P, 2, CH], F32, name="turned", bufs=3)
+                    for e in range(2):
+                        for jt in range(JT):
+                            nc.tensor.transpose(turned[:, e, jt * P : (jt + 1) * P], th[jt][:, b, 2 * u + e, :], ident[:])
+                    for e in range(2):
+                        t = 2 * u + e
+                        nc.scalar.activation(h_rows[:, b, t, :], turned[:, e, :], ACT.Copy, scale=sm_t[:, b, t : t + 1])
+            h_words = ring.tile([P, 2, CH, PACK], BF16, name="h_words", align_bytes=64)
+            for b in range(2):
+                (nc.vector.tensor_copy if b == 0 else nc.scalar.copy)(
+                    h_words[:, b].rearrange("p (c i) t -> p c t i", i=4),
+                    h_rows[:, b].rearrange("p t (c i) -> p c t i", i=4),
+                )
+            codes = ring.tile([P, 2, CH], U32, name="codes", align_bytes=64)
+            scales = ring.tile([P, 2, CH], U8, name="scales", align_bytes=64)
+            nc.vector.quantize_mx(
+                codes[:].rearrange("p b j -> p (b j)").bitcast(FP8X4),
+                scales[:].rearrange("p b j -> p (b j)"),
+                h_words[:].rearrange("p b j t -> p (b j t)"),
+            )
+            h_q[c] = (codes, scales)
+
+        def gather_gates(c):
+            g = ring.tile([P, PACK, CH], F32, name="picked", bufs=3)
+            for t in range(PACK):
+                nc.vector.tensor_copy(
+                    g[:, t, :], gates[:, t * T : (t + 1) * T].indirect(src_list[:, c * OC : (c + 1) * OC])
+                )
+            picked[c] = g
+
+        def second_stage(c):
+            codes, scales = h_q[c]
+            msg = ring.tile([P, PACK, CH], F32, name="msg")
+            for jt in range(JT):
+                jc = slice(jt * P, (jt + 1) * P)
+                y = psum.tile([P, BANK], F32, name="y")
+                for b in range(2):
+                    nc.tensor.matmul_mx(
+                        y[:], lhsT=codes[:, b, jc].bitcast(FP8X4), lhsT_scale=scales[:, b, jc],
+                        rhs=wd_w[:, b, :].bitcast(FP4X4), rhs_scale=wd_sc[:, b, :],
+                        start=(b == 0), stop=(b == 1),
+                    )
+                y_w = ring.tile([P, PACK, P], F32, name="y_w")
+                e = c * JT + jt
+                nc.scalar.activation(y_w[:], y[:].rearrange("p (m t) -> p t m", t=PACK), ACT.Copy, scale=wg[:, e : e + 1])
+                y_turned = psum.tile([P, PACK, P], F32, name="y_turned")
+                for t in range(PACK):
+                    nc.tensor.transpose(y_turned[:, t, :], y_w[:, t, :], ident[:])
+                nc.scalar.copy(msg[:, :, jc], y_turned[:])
+            msgs[c] = msg
+
+        def scatter(c, t):
+            nc.vector.tensor_tensor(
+                pages[t][:].indirect(dst_list[:, c * OC : (c + 1) * OC]), msgs[c][:, t, :], picked[c][:, t, :], MULT
+            )
+
+        first_stage(0)
+        gather_gates(0)
+        for c in range(1, NCH):
+            first_stage(c)
+            gather_gates(c)
+            second_stage(c - 1)
+            if c < NCH - 1:
+                for t in range(PACK):
+                    scatter(c - 1, t)
+        second_stage(NCH - 1)
+        for c, t in ((2, 0), (2, 1), (3, 0), (3, 1), (2, 2), (3, 2), (2, 3), (3, 3)):
+            scatter(c, t)
+
+        out_rows = out_0.rearrange("(p t) c -> p t c", t=PACK)
+        o_rows = keep.tile([P, PACK, T], BF16, name="o_rows", align_bytes=64)
+        for t in range(PACK):
+            nc.sync.dma_start(out_rows[:, t, :], pages[t][:])
+            if t < PACK - 1:
+                nc.scalar.copy(o_rows[:, t, :], pages[t][:])
+            else:
+                nc.vector.tensor_copy(o_rows[:, t, :], pages[t][:])
+        o_sc = keep.tile([P, T], U8, name="o_sc", align_bytes=64)
+        out_words = out_1[0].rearrange("p t i -> p (t i)").bitcast(I32)
+        for s in range(T // PIECE):
+            o_words = keep.tile([P, PIECE, PACK], BF16, name="o_words%d" % s, align_bytes=64)
+            c0 = s * PIECE
+            dst = o_words[:].rearrange("p (c i) t -> p c t i", i=4)
+            src = o_rows[:, :, c0 : c0 + PIECE].rearrange("p t (c i) -> p c t i", i=4)
+            nc.scalar.copy(dst[:, VCOLS // 4 :], src[:, VCOLS // 4 :])
+            nc.vector.tensor_copy(dst[:, : VCOLS // 4], src[:, : VCOLS // 4])
+            o_codes = keep.tile([P, PIECE], I32, name="o_codes%d" % s, align_bytes=64)
+            nc.vector.quantize_mx(
+                o_codes[:].bitcast(FP8X4), o_sc[:, c0 : c0 + PIECE], o_words[:].rearrange("p c t -> p (c t)")
+            )
+            nc.sync.dma_start(out_words[:, c0 : c0 + PIECE], o_codes[:])
+        for q in range(4):
+            nc.sync.dma_start(out_2[0, 4 * q : 4 * q + 4, :].bitcast(I32), o_sc[32 * q : 32 * q + 4, :].bitcast(I32))

@@ -24,9 +24,11 @@ CH = 256
 NCH = J // CH
 JT = CH // P
 OC = CH // 16
+HALF = J // 2
 PIECE = 512
 VCOLS = 256
-LIVE = 24
+CLEAR = 512
+IL_ON_VECTOR = [1,1,1,1]
 
 
 def tile_list_msg_tanh_gateP_kernel(
@@ -43,61 +45,66 @@ def tile_list_msg_tanh_gateP_kernel(
         dst_list = keep.tile([P, J // 16], U16, name="dst_list")
         lists = (src_list, dst_list)
 
-        tab_sc = keep.tile([P, T // 4], I32, name="tab_sc", tag="big", align_bytes=64)
-        for q in range(4):
-            nc.vector.memset(tab_sc[32 * q : 32 * q + LIVE, :], 0)
+        tab_sc = keep.tile([P, T // 4], I32, name="tab_sc", tag="tab_sc", align_bytes=64)
+        for p0, p1 in ((0, 48), (64, 80), (96, 128)):
+            nc.gpsimd.memset(tab_sc[p0:p1, :], 0)
         ws_sc = keep.tile([P, 2, R], U8, name="ws_sc", align_bytes=64)
         wt_sc = keep.tile([P, 2, R], U8, name="wt_sc", align_bytes=64)
-        nc.gpsimd.memset(ws_sc[:].rearrange("p a r -> p (a r)").bitcast(I32), 0)
-        nc.gpsimd.memset(wt_sc[:].rearrange("p a r -> p (a r)").bitcast(I32), 0)
+        nc.vector.memset(wt_sc[:].rearrange("p a r -> p (a r)").bitcast(I32), 0)
+        nc.vector.memset(ws_sc[:].rearrange("p a r -> p (a r)").bitcast(I32), 0)
         nc.sync.dma_start(src_list[:], offs)
         nc.sync.dma_start(dst_list[:], offs2)
-        for q in range(4):
-            nc.sync.dma_start(
-                tab_sc[32 * q + LIVE : 32 * q + 32, :],
-                tab_scales[:, 4 * q : 4 * q + 4, :].bitcast(I32),
-            )
-        tab_w = keep.tile([P, T], I32, name="tab_w", align_bytes=64)
+        tab_rows = tab_scales.rearrange("a (u x r) t -> x (a u) r t", x=2, r=4).bitcast(I32)
+        for x in range(2):
+            nc.sync.dma_start(tab_sc[48 + 32 * x : 64 + 32 * x, :], tab_rows[x])
+        tab_w = keep.tile([P, T], I32, name="tab_w", tag="tab_w", align_bytes=64)
         nc.sync.dma_start(tab_w[:], tab_words[0].rearrange("p t i -> p (t i)").bitcast(I32))
-        ws_w = keep.tile([P, 2, 2 * R], U8, name="ws_w", align_bytes=64)
-        nc.sync.dma_start(ws_w[:].bitcast(I32), ws_words.rearrange("a p c -> p a c").bitcast(I32))
-        for plane, scales, queue in ((ws_sc, ws_scales, nc.sync), (wt_sc, wt_scales, nc.sync)):
+        ws_w = [keep.tile([P, 2, BANK // 2], I32, name="ws_w%d" % b, align_bytes=64) for b in range(2)]
+        wt_w = [keep.tile([P, 2, BANK], I32, name="wt_w%d" % b, align_bytes=64) for b in range(2)]
+        ws_src = ws_words.rearrange("a p c -> p a c").bitcast(I32)
+        wt_src = wt_words.rearrange("a p r i -> p a (r i)").bitcast(I32)
+        nc.sync.dma_start(ws_w[0][:], ws_src[:, :, : BANK // 2])
+
+        def load_plane(plane, scales, queue):
             for q in range(4):
                 queue.dma_start(
                     plane[32 * q : 32 * q + 4].bitcast(I32),
                     scales[:, 4 * q : 4 * q + 4, :].rearrange("a q r -> q a r").bitcast(I32),
                 )
-        w_sc = (ws_sc, wt_sc)
-        wt_w = keep.tile([P, 2, R], I32, name="wt_w", align_bytes=64)
-        nc.sync.dma_start(wt_w[:], wt_words.rearrange("a p r i -> p a (r i)").bitcast(I32))
 
-        HALF = J // 2
+        load_plane(ws_sc, ws_scales, nc.sync)
+        load_plane(wt_sc, wt_scales, nc.gpsimd)
+        nc.sync.dma_start(wt_w[0][:], wt_src[:, :, :BANK])
+        nc.sync.dma_start(wt_w[1][:], wt_src[:, :, BANK:])
+        nc.sync.dma_start(ws_w[1][:], ws_src[:, :, BANK // 2 :])
+        w_sc = (ws_sc, wt_sc)
+
         v_sc = [keep.tile([P, 2, 2, HALF], U8, name="v_sc_%d" % h, align_bytes=64) for h in range(2)]
-        for h in range(2):
-            nc.vector.memset(v_sc[h][:].rearrange("p a l j -> p (a l j)").bitcast(I32), 0)
         ident = keep.tile([P, P], F32, name="ident")
         make_identity(nc, ident[:])
         sm_t = keep.tile([P, 2, PACK], F32, name="sm_t")
         nc.gpsimd.dma_start(sm_t[:], sm.rearrange("(b p t) -> p b t", b=2, t=PACK))
-        pages = [keep.tile([P, T], F32, name="page%d" % t) for t in range(PACK)]
         wd_sc = keep.tile([P, 2, N], U8, name="wd_sc", align_bytes=64)
-        for t in range(PACK):
-            nc.gpsimd.memset(pages[t][:], 0.0)
-            if t == 1:
-                nc.gpsimd.memset(wd_sc[:].rearrange("p a n -> p (a n)").bitcast(I32), 0)
+        nc.gpsimd.memset(wd_sc[:].rearrange("p a n -> p (a n)").bitcast(I32), 0)
+        load_plane(wd_sc, wd_scales, nc.gpsimd)
 
+        wg_rows = keep.tile([P, P], F32, name="wg_rows", align_bytes=64)
+        nc.gpsimd.dma_start(wg_rows[:], wgo[0:16].rearrange("g (c i) -> (g c) i", i=P))
         v_w = []
 
         def gather_scales(h, tag):
-            got = keep.tile([P, 2, HALF], U8, name="v_sc0", tag=tag, align_bytes=64)
+            got = keep.tile([P, 2, HALF], U8, name="got%d" % h, tag=tag, align_bytes=64)
             for l in range(2):
-                nc.vector.tensor_copy(got[:, l, :], tab_sc[:].bitcast(U8).indirect(lists[l][:, h * 2 * OC : (h + 1) * 2 * OC]))
-            for a in range(2):
-                shift = LIVE + 4 * a
-                (nc.scalar if h == 0 else nc.sync).dma_start(
-                    v_sc[h][: P - shift, a].rearrange("p l j -> p (l j)").bitcast(I32),
-                    got[shift:].rearrange("p l j -> p (l j)").bitcast(I32),
+                nc.vector.tensor_copy(
+                    got[:, l, :], tab_sc[:].bitcast(U8).indirect(lists[l][:, h * 2 * OC : (h + 1) * 2 * OC])
                 )
+            for a in range(2):
+                for u in range(2):
+                    first = 48 + 8 * a + 4 * u
+                    (nc.scalar if h == 0 else nc.sync).dma_start(
+                        v_sc[h][64 * u : 64 * u + 64, a].rearrange("p l j -> p (l j)").bitcast(I32),
+                        got[first : first + 64].rearrange("p l j -> p (l j)").bitcast(I32),
+                    )
 
         def gather_words(c):
             both = keep.tile([P, 2, CH], U32, name="both", tag="both%d" % c, align_bytes=64)
@@ -112,72 +119,86 @@ def tile_list_msg_tanh_gateP_kernel(
             )
             v_w.append(parted)
 
-        gather_scales(0, "v_sc0")
+        gather_scales(0, "got0")
         gather_words(0)
+        gates = [keep.tile([P, 2 * T], F32, name="gates%d" % u, tag=["gates0","both0"][u], align_bytes=64) for u in range(2)]
+        gT_rows = gT.rearrange("(p t) c -> p t c", t=PACK)
+        wd_w = keep.tile([P, 2, 2 * N], U8, name="wd_w", align_bytes=64)
         gather_words(1)
-        gather_scales(1, "both0")
+        gather_scales(1, "both1")
         gather_words(2)
         gather_words(3)
-
-        gates = keep.tile([P, PACK * T], F32, name="gates", tag="big", align_bytes=64)
-        gT_rows = gT.rearrange("(p t) c -> p t c", t=PACK)
-        wd_w = keep.tile([P, 2, 2 * N], U8, name="wd_w", tag="both1", align_bytes=64)
         nc.sync.dma_start(wd_w[:].bitcast(I32), wd_words.rearrange("a p c -> p a c").bitcast(I32))
-        for q in range(4):
-            nc.sync.dma_start(
-                wd_sc[32 * q : 32 * q + 4].bitcast(I32),
-                wd_scales[:, 4 * q : 4 * q + 4, :].rearrange("a q n -> q a n").bitcast(I32),
-            )
-        wg = keep.tile([P, J // P], F32, name="wg", tag="both2", align_bytes=64)
-        with nc.allow_non_contiguous_dma(reason="one edge weight a partition"):
-            nc.sync.dma_start(wg[:], wgo[0].rearrange("(c p) -> p c", p=P))
+
         for t in range(PACK):
-            nc.sync.dma_start(gates[:, t * T : (t + 1) * T], gT_rows[:, t, :])
+            nc.sync.dma_start(gates[t // 2][:, (t % 2) * T : (t % 2 + 1) * T], gT_rows[:, t, :])
 
+        pages = [
+            keep.tile([P, T], F32, name="page%d" % t, tag=["tab_sc","both2","both3","tab_w"][t], align_bytes=64)
+            for t in range(PACK)
+        ]
+        for t in range(PACK):
+            for c0 in range(0, T, CLEAR):
+                nc.gpsimd.memset(pages[t][:, c0 : c0 + CLEAR], 0.0)
+
+        wg = keep.tile([P, J // P], F32, name="wg")
+        wg_turned = psum.tile([P, PACK, P], F32, name="wg_turned", tag="turned", bufs=5)
+        nc.tensor.transpose(wg_turned[:, 0, :], wg_rows[:], ident[:])
+        nc.scalar.copy(wg[:], wg_turned[:, 0, : J // P])
+
+        th = {}
         h_q = {}
+        h_w = {}
         picked = {}
-        msgs = {}
+        msgs = [keep.tile([P, PACK, HALF], F32, name="msgs%d" % h) for h in range(2)]
 
-        def first_stage(c):
-            th = []
-            for jt in range(JT):
-                th_t = ring.tile([P, 2, PACK, P], F32, name="th", bufs=3)
-                h = c // 2
-                jc = slice((c % 2) * CH + jt * P, (c % 2) * CH + (jt + 1) * P)
-                jw = slice(2 * jt * P, 2 * (jt + 1) * P)
-                for b in range(2):
+        def sums(c):
+            h = c // 2
+            for b in range(2):
+                for jt in range(JT):
+                    th_t = ring.tile([P, PACK, P], F32, name="th", bufs=8)
+                    jc = slice((c % 2) * CH + jt * P, (c % 2) * CH + (jt + 1) * P)
+                    jw = slice(2 * jt * P, 2 * (jt + 1) * P)
                     acc = psum.tile([P, BANK], F32, name="acc", bufs=3)
                     rc = slice(b * BANK, (b + 1) * BANK)
                     for a in range(2):
                         nc.tensor.matmul_mx(
                             acc[:], lhsT=v_w[c][:, 0, a, jw].bitcast(FP4X4), lhsT_scale=v_sc[h][:, a, 0, jc],
-                            rhs=ws_w[:, a, 2 * b * BANK : 2 * (b + 1) * BANK].bitcast(FP4X4),
+                            rhs=ws_w[b][:, a, :].bitcast(FP4X4),
                             rhs_scale=w_sc[0][:, a, rc], start=(a == 0), stop=False,
                         )
                         nc.tensor.matmul_mx(
                             acc[:], lhsT=v_w[c][:, 1, a, jw].bitcast(FP4X4), lhsT_scale=v_sc[h][:, a, 1, jc],
-                            rhs=wt_w[:, a, rc].bitcast(FP8X4),
+                            rhs=wt_w[b][:, a, :].bitcast(FP8X4),
                             rhs_scale=w_sc[1][:, a, rc], start=False, stop=(a == 1),
                         )
-                    nc.scalar.activation(th_t[:, b], acc[:].rearrange("p (m t) -> p t m", t=PACK), ACT.Tanh)
-                th.append(th_t)
+                    nc.scalar.activation(th_t[:], acc[:].rearrange("p (m t) -> p t m", t=PACK), ACT.Tanh)
+                    th[c, jt, b] = th_t
+
+        def hidden(c):
             h_rows = ring.tile([P, 2, PACK, CH], BF16, name="h_rows", align_bytes=64)
+            h_words = keep.tile([P, 2, CH, PACK], BF16, name="h_words", tag="h_words%d" % c, align_bytes=64)
             for b in range(2):
                 for u in range(2):
-                    turned = psum.tile([P, 2, CH], F32, name="turned", bufs=3)
+                    turned = psum.tile([P, 2, CH], F32, name="turned", bufs=5)
                     for e in range(2):
                         for jt in range(JT):
-                            nc.tensor.transpose(turned[:, e, jt * P : (jt + 1) * P], th[jt][:, b, 2 * u + e, :], ident[:])
+                            nc.tensor.transpose(turned[:, e, jt * P : (jt + 1) * P], th[c, jt, b][:, 2 * u + e, :], ident[:])
                     for e in range(2):
                         t = 2 * u + e
                         nc.scalar.activation(h_rows[:, b, t, :], turned[:, e, :], ACT.Copy, scale=sm_t[:, b, t : t + 1])
-            h_words = ring.tile([P, 2, CH, PACK], BF16, name="h_words", align_bytes=64)
-            for b in range(2):
-                (nc.vector.tensor_copy if b == 0 else nc.scalar.copy)(
+                (nc.vector.tensor_copy if b < IL_ON_VECTOR[c] else nc.scalar.copy)(
                     h_words[:, b].rearrange("p (c i) t -> p c t i", i=4),
                     h_rows[:, b].rearrange("p t (c i) -> p c t i", i=4),
                 )
-            codes = ring.tile([P, 2, CH], U32, name="codes", align_bytes=64)
+            h_w[c] = h_words
+
+        def quantise(c):
+            h_words = h_w[c]
+            if c == NCH - 1:
+                codes = keep.tile([P, 2, CH], U32, name="codes", tag="last", align_bytes=64)
+            else:
+                codes = ring.tile([P, 2, CH], U32, name="codes", align_bytes=64)
             scales = ring.tile([P, 2, CH], U8, name="scales", align_bytes=64)
             nc.vector.quantize_mx(
                 codes[:].rearrange("p b j -> p (b j)").bitcast(FP8X4),
@@ -187,51 +208,79 @@ def tile_list_msg_tanh_gateP_kernel(
             h_q[c] = (codes, scales)
 
         def gather_gates(c):
-            g = ring.tile([P, PACK, CH], F32, name="picked", bufs=3)
+            if c < 3:
+                tag = ["picked0","picked1","h_words0"][c]
+                picked[c] = keep.tile([P, PACK, CH if c < 2 else HALF], F32, name="picked", tag=tag, align_bytes=64)
+            cols = slice(max(c - 2, 0) * CH, (max(c - 2, 0) + 1) * CH)
             for t in range(PACK):
-                nc.vector.tensor_copy(
-                    g[:, t, :], gates[:, t * T : (t + 1) * T].indirect(src_list[:, c * OC : (c + 1) * OC])
-                )
-            picked[c] = g
+                window = gates[t // 2][:, (t % 2) * T : (t % 2 + 1) * T]
+                nc.vector.tensor_copy(picked[min(c, 2)][:, t, cols], window.indirect(src_list[:, c * OC : (c + 1) * OC]))
 
-        def second_stage(c):
+        def messages(c):
             codes, scales = h_q[c]
-            msg = ring.tile([P, PACK, CH], F32, name="msg")
             for jt in range(JT):
                 jc = slice(jt * P, (jt + 1) * P)
-                y = psum.tile([P, BANK], F32, name="y")
+                y = psum.tile([P, BANK], F32, name="y", tag="turned", bufs=5)
                 for b in range(2):
                     nc.tensor.matmul_mx(
                         y[:], lhsT=codes[:, b, jc].bitcast(FP8X4), lhsT_scale=scales[:, b, jc],
                         rhs=wd_w[:, b, :].bitcast(FP4X4), rhs_scale=wd_sc[:, b, :],
                         start=(b == 0), stop=(b == 1),
                     )
-                y_w = ring.tile([P, PACK, P], F32, name="y_w")
+                if (c, jt) == (NCH - 2, JT - 1):
+                    y_w = keep.tile([P, PACK, P], F32, name="y_w", tag="last", align_bytes=64)
+                else:
+                    y_w = ring.tile([P, PACK, P], F32, name="y_w")
                 e = c * JT + jt
                 nc.scalar.activation(y_w[:], y[:].rearrange("p (m t) -> p t m", t=PACK), ACT.Copy, scale=wg[:, e : e + 1])
-                y_turned = psum.tile([P, PACK, P], F32, name="y_turned")
+                y_turned = psum.tile([P, PACK, P], F32, name="y_turned", tag="turned", bufs=5)
                 for t in range(PACK):
                     nc.tensor.transpose(y_turned[:, t, :], y_w[:, t, :], ident[:])
-                nc.scalar.copy(msg[:, :, jc], y_turned[:])
-            msgs[c] = msg
+                j0 = (c % 2) * CH + jt * P
+                nc.scalar.copy(msgs[c // 2][:, :, j0 : j0 + P], y_turned[:])
 
-        def scatter(c, t):
+        def scatter(c, t, n):
+            cols = slice((c % 2) * CH, (c % 2 + n) * CH)
             nc.vector.tensor_tensor(
-                pages[t][:].indirect(dst_list[:, c * OC : (c + 1) * OC]), msgs[c][:, t, :], picked[c][:, t, :], MULT
+                pages[t][:].indirect(dst_list[:, c * OC : (c + n) * OC]),
+                msgs[c // 2][:, t, cols], picked[min(c, 2)][:, t, max(c - 2, 0) * CH : (max(c - 2, 0) + n) * CH], MULT,
             )
 
-        first_stage(0)
+        sums(0)
+        hidden(0)
+        quantise(0)
         gather_gates(0)
-        for c in range(1, NCH):
-            first_stage(c)
-            gather_gates(c)
-            second_stage(c - 1)
-            if c < NCH - 1:
-                for t in range(PACK):
-                    scatter(c - 1, t)
-        second_stage(NCH - 1)
-        for c, t in ((2, 0), (2, 1), (3, 0), (3, 1), (2, 2), (3, 2), (2, 3), (3, 3)):
-            scatter(c, t)
+        sums(1)
+        hidden(1)
+        quantise(1)
+        gather_gates(1)
+        messages(0)
+        scatter(0, 0, 1)
+        scatter(0, 1, 1)
+        scatter(0, 2, 1)
+        scatter(0, 3, 1)
+        sums(2)
+        hidden(2)
+        quantise(2)
+        gather_gates(2)
+        messages(1)
+        scatter(1, 0, 1)
+        scatter(1, 1, 1)
+        scatter(1, 2, 1)
+        scatter(1, 3, 1)
+        sums(3)
+        hidden(3)
+        gather_gates(3)
+        messages(2)
+        quantise(3)
+        messages(3)
+        scatter(2, 0, 1)
+        scatter(2, 1, 1)
+        scatter(2, 2, 1)
+        scatter(3, 0, 1)
+        scatter(3, 1, 1)
+        scatter(3, 2, 1)
+        scatter(2, 3, 2)
 
         out_rows = out_0.rearrange("(p t) c -> p t c", t=PACK)
         o_rows = keep.tile([P, PACK, T], BF16, name="o_rows", align_bytes=64)
@@ -240,7 +289,8 @@ def tile_list_msg_tanh_gateP_kernel(
             if t < PACK - 1:
                 nc.scalar.copy(o_rows[:, t, :], pages[t][:])
             else:
-                nc.vector.tensor_copy(o_rows[:, t, :], pages[t][:])
+                nc.vector.tensor_copy(o_rows[:, t, : T // 2], pages[t][:, : T // 2])
+                nc.scalar.copy(o_rows[:, t, T // 2 :], pages[t][:, T // 2 :])
         o_sc = keep.tile([P, T], U8, name="o_sc", align_bytes=64)
         out_words = out_1[0].rearrange("p t i -> p (t i)").bitcast(I32)
         for s in range(T // PIECE):
@@ -248,8 +298,11 @@ def tile_list_msg_tanh_gateP_kernel(
             c0 = s * PIECE
             dst = o_words[:].rearrange("p (c i) t -> p c t i", i=4)
             src = o_rows[:, :, c0 : c0 + PIECE].rearrange("p t (c i) -> p c t i", i=4)
-            nc.scalar.copy(dst[:, VCOLS // 4 :], src[:, VCOLS // 4 :])
-            nc.vector.tensor_copy(dst[:, : VCOLS // 4], src[:, : VCOLS // 4])
+            vc = [512,384,128,128][s] // 4
+            if vc < PIECE // 4:
+                nc.scalar.copy(dst[:, vc:], src[:, vc:])
+            if vc > 0:
+                nc.vector.tensor_copy(dst[:, :vc], src[:, :vc])
             o_codes = keep.tile([P, PIECE], I32, name="o_codes%d" % s, align_bytes=64)
             nc.vector.quantize_mx(
                 o_codes[:].bitcast(FP8X4), o_sc[:, c0 : c0 + PIECE], o_words[:].rearrange("p c t -> p (c t)")

@@ -28,7 +28,7 @@ HALF = J // 2
 PIECE = 512
 VCOLS = 256
 CLEAR = 512
-IL_ON_VECTOR = [1,1,1,1]
+IL_ON_VECTOR = [2,2,1,1]
 
 
 def tile_list_msg_tanh_gateP_kernel(
@@ -172,7 +172,9 @@ def tile_list_msg_tanh_gateP_kernel(
                             rhs=wt_w[b][:, a, :].bitcast(FP8X4),
                             rhs_scale=w_sc[1][:, a, rc], start=False, stop=(a == 1),
                         )
-                    nc.scalar.activation(th_t[:], acc[:].rearrange("p (m t) -> p t m", t=PACK), ACT.Tanh)
+                    nc.scalar.activation(
+                        th_t[:].rearrange("p t m -> p m t"), acc[:].rearrange("p (m t) -> p m t", t=PACK), ACT.Tanh
+                    )
                     th[c, jt, b] = th_t
 
         def hidden(c):
@@ -232,7 +234,10 @@ def tile_list_msg_tanh_gateP_kernel(
                 else:
                     y_w = ring.tile([P, PACK, P], F32, name="y_w")
                 e = c * JT + jt
-                nc.scalar.activation(y_w[:], y[:].rearrange("p (m t) -> p t m", t=PACK), ACT.Copy, scale=wg[:, e : e + 1])
+                nc.scalar.activation(
+                    y_w[:].rearrange("p t m -> p m t"), y[:].rearrange("p (m t) -> p m t", t=PACK),
+                    ACT.Copy, scale=wg[:, e : e + 1],
+                )
                 y_turned = psum.tile([P, PACK, P], F32, name="y_turned", tag="turned", bufs=5)
                 for t in range(PACK):
                     nc.tensor.transpose(y_turned[:, t, :], y_w[:, t, :], ident[:])

@@ -25,10 +25,11 @@ NCH = J // CH
 JT = CH // P
 OC = CH // 16
 HALF = J // 2
+PTAGS = ["tab_w","both3","both1"]
 PIECE = 512
 VCOLS = 256
-CLEAR = 512
-IL_ON_VECTOR = [2,2,1,1]
+CLEAR = 2048
+IL_ON_VECTOR = [1,1,1,1]
 
 
 def tile_list_msg_tanh_gateP_kernel(
@@ -45,13 +46,13 @@ def tile_list_msg_tanh_gateP_kernel(
         dst_list = keep.tile([P, J // 16], U16, name="dst_list")
         lists = (src_list, dst_list)
 
+        ws_sc = keep.tile([P, 2, R], U8, name="ws_sc", align_bytes=64)
+        nc.vector.memset(ws_sc[:].rearrange("p a r -> p (a r)").bitcast(I32), 0)
         tab_sc = keep.tile([P, T // 4], I32, name="tab_sc", tag="tab_sc", align_bytes=64)
         for p0, p1 in ((0, 48), (64, 80), (96, 128)):
-            nc.gpsimd.memset(tab_sc[p0:p1, :], 0)
-        ws_sc = keep.tile([P, 2, R], U8, name="ws_sc", align_bytes=64)
+            nc.vector.memset(tab_sc[p0:p1, :], 0)
         wt_sc = keep.tile([P, 2, R], U8, name="wt_sc", align_bytes=64)
-        nc.vector.memset(wt_sc[:].rearrange("p a r -> p (a r)").bitcast(I32), 0)
-        nc.vector.memset(ws_sc[:].rearrange("p a r -> p (a r)").bitcast(I32), 0)
+        nc.gpsimd.memset(wt_sc[:].rearrange("p a r -> p (a r)").bitcast(I32), 0)
         nc.sync.dma_start(src_list[:], offs)
         nc.sync.dma_start(dst_list[:], offs2)
         tab_rows = tab_scales.rearrange("a (u x r) t -> x (a u) r t", x=2, r=4).bitcast(I32)
@@ -83,12 +84,10 @@ def tile_list_msg_tanh_gateP_kernel(
         ident = keep.tile([P, P], F32, name="ident")
         make_identity(nc, ident[:])
         sm_t = keep.tile([P, 2, PACK], F32, name="sm_t")
-        nc.gpsimd.dma_start(sm_t[:], sm.rearrange("(b p t) -> p b t", b=2, t=PACK))
-        wd_sc = keep.tile([P, 2, N], U8, name="wd_sc", align_bytes=64)
-        nc.gpsimd.memset(wd_sc[:].rearrange("p a n -> p (a n)").bitcast(I32), 0)
-        load_plane(wd_sc, wd_scales, nc.gpsimd)
+
 
         wg_rows = keep.tile([P, P], F32, name="wg_rows", align_bytes=64)
+        nc.gpsimd.dma_start(sm_t[:], sm.rearrange("(b p t) -> p b t", b=2, t=PACK))
         nc.gpsimd.dma_start(wg_rows[:], wgo[0:16].rearrange("g (c i) -> (g c) i", i=P))
         v_w = []
 
@@ -119,27 +118,27 @@ def tile_list_msg_tanh_gateP_kernel(
             )
             v_w.append(parted)
 
+        pages = [keep.tile([P, T], F32, name="page0", align_bytes=64)]
+        nc.vector.memset(pages[0][:], 0.0)
         gather_scales(0, "got0")
         gather_words(0)
-        gates = [keep.tile([P, 2 * T], F32, name="gates%d" % u, tag=["gates0","both0"][u], align_bytes=64) for u in range(2)]
+        gates = [keep.tile([P, 2 * T], F32, name="gates%d" % u, tag=["both0","got0"][u], align_bytes=64) for u in range(2)]
         gT_rows = gT.rearrange("(p t) c -> p t c", t=PACK)
-        wd_w = keep.tile([P, 2, 2 * N], U8, name="wd_w", align_bytes=64)
+        wd_w = keep.tile([P, 2, 2 * N], U8, name="wd_w", tag="tab_sc", align_bytes=64)
+        for t in range(PACK):
+            nc.sync.dma_start(gates[t // 2][:, (t % 2) * T : (t % 2 + 1) * T], gT_rows[:, t, :])
         gather_words(1)
         gather_scales(1, "both1")
         gather_words(2)
         gather_words(3)
+        wd_sc = keep.tile([P, 2, N], U8, name="wd_sc", tag="both2", align_bytes=64)
+        nc.gpsimd.memset(wd_sc[:].rearrange("p a n -> p (a n)").bitcast(I32), 0)
         nc.sync.dma_start(wd_w[:].bitcast(I32), wd_words.rearrange("a p c -> p a c").bitcast(I32))
+        load_plane(wd_sc, wd_scales, nc.sync)
 
-        for t in range(PACK):
-            nc.sync.dma_start(gates[t // 2][:, (t % 2) * T : (t % 2 + 1) * T], gT_rows[:, t, :])
-
-        pages = [
-            keep.tile([P, T], F32, name="page%d" % t, tag=["tab_sc","both2","both3","tab_w"][t], align_bytes=64)
-            for t in range(PACK)
-        ]
-        for t in range(PACK):
-            for c0 in range(0, T, CLEAR):
-                nc.gpsimd.memset(pages[t][:, c0 : c0 + CLEAR], 0.0)
+        for t in range(1, PACK):
+            pages.append(keep.tile([P, T], F32, name="page%d" % t, tag=PTAGS[t - 1], align_bytes=64))
+            nc.vector.memset(pages[t][:], 0.0)
 
         wg = keep.tile([P, J // P], F32, name="wg")
         wg_turned = psum.tile([P, PACK, P], F32, name="wg_turned", tag="turned", bufs=5)
@@ -209,14 +208,11 @@ def tile_list_msg_tanh_gateP_kernel(
             )
             h_q[c] = (codes, scales)
 
-        def gather_gates(c):
-            if c < 3:
-                tag = ["picked0","picked1","h_words0"][c]
-                picked[c] = keep.tile([P, PACK, CH if c < 2 else HALF], F32, name="picked", tag=tag, align_bytes=64)
-            cols = slice(max(c - 2, 0) * CH, (max(c - 2, 0) + 1) * CH)
+        def gather_gates(c, n):
+            picked[c] = keep.tile([P, PACK, n * CH], F32, name="picked", tag=["picked0","h_words0","h_words1"][c], align_bytes=64)
             for t in range(PACK):
                 window = gates[t // 2][:, (t % 2) * T : (t % 2 + 1) * T]
-                nc.vector.tensor_copy(picked[min(c, 2)][:, t, cols], window.indirect(src_list[:, c * OC : (c + 1) * OC]))
+                nc.vector.tensor_copy(picked[c][:, t, :], window.indirect(src_list[:, c * OC : (c + n) * OC]))
 
         def messages(c):
             codes, scales = h_q[c]
@@ -254,11 +250,11 @@ def tile_list_msg_tanh_gateP_kernel(
         sums(0)
         hidden(0)
         quantise(0)
-        gather_gates(0)
+        gather_gates(0, 1)
         sums(1)
         hidden(1)
         quantise(1)
-        gather_gates(1)
+        gather_gates(1, 1)
         messages(0)
         scatter(0, 0, 1)
         scatter(0, 1, 1)
@@ -267,7 +263,7 @@ def tile_list_msg_tanh_gateP_kernel(
         sums(2)
         hidden(2)
         quantise(2)
-        gather_gates(2)
+        gather_gates(2, 2)
         messages(1)
         scatter(1, 0, 1)
         scatter(1, 1, 1)
@@ -275,7 +271,6 @@ def tile_list_msg_tanh_gateP_kernel(
         scatter(1, 3, 1)
         sums(3)
         hidden(3)
-        gather_gates(3)
         messages(2)
         quantise(3)
         messages(3)
@@ -303,7 +298,7 @@ def tile_list_msg_tanh_gateP_kernel(
             c0 = s * PIECE
             dst = o_words[:].rearrange("p (c i) t -> p c t i", i=4)
             src = o_rows[:, :, c0 : c0 + PIECE].rearrange("p t (c i) -> p c t i", i=4)
-            vc = [512,384,128,128][s] // 4
+            vc = [512,512,128,0][s] // 4
             if vc < PIECE // 4:
                 nc.scalar.copy(dst[:, vc:], src[:, vc:])
             if vc > 0:

@@ -19,17 +19,18 @@ MULT = mybir.AluOpType.mult
 
 P = 128
 PACK = 4
+PASSES = 2
 BANK = 512
-CH = 256
-NCH = J // CH
-JT = CH // P
-OC = CH // 16
+CHUNK = 256
+CHUNKS = J // CHUNK
+EDGE_TILES = CHUNK // P
+LIST_COLS = CHUNK // 16
 HALF = J // 2
-PTAGS = ["tab_w","both3","both1"]
+SCALE_ROW = 48
 PIECE = 512
-VCOLS = 256
-CLEAR = 2048
-IL_ON_VECTOR = [1,1,1,1]
+VECTOR_COLS = 1152
+SUM_BANKS = 3
+TURN_BANKS = 5
 
 
 def tile_list_msg_tanh_gateP_kernel(
@@ -46,241 +47,256 @@ def tile_list_msg_tanh_gateP_kernel(
         dst_list = keep.tile([P, J // 16], U16, name="dst_list")
         lists = (src_list, dst_list)
 
-        ws_sc = keep.tile([P, 2, R], U8, name="ws_sc", align_bytes=64)
-        nc.vector.memset(ws_sc[:].rearrange("p a r -> p (a r)").bitcast(I32), 0)
-        tab_sc = keep.tile([P, T // 4], I32, name="tab_sc", tag="tab_sc", align_bytes=64)
-        for p0, p1 in ((0, 48), (64, 80), (96, 128)):
-            nc.vector.memset(tab_sc[p0:p1, :], 0)
-        wt_sc = keep.tile([P, 2, R], U8, name="wt_sc", align_bytes=64)
-        nc.gpsimd.memset(wt_sc[:].rearrange("p a r -> p (a r)").bitcast(I32), 0)
+        def load_plane(plane, plane_src, queue):
+            for quad in range(4):
+                queue.dma_start(
+                    plane[32 * quad : 32 * quad + 4].bitcast(I32),
+                    plane_src[:, 4 * quad : 4 * quad + 4, :].rearrange("a q c -> q a c").bitcast(I32),
+                )
+
+        def interleave(copy, words, rows):
+            copy(words.rearrange("p (c i) t -> p c t i", i=4), rows.rearrange("p t (c i) -> p c t i", i=4))
+
+        ws_plane = keep.tile([P, PASSES, R], U8, name="ws_plane", align_bytes=64)
+        nc.vector.memset(ws_plane[:].rearrange("p a r -> p (a r)").bitcast(I32), 0)
+        tab_rows = keep.tile([P, T // 4], I32, name="tab_rows", tag="tab_rows", align_bytes=64)
+        for first, end in ((0, SCALE_ROW), (SCALE_ROW + 16, SCALE_ROW + 32), (SCALE_ROW + 48, P)):
+            nc.vector.memset(tab_rows[first:end, :], 0)
+        wt_plane = keep.tile([P, PASSES, R], U8, name="wt_plane", align_bytes=64)
+        nc.gpsimd.memset(wt_plane[:].rearrange("p a r -> p (a r)").bitcast(I32), 0)
         nc.sync.dma_start(src_list[:], offs)
         nc.sync.dma_start(dst_list[:], offs2)
-        tab_rows = tab_scales.rearrange("a (u x r) t -> x (a u) r t", x=2, r=4).bitcast(I32)
+        tab_rows_src = tab_scales.rearrange("a (u x r) t -> x (a u) r t", x=2, r=4).bitcast(I32)
         for x in range(2):
-            nc.sync.dma_start(tab_sc[48 + 32 * x : 64 + 32 * x, :], tab_rows[x])
+            nc.sync.dma_start(tab_rows[SCALE_ROW + 32 * x : SCALE_ROW + 32 * x + 16, :], tab_rows_src[x])
         tab_w = keep.tile([P, T], I32, name="tab_w", tag="tab_w", align_bytes=64)
         nc.sync.dma_start(tab_w[:], tab_words[0].rearrange("p t i -> p (t i)").bitcast(I32))
-        ws_w = [keep.tile([P, 2, BANK // 2], I32, name="ws_w%d" % b, align_bytes=64) for b in range(2)]
-        wt_w = [keep.tile([P, 2, BANK], I32, name="wt_w%d" % b, align_bytes=64) for b in range(2)]
+
+        ws_w = [keep.tile([P, PASSES, BANK // 2], I32, name="ws_w%d" % b, align_bytes=64) for b in range(PASSES)]
+        wt_w = [keep.tile([P, PASSES, BANK], I32, name="wt_w%d" % b, align_bytes=64) for b in range(PASSES)]
         ws_src = ws_words.rearrange("a p c -> p a c").bitcast(I32)
         wt_src = wt_words.rearrange("a p r i -> p a (r i)").bitcast(I32)
         nc.sync.dma_start(ws_w[0][:], ws_src[:, :, : BANK // 2])
-
-        def load_plane(plane, scales, queue):
-            for q in range(4):
-                queue.dma_start(
-                    plane[32 * q : 32 * q + 4].bitcast(I32),
-                    scales[:, 4 * q : 4 * q + 4, :].rearrange("a q r -> q a r").bitcast(I32),
-                )
-
-        load_plane(ws_sc, ws_scales, nc.sync)
-        load_plane(wt_sc, wt_scales, nc.gpsimd)
+        load_plane(ws_plane, ws_scales, nc.sync)
+        load_plane(wt_plane, wt_scales, nc.gpsimd)
         nc.sync.dma_start(wt_w[0][:], wt_src[:, :, :BANK])
         nc.sync.dma_start(wt_w[1][:], wt_src[:, :, BANK:])
         nc.sync.dma_start(ws_w[1][:], ws_src[:, :, BANK // 2 :])
-        w_sc = (ws_sc, wt_sc)
 
-        v_sc = [keep.tile([P, 2, 2, HALF], U8, name="v_sc_%d" % h, align_bytes=64) for h in range(2)]
+        v_plane = [keep.tile([P, PASSES, 2, HALF], U8, name="v_plane%d" % h, align_bytes=64) for h in range(2)]
         ident = keep.tile([P, P], F32, name="ident")
         make_identity(nc, ident[:])
-        sm_t = keep.tile([P, 2, PACK], F32, name="sm_t")
+        sm_t = keep.tile([P, PASSES, PACK], F32, name="sm_t")
+        wgo_rows = keep.tile([P, P], F32, name="wgo_rows", align_bytes=64)
+        nc.gpsimd.dma_start(sm_t[:], sm.rearrange("(b p t) -> p b t", b=PASSES, t=PACK))
+        nc.gpsimd.dma_start(wgo_rows[:], wgo[0:16].rearrange("g (e i) -> (g e) i", i=P))
 
+        v_words = []
 
-        wg_rows = keep.tile([P, P], F32, name="wg_rows", align_bytes=64)
-        nc.gpsimd.dma_start(sm_t[:], sm.rearrange("(b p t) -> p b t", b=2, t=PACK))
-        nc.gpsimd.dma_start(wg_rows[:], wgo[0:16].rearrange("g (c i) -> (g c) i", i=P))
-        v_w = []
-
-        def gather_scales(h, tag):
+        def gather_scales(h, tag, queue):
             got = keep.tile([P, 2, HALF], U8, name="got%d" % h, tag=tag, align_bytes=64)
             for l in range(2):
-                nc.vector.tensor_copy(
-                    got[:, l, :], tab_sc[:].bitcast(U8).indirect(lists[l][:, h * 2 * OC : (h + 1) * 2 * OC])
-                )
-            for a in range(2):
+                offsets = lists[l][:, 2 * h * LIST_COLS : 2 * (h + 1) * LIST_COLS]
+                nc.vector.tensor_copy(got[:, l, :], tab_rows[:].bitcast(U8).indirect(offsets))
+            for a in range(PASSES):
                 for u in range(2):
-                    first = 48 + 8 * a + 4 * u
-                    (nc.scalar if h == 0 else nc.sync).dma_start(
-                        v_sc[h][64 * u : 64 * u + 64, a].rearrange("p l j -> p (l j)").bitcast(I32),
+                    first = SCALE_ROW + 8 * a + 4 * u
+                    queue.dma_start(
+                        v_plane[h][64 * u : 64 * u + 64, a].rearrange("p l j -> p (l j)").bitcast(I32),
                         got[first : first + 64].rearrange("p l j -> p (l j)").bitcast(I32),
                     )
 
         def gather_words(c):
-            both = keep.tile([P, 2, CH], U32, name="both", tag="both%d" % c, align_bytes=64)
+            both = keep.tile([P, 2, CHUNK], U32, name="both", tag="both%d" % c, align_bytes=64)
             for l in range(2):
-                nc.vector.tensor_copy(
-                    both[:, l, :], tab_w[:].bitcast(U32).indirect(lists[l][:, c * OC : (c + 1) * OC])
-                )
-            parted = keep.tile([P, 2, 2, 2 * CH], U8, name="parted%d" % c, align_bytes=64)
+                offsets = lists[l][:, c * LIST_COLS : (c + 1) * LIST_COLS]
+                nc.vector.tensor_copy(both[:, l, :], tab_w[:].bitcast(U32).indirect(offsets))
+            parted = keep.tile([P, 2, PASSES, 2 * CHUNK], U8, name="parted%d" % c, align_bytes=64)
             nc.vector.tensor_copy(
                 parted[:].bitcast(U16),
-                both[:].bitcast(U16).rearrange("p l (j d) -> p l d j", d=2),
+                both[:].bitcast(U16).rearrange("p l (j a) -> p l a j", a=PASSES),
             )
-            v_w.append(parted)
+            v_words.append(parted)
 
-        pages = [keep.tile([P, T], F32, name="page0", align_bytes=64)]
-        nc.vector.memset(pages[0][:], 0.0)
-        gather_scales(0, "got0")
+        gather_scales(0, "got0", nc.scalar)
         gather_words(0)
-        gates = [keep.tile([P, 2 * T], F32, name="gates%d" % u, tag=["both0","got0"][u], align_bytes=64) for u in range(2)]
+        gates = keep.tile([P, PACK * T], F32, name="gates", tag="got0", align_bytes=64)
+        gate_windows = [gates[:, t * T : (t + 1) * T] for t in range(PACK)]
         gT_rows = gT.rearrange("(p t) c -> p t c", t=PACK)
-        wd_w = keep.tile([P, 2, 2 * N], U8, name="wd_w", tag="tab_sc", align_bytes=64)
+        wd_w = keep.tile([P, PASSES, 2 * N], U8, name="wd_w", align_bytes=64)
+        nc.sync.dma_start(wd_w[:].bitcast(I32), wd_words.rearrange("a p c -> p a c").bitcast(I32))
+        wd_plane = keep.tile([P, PASSES, N], U8, name="wd_plane", tag="both0", align_bytes=64)
+        nc.gpsimd.memset(wd_plane[:].rearrange("p a n -> p (a n)").bitcast(I32), 0)
+        load_plane(wd_plane, wd_scales, nc.sync)
         for t in range(PACK):
-            nc.sync.dma_start(gates[t // 2][:, (t % 2) * T : (t % 2 + 1) * T], gT_rows[:, t, :])
+            nc.sync.dma_start(gate_windows[t], gT_rows[:, t, :])
         gather_words(1)
-        gather_scales(1, "both1")
+        gather_scales(1, "both1", nc.sync)
         gather_words(2)
         gather_words(3)
-        wd_sc = keep.tile([P, 2, N], U8, name="wd_sc", tag="both2", align_bytes=64)
-        nc.gpsimd.memset(wd_sc[:].rearrange("p a n -> p (a n)").bitcast(I32), 0)
-        nc.sync.dma_start(wd_w[:].bitcast(I32), wd_words.rearrange("a p c -> p a c").bitcast(I32))
-        load_plane(wd_sc, wd_scales, nc.sync)
 
-        for t in range(1, PACK):
-            pages.append(keep.tile([P, T], F32, name="page%d" % t, tag=PTAGS[t - 1], align_bytes=64))
-            nc.vector.memset(pages[t][:], 0.0)
+        pages = [keep.tile([P, T], F32, name="page0", tag="tab_w", align_bytes=64)]
+        nc.vector.memset(pages[0][:].bitcast(I32), 0)
 
-        wg = keep.tile([P, J // P], F32, name="wg")
-        wg_turned = psum.tile([P, PACK, P], F32, name="wg_turned", tag="turned", bufs=5)
-        nc.tensor.transpose(wg_turned[:, 0, :], wg_rows[:], ident[:])
-        nc.scalar.copy(wg[:], wg_turned[:, 0, : J // P])
+        edge_weight = keep.tile([P, J // P], F32, name="edge_weight")
+        wgo_turned = psum.tile([P, PACK, P], F32, name="wgo_turned", tag="turned", bufs=TURN_BANKS)
+        nc.tensor.transpose(wgo_turned[:, 0, :], wgo_rows[:], ident[:])
+        nc.scalar.copy(edge_weight[:], wgo_turned[:, 0, : J // P])
 
-        th = {}
-        h_q = {}
-        h_w = {}
+        tanhs = {}
+        h_words = {}
+        h_quantised = {}
         picked = {}
         msgs = [keep.tile([P, PACK, HALF], F32, name="msgs%d" % h) for h in range(2)]
 
         def sums(c):
-            h = c // 2
-            for b in range(2):
-                for jt in range(JT):
-                    th_t = ring.tile([P, PACK, P], F32, name="th", bufs=8)
-                    jc = slice((c % 2) * CH + jt * P, (c % 2) * CH + (jt + 1) * P)
-                    jw = slice(2 * jt * P, 2 * (jt + 1) * P)
-                    acc = psum.tile([P, BANK], F32, name="acc", bufs=3)
-                    rc = slice(b * BANK, (b + 1) * BANK)
-                    for a in range(2):
+            plane = v_plane[c // 2]
+            for b in range(PASSES):
+                for e in range(EDGE_TILES):
+                    if (c, b, e) == (2, 0, 0):
+                        tanh = keep.tile([P, PACK, P], F32, name="tanh", tag="page3", align_bytes=64)
+                    else:
+                        tanh = ring.tile([P, PACK, P], F32, name="tanh", bufs=2 * PASSES * EDGE_TILES)
+                    edge_scales = slice((c % 2) * CHUNK + e * P, (c % 2) * CHUNK + (e + 1) * P)
+                    edge_bytes = slice(2 * e * P, 2 * (e + 1) * P)
+                    acc = psum.tile([P, BANK], F32, name="acc", bufs=SUM_BANKS)
+                    r_cols = slice(b * BANK, (b + 1) * BANK)
+                    for a in range(PASSES):
                         nc.tensor.matmul_mx(
-                            acc[:], lhsT=v_w[c][:, 0, a, jw].bitcast(FP4X4), lhsT_scale=v_sc[h][:, a, 0, jc],
+                            acc[:],
+                            lhsT=v_words[c][:, 0, a, edge_bytes].bitcast(FP4X4),
+                            lhsT_scale=plane[:, a, 0, edge_scales],
                             rhs=ws_w[b][:, a, :].bitcast(FP4X4),
-                            rhs_scale=w_sc[0][:, a, rc], start=(a == 0), stop=False,
+                            rhs_scale=ws_plane[:, a, r_cols],
+                            start=(a == 0), stop=False,
                         )
                         nc.tensor.matmul_mx(
-                            acc[:], lhsT=v_w[c][:, 1, a, jw].bitcast(FP4X4), lhsT_scale=v_sc[h][:, a, 1, jc],
+                            acc[:],
+                            lhsT=v_words[c][:, 1, a, edge_bytes].bitcast(FP4X4),
+                            lhsT_scale=plane[:, a, 1, edge_scales],
                             rhs=wt_w[b][:, a, :].bitcast(FP8X4),
-                            rhs_scale=w_sc[1][:, a, rc], start=False, stop=(a == 1),
+                            rhs_scale=wt_plane[:, a, r_cols],
+                            start=False, stop=(a == PASSES - 1),
                         )
                     nc.scalar.activation(
-                        th_t[:].rearrange("p t m -> p m t"), acc[:].rearrange("p (m t) -> p m t", t=PACK), ACT.Tanh
+                        tanh[:].rearrange("p t m -> p m t"), acc[:].rearrange("p (m t) -> p m t", t=PACK), ACT.Tanh
                     )
-                    th[c, jt, b] = th_t
+                    tanhs[c, e, b] = tanh
 
         def hidden(c):
-            h_rows = ring.tile([P, 2, PACK, CH], BF16, name="h_rows", align_bytes=64)
-            h_words = keep.tile([P, 2, CH, PACK], BF16, name="h_words", tag="h_words%d" % c, align_bytes=64)
-            for b in range(2):
-                for u in range(2):
-                    turned = psum.tile([P, 2, CH], F32, name="turned", bufs=5)
-                    for e in range(2):
-                        for jt in range(JT):
-                            nc.tensor.transpose(turned[:, e, jt * P : (jt + 1) * P], th[c, jt, b][:, 2 * u + e, :], ident[:])
-                    for e in range(2):
-                        t = 2 * u + e
-                        nc.scalar.activation(h_rows[:, b, t, :], turned[:, e, :], ACT.Copy, scale=sm_t[:, b, t : t + 1])
-                (nc.vector.tensor_copy if b < IL_ON_VECTOR[c] else nc.scalar.copy)(
-                    h_words[:, b].rearrange("p (c i) t -> p c t i", i=4),
-                    h_rows[:, b].rearrange("p t (c i) -> p c t i", i=4),
-                )
-            h_w[c] = h_words
+            rows = ring.tile([P, PASSES, PACK, CHUNK], BF16, name="h_rows", align_bytes=64)
+            words = keep.tile([P, PASSES, CHUNK, PACK], BF16, name="h_words", tag="h_words%d" % c, align_bytes=64)
+            for b in range(PASSES):
+                for pair in range(2):
+                    turned = psum.tile([P, 2, CHUNK], F32, name="turned", bufs=TURN_BANKS)
+                    for s in range(2):
+                        for e in range(EDGE_TILES):
+                            nc.tensor.transpose(
+                                turned[:, s, e * P : (e + 1) * P], tanhs[c, e, b][:, 2 * pair + s, :], ident[:]
+                            )
+                    for s in range(2):
+                        t = 2 * pair + s
+                        nc.scalar.activation(rows[:, b, t, :], turned[:, s, :], ACT.Copy, scale=sm_t[:, b, t : t + 1])
+                interleave(nc.vector.tensor_copy if b == 0 else nc.scalar.copy, words[:, b], rows[:, b])
+            h_words[c] = words
 
         def quantise(c):
-            h_words = h_w[c]
-            if c == NCH - 1:
-                codes = keep.tile([P, 2, CH], U32, name="codes", tag="last", align_bytes=64)
+            if c == CHUNKS - 1:
+                codes = keep.tile([P, PASSES, CHUNK], U32, name="codes", tag="last", align_bytes=64)
             else:
-                codes = ring.tile([P, 2, CH], U32, name="codes", align_bytes=64)
-            scales = ring.tile([P, 2, CH], U8, name="scales", align_bytes=64)
+                codes = ring.tile([P, PASSES, CHUNK], U32, name="codes", align_bytes=64)
+            h_plane = ring.tile([P, PASSES, CHUNK], U8, name="h_plane", align_bytes=64)
             nc.vector.quantize_mx(
                 codes[:].rearrange("p b j -> p (b j)").bitcast(FP8X4),
-                scales[:].rearrange("p b j -> p (b j)"),
-                h_words[:].rearrange("p b j t -> p (b j t)"),
+                h_plane[:].rearrange("p b j -> p (b j)"),
+                h_words[c][:].rearrange("p b j t -> p (b j t)"),
             )
-            h_q[c] = (codes, scales)
+            h_quantised[c] = (codes, h_plane)
 
-        def gather_gates(c, n):
-            picked[c] = keep.tile([P, PACK, n * CH], F32, name="picked", tag=["picked0","h_words0","h_words1"][c], align_bytes=64)
+        def gather_gates(c, count, tag):
+            got = keep.tile([P, PACK, count * CHUNK], F32, name="picked", tag=tag, align_bytes=64)
             for t in range(PACK):
-                window = gates[t // 2][:, (t % 2) * T : (t % 2 + 1) * T]
-                nc.vector.tensor_copy(picked[c][:, t, :], window.indirect(src_list[:, c * OC : (c + n) * OC]))
+                offsets = src_list[:, c * LIST_COLS : (c + count) * LIST_COLS]
+                nc.vector.tensor_copy(got[:, t, :], gate_windows[t].indirect(offsets))
+            for i in range(count):
+                picked[c + i] = (got, i * CHUNK)
 
         def messages(c):
-            codes, scales = h_q[c]
-            for jt in range(JT):
-                jc = slice(jt * P, (jt + 1) * P)
-                y = psum.tile([P, BANK], F32, name="y", tag="turned", bufs=5)
-                for b in range(2):
+            codes, h_plane = h_quantised[c]
+            for e in range(EDGE_TILES):
+                edges = slice(e * P, (e + 1) * P)
+                y = psum.tile([P, BANK], F32, name="y", tag="turned", bufs=TURN_BANKS)
+                for b in range(PASSES):
                     nc.tensor.matmul_mx(
-                        y[:], lhsT=codes[:, b, jc].bitcast(FP8X4), lhsT_scale=scales[:, b, jc],
-                        rhs=wd_w[:, b, :].bitcast(FP4X4), rhs_scale=wd_sc[:, b, :],
-                        start=(b == 0), stop=(b == 1),
+                        y[:],
+                        lhsT=codes[:, b, edges].bitcast(FP8X4),
+                        lhsT_scale=h_plane[:, b, edges],
+                        rhs=wd_w[:, b, :].bitcast(FP4X4),
+                        rhs_scale=wd_plane[:, b, :],
+                        start=(b == 0), stop=(b == PASSES - 1),
                     )
-                if (c, jt) == (NCH - 2, JT - 1):
-                    y_w = keep.tile([P, PACK, P], F32, name="y_w", tag="last", align_bytes=64)
+                if (c, e) == (CHUNKS - 2, EDGE_TILES - 1):
+                    weighted = keep.tile([P, PACK, P], F32, name="weighted", tag="last", align_bytes=64)
+                elif (c, e) == (0, EDGE_TILES - 1):
+                    weighted = keep.tile([P, PACK, P], F32, name="weighted", tag="page2", align_bytes=64)
                 else:
-                    y_w = ring.tile([P, PACK, P], F32, name="y_w")
-                e = c * JT + jt
+                    weighted = ring.tile([P, PACK, P], F32, name="weighted")
+                tile_no = c * EDGE_TILES + e
                 nc.scalar.activation(
-                    y_w[:].rearrange("p t m -> p m t"), y[:].rearrange("p (m t) -> p m t", t=PACK),
-                    ACT.Copy, scale=wg[:, e : e + 1],
+                    weighted[:].rearrange("p t m -> p m t"), y[:].rearrange("p (m t) -> p m t", t=PACK),
+                    ACT.Copy, scale=edge_weight[:, tile_no : tile_no + 1],
                 )
-                y_turned = psum.tile([P, PACK, P], F32, name="y_turned", tag="turned", bufs=5)
+                y_turned = psum.tile([P, PACK, P], F32, name="y_turned", tag="turned", bufs=TURN_BANKS)
                 for t in range(PACK):
-                    nc.tensor.transpose(y_turned[:, t, :], y_w[:, t, :], ident[:])
-                j0 = (c % 2) * CH + jt * P
-                nc.scalar.copy(msgs[c // 2][:, :, j0 : j0 + P], y_turned[:])
+                    nc.tensor.transpose(y_turned[:, t, :], weighted[:, t, :], ident[:])
+                first = (c % 2) * CHUNK + e * P
+                nc.scalar.copy(msgs[c // 2][:, :, first : first + P], y_turned[:])
 
-        def scatter(c, t, n):
-            cols = slice((c % 2) * CH, (c % 2 + n) * CH)
+        def clear_page(t, tag):
+            pages.append(keep.tile([P, T], F32, name="page%d" % t, tag=tag, align_bytes=64))
+            nc.gpsimd.memset(pages[t][:].bitcast(I32), 0)
+
+        def scatter(c, t, count):
+            gate, first = picked[c]
             nc.vector.tensor_tensor(
-                pages[t][:].indirect(dst_list[:, c * OC : (c + n) * OC]),
-                msgs[c // 2][:, t, cols], picked[min(c, 2)][:, t, max(c - 2, 0) * CH : (max(c - 2, 0) + n) * CH], MULT,
+                pages[t][:].indirect(dst_list[:, c * LIST_COLS : (c + count) * LIST_COLS]),
+                msgs[c // 2][:, t, (c % 2) * CHUNK : (c % 2 + count) * CHUNK],
+                gate[:, t, first : first + count * CHUNK],
+                MULT,
             )
 
         sums(0)
         hidden(0)
         quantise(0)
-        gather_gates(0, 1)
+        gather_gates(0, 1, "picked0")
         sums(1)
         hidden(1)
         quantise(1)
-        gather_gates(1, 1)
+        gather_gates(1, 1, "picked1")
+        gather_gates(2, 2, "h_words0")
         messages(0)
-        scatter(0, 0, 1)
-        scatter(0, 1, 1)
-        scatter(0, 2, 1)
-        scatter(0, 3, 1)
+        clear_page(1, "h_words1")
+        clear_page(2, "page2")
+        for t in range(PACK - 1):
+            scatter(0, t, 1)
         sums(2)
         hidden(2)
+        clear_page(3, "page3")
+        scatter(0, PACK - 1, 1)
         quantise(2)
-        gather_gates(2, 2)
         messages(1)
-        scatter(1, 0, 1)
-        scatter(1, 1, 1)
-        scatter(1, 2, 1)
-        scatter(1, 3, 1)
-        sums(3)
-        hidden(3)
-        messages(2)
-        quantise(3)
-        messages(3)
-        scatter(2, 0, 1)
-        scatter(2, 1, 1)
-        scatter(2, 2, 1)
-        scatter(3, 0, 1)
-        scatter(3, 1, 1)
-        scatter(3, 2, 1)
-        scatter(2, 3, 2)
+        for t in range(PACK):
+            scatter(1, t, 1)
+        last = CHUNKS - 1
+        sums(last)
+        hidden(last)
+        messages(last - 1)
+        quantise(last)
+        messages(last)
+        for c in (last - 1, last):
+            for t in range(PACK - 1):
+                scatter(c, t, 1)
+        scatter(last - 1, PACK - 1, 2)
 
         out_rows = out_0.rearrange("(p t) c -> p t c", t=PACK)
         o_rows = keep.tile([P, PACK, T], BF16, name="o_rows", align_bytes=64)
@@ -291,22 +307,22 @@ def tile_list_msg_tanh_gateP_kernel(
             else:
                 nc.vector.tensor_copy(o_rows[:, t, : T // 2], pages[t][:, : T // 2])
                 nc.scalar.copy(o_rows[:, t, T // 2 :], pages[t][:, T // 2 :])
-        o_sc = keep.tile([P, T], U8, name="o_sc", align_bytes=64)
+
+        o_plane = keep.tile([P, T], U8, name="o_plane", align_bytes=64)
         out_words = out_1[0].rearrange("p t i -> p (t i)").bitcast(I32)
-        for s in range(T // PIECE):
-            o_words = keep.tile([P, PIECE, PACK], BF16, name="o_words%d" % s, align_bytes=64)
-            c0 = s * PIECE
-            dst = o_words[:].rearrange("p (c i) t -> p c t i", i=4)
-            src = o_rows[:, :, c0 : c0 + PIECE].rearrange("p t (c i) -> p c t i", i=4)
-            vc = [512,512,128,0][s] // 4
-            if vc < PIECE // 4:
-                nc.scalar.copy(dst[:, vc:], src[:, vc:])
-            if vc > 0:
-                nc.vector.tensor_copy(dst[:, :vc], src[:, :vc])
-            o_codes = keep.tile([P, PIECE], I32, name="o_codes%d" % s, align_bytes=64)
+        for first in range(0, T, PIECE):
+            o_words = keep.tile([P, PIECE, PACK], BF16, name="o_words%d" % first, align_bytes=64)
+            split = min(max(VECTOR_COLS - first, 0), PIECE)
+            if split < PIECE:
+                interleave(nc.scalar.copy, o_words[:, split:, :], o_rows[:, :, first + split : first + PIECE])
+            if split > 0:
+                interleave(nc.vector.tensor_copy, o_words[:, :split, :], o_rows[:, :, first : first + split])
+            o_codes = keep.tile([P, PIECE], I32, name="o_codes%d" % first, align_bytes=64)
             nc.vector.quantize_mx(
-                o_codes[:].bitcast(FP8X4), o_sc[:, c0 : c0 + PIECE], o_words[:].rearrange("p c t -> p (c t)")
+                o_codes[:].bitcast(FP8X4), o_plane[:, first : first + PIECE], o_words[:].rearrange("p c t -> p (c t)")
             )
-            nc.sync.dma_start(out_words[:, c0 : c0 + PIECE], o_codes[:])
-        for q in range(4):
-            nc.sync.dma_start(out_2[0, 4 * q : 4 * q + 4, :].bitcast(I32), o_sc[32 * q : 32 * q + 4, :].bitcast(I32))
+            nc.sync.dma_start(out_words[:, first : first + PIECE], o_codes[:])
+        for quad in range(4):
+            nc.sync.dma_start(
+                out_2[0, 4 * quad : 4 * quad + 4, :].bitcast(I32), o_plane[32 * quad : 32 * quad + 4, :].bitcast(I32)
+            )

@@ -29,8 +29,11 @@ HALF = J // 2
 SCALE_ROW = 48
 PIECE = 512
 VECTOR_COLS = 1152
+OVERLAP = 1024
+ANCHOR = (1024, 11264, 16384, 22528)
 SUM_BANKS = 3
-TURN_BANKS = 5
+TURN_BANKS = 3
+Y_BANKS = 2
 
 
 def tile_list_msg_tanh_gateP_kernel(
@@ -41,6 +44,7 @@ def tile_list_msg_tanh_gateP_kernel(
     with ExitStack() as ctx:
         keep = ctx.enter_context(tc.tile_pool(name="keep", bufs=1))
         ring = ctx.enter_context(tc.tile_pool(name="ring", bufs=2))
+        laid = ctx.enter_context(tc.tile_pool(name="laid", bufs=1))
         psum = ctx.enter_context(tc.psum_pool(name="psum", bufs=1))
 
         src_list = keep.tile([P, J // 16], U16, name="src_list")
@@ -62,6 +66,8 @@ def tile_list_msg_tanh_gateP_kernel(
         tab_rows = keep.tile([P, T // 4], I32, name="tab_rows", tag="tab_rows", align_bytes=64)
         for first, end in ((0, SCALE_ROW), (SCALE_ROW + 16, SCALE_ROW + 32), (SCALE_ROW + 48, P)):
             nc.vector.memset(tab_rows[first:end, :], 0)
+        wd_rows = keep.tile([P, PASSES, N], U8, name="wd_rows", tag="wd_rows", align_bytes=64)
+        nc.vector.memset(wd_rows[:].rearrange("p a n -> p (a n)").bitcast(I32), 0)
         wt_plane = keep.tile([P, PASSES, R], U8, name="wt_plane", align_bytes=64)
         nc.gpsimd.memset(wt_plane[:].rearrange("p a r -> p (a r)").bitcast(I32), 0)
         nc.sync.dma_start(src_list[:], offs)
@@ -87,9 +93,12 @@ def tile_list_msg_tanh_gateP_kernel(
         ident = keep.tile([P, P], F32, name="ident")
         make_identity(nc, ident[:])
         sm_t = keep.tile([P, PASSES, PACK], F32, name="sm_t")
-        wgo_rows = keep.tile([P, P], F32, name="wgo_rows", align_bytes=64)
         nc.gpsimd.dma_start(sm_t[:], sm.rearrange("(b p t) -> p b t", b=PASSES, t=PACK))
-        nc.gpsimd.dma_start(wgo_rows[:], wgo[0:16].rearrange("g (e i) -> (g e) i", i=P))
+        wd_w = keep.tile([P, PASSES, 2 * N], U8, name="wd_w", tag="wd_w", align_bytes=64)
+        nc.sync.dma_start(wd_w[:].bitcast(I32), wd_words.rearrange("a p c -> p a c").bitcast(I32))
+        load_plane(wd_rows, wd_scales, nc.sync)
+        edge_weight = keep.tile([P, J], F32, name="edge_weight", align_bytes=64)
+        nc.sync.dma_start(edge_weight[:], wgo)
 
         v_words = []
 
@@ -118,45 +127,42 @@ def tile_list_msg_tanh_gateP_kernel(
             )
             v_words.append(parted)
 
+        gT_rows = gT.rearrange("(p t) c -> p t c", t=PACK)
+        gate_windows = []
+
+        def load_gates(tag):
+            t = len(gate_windows)
+            gate_windows.append(keep.tile([P, T], F32, name="gates%d" % t, tag=tag, align_bytes=64))
+            nc.sync.dma_start(gate_windows[t][:], gT_rows[:, t, :])
+
         gather_scales(0, "got0", nc.scalar)
         gather_words(0)
-        gates = keep.tile([P, PACK * T], F32, name="gates", tag="got0", align_bytes=64)
-        gate_windows = [gates[:, t * T : (t + 1) * T] for t in range(PACK)]
-        gT_rows = gT.rearrange("(p t) c -> p t c", t=PACK)
-        wd_w = keep.tile([P, PASSES, 2 * N], U8, name="wd_w", align_bytes=64)
-        nc.sync.dma_start(wd_w[:].bitcast(I32), wd_words.rearrange("a p c -> p a c").bitcast(I32))
-        wd_plane = keep.tile([P, PASSES, N], U8, name="wd_plane", tag="both0", align_bytes=64)
-        nc.gpsimd.memset(wd_plane[:].rearrange("p a n -> p (a n)").bitcast(I32), 0)
-        load_plane(wd_plane, wd_scales, nc.sync)
-        for t in range(PACK):
-            nc.sync.dma_start(gate_windows[t], gT_rows[:, t, :])
+        load_gates("both0")
+        load_gates("got0")
         gather_words(1)
         gather_scales(1, "both1", nc.sync)
         gather_words(2)
+        load_gates("both2")
         gather_words(3)
+        load_gates("both3")
 
-        pages = [keep.tile([P, T], F32, name="page0", tag="tab_w", align_bytes=64)]
-        nc.vector.memset(pages[0][:].bitcast(I32), 0)
+        wd_dealt = keep.tile([P, PASSES, PACK, 2 * P], U8, name="wd_dealt", align_bytes=64)
+        nc.vector.tensor_copy(wd_dealt[:].bitcast(U16), wd_w[:].bitcast(U16).rearrange("p a (m t) -> p a t m", t=PACK))
+        wd_plane = keep.tile([P, PASSES, PACK, P], U8, name="wd_plane", align_bytes=64)
+        nc.vector.tensor_copy(wd_plane[:], wd_rows[:].rearrange("p a (m t) -> p a t m", t=PACK))
 
-        edge_weight = keep.tile([P, J // P], F32, name="edge_weight")
-        wgo_turned = psum.tile([P, PACK, P], F32, name="wgo_turned", tag="turned", bufs=TURN_BANKS)
-        nc.tensor.transpose(wgo_turned[:, 0, :], wgo_rows[:], ident[:])
-        nc.scalar.copy(edge_weight[:], wgo_turned[:, 0, : J // P])
-
+        pages = {}
         tanhs = {}
         h_words = {}
         h_quantised = {}
         picked = {}
-        msgs = [keep.tile([P, PACK, HALF], F32, name="msgs%d" % h) for h in range(2)]
+        msgs = keep.tile([P, PACK, J], F32, name="msgs", align_bytes=64)
 
         def sums(c):
             plane = v_plane[c // 2]
             for b in range(PASSES):
                 for e in range(EDGE_TILES):
-                    if (c, b, e) == (2, 0, 0):
-                        tanh = keep.tile([P, PACK, P], F32, name="tanh", tag="page3", align_bytes=64)
-                    else:
-                        tanh = ring.tile([P, PACK, P], F32, name="tanh", bufs=2 * PASSES * EDGE_TILES)
+                    tanh = ring.tile([P, PACK, P], F32, name="tanh", bufs=2 * PASSES * EDGE_TILES)
                     edge_scales = slice((c % 2) * CHUNK + e * P, (c % 2) * CHUNK + (e + 1) * P)
                     edge_bytes = slice(2 * e * P, 2 * (e + 1) * P)
                     acc = psum.tile([P, BANK], F32, name="acc", bufs=SUM_BANKS)
@@ -185,7 +191,9 @@ def tile_list_msg_tanh_gateP_kernel(
 
         def hidden(c):
             rows = ring.tile([P, PASSES, PACK, CHUNK], BF16, name="h_rows", align_bytes=64)
-            words = keep.tile([P, PASSES, CHUNK, PACK], BF16, name="h_words", tag="h_words%d" % c, align_bytes=64)
+            words = laid.tile(
+                [P, PASSES, CHUNK, PACK], BF16, name="h_words%d" % c, offset=ANCHOR[c] - OVERLAP, align_bytes=64
+            )
             for b in range(PASSES):
                 for pair in range(2):
                     turned = psum.tile([P, 2, CHUNK], F32, name="turned", bufs=TURN_BANKS)
@@ -197,14 +205,11 @@ def tile_list_msg_tanh_gateP_kernel(
                     for s in range(2):
                         t = 2 * pair + s
                         nc.scalar.activation(rows[:, b, t, :], turned[:, s, :], ACT.Copy, scale=sm_t[:, b, t : t + 1])
-                interleave(nc.vector.tensor_copy if b == 0 else nc.scalar.copy, words[:, b], rows[:, b])
+                interleave(nc.scalar.copy, words[:, b], rows[:, b])
             h_words[c] = words
 
         def quantise(c):
-            if c == CHUNKS - 1:
-                codes = keep.tile([P, PASSES, CHUNK], U32, name="codes", tag="last", align_bytes=64)
-            else:
-                codes = ring.tile([P, PASSES, CHUNK], U32, name="codes", align_bytes=64)
+            codes = keep.tile([P, PASSES, CHUNK], U32, name="codes", tag="codes%d" % c, align_bytes=64)
             h_plane = ring.tile([P, PASSES, CHUNK], U8, name="h_plane", align_bytes=64)
             nc.vector.quantize_mx(
                 codes[:].rearrange("p b j -> p (b j)").bitcast(FP8X4),
@@ -213,90 +218,94 @@ def tile_list_msg_tanh_gateP_kernel(
             )
             h_quantised[c] = (codes, h_plane)
 
-        def gather_gates(c, count, tag):
-            got = keep.tile([P, PACK, count * CHUNK], F32, name="picked", tag=tag, align_bytes=64)
-            for t in range(PACK):
+        def gather_gates(after, units):
+            width = sum(count for t, c, count in units) * CHUNK
+            if after is None:
+                got = keep.tile([P, width], F32, name="picked_early", align_bytes=64)
+            else:
+                got = laid.tile(
+                    [P, width], F32, name="picked%d" % after, offset=ANCHOR[after] - 4 * width, align_bytes=64
+                )
+            first = 0
+            for t, c, count in units:
                 offsets = src_list[:, c * LIST_COLS : (c + count) * LIST_COLS]
-                nc.vector.tensor_copy(got[:, t, :], gate_windows[t].indirect(offsets))
-            for i in range(count):
-                picked[c + i] = (got, i * CHUNK)
+                nc.vector.tensor_tensor(
+                    got[:, first : first + count * CHUNK],
+                    gate_windows[t][:].indirect(offsets),
+                    edge_weight[:, c * CHUNK : (c + count) * CHUNK],
+                    MULT,
+                )
+                for i in range(count):
+                    picked[t, c + i] = (got, first + i * CHUNK)
+                first = first + count * CHUNK
 
         def messages(c):
             codes, h_plane = h_quantised[c]
-            for e in range(EDGE_TILES):
-                edges = slice(e * P, (e + 1) * P)
-                y = psum.tile([P, BANK], F32, name="y", tag="turned", bufs=TURN_BANKS)
-                for b in range(PASSES):
-                    nc.tensor.matmul_mx(
-                        y[:],
-                        lhsT=codes[:, b, edges].bitcast(FP8X4),
-                        lhsT_scale=h_plane[:, b, edges],
-                        rhs=wd_w[:, b, :].bitcast(FP4X4),
-                        rhs_scale=wd_plane[:, b, :],
-                        start=(b == 0), stop=(b == PASSES - 1),
-                    )
-                if (c, e) == (CHUNKS - 2, EDGE_TILES - 1):
-                    weighted = keep.tile([P, PACK, P], F32, name="weighted", tag="last", align_bytes=64)
-                elif (c, e) == (0, EDGE_TILES - 1):
-                    weighted = keep.tile([P, PACK, P], F32, name="weighted", tag="page2", align_bytes=64)
-                else:
-                    weighted = ring.tile([P, PACK, P], F32, name="weighted")
-                tile_no = c * EDGE_TILES + e
-                nc.scalar.activation(
-                    weighted[:].rearrange("p t m -> p m t"), y[:].rearrange("p (m t) -> p m t", t=PACK),
-                    ACT.Copy, scale=edge_weight[:, tile_no : tile_no + 1],
-                )
-                y_turned = psum.tile([P, PACK, P], F32, name="y_turned", tag="turned", bufs=TURN_BANKS)
-                for t in range(PACK):
-                    nc.tensor.transpose(y_turned[:, t, :], weighted[:, t, :], ident[:])
-                first = (c % 2) * CHUNK + e * P
-                nc.scalar.copy(msgs[c // 2][:, :, first : first + P], y_turned[:])
+            for pair in range(2):
+                y = psum.tile([P, 2, CHUNK], F32, name="y", bufs=Y_BANKS)
+                for s in range(2):
+                    t = 2 * pair + s
+                    for e in range(EDGE_TILES):
+                        edges = slice(e * P, (e + 1) * P)
+                        for b in range(PASSES):
+                            nc.tensor.matmul_mx(
+                                y[:, s, edges],
+                                lhsT=wd_dealt[:, b, t, :].bitcast(FP4X4),
+                                lhsT_scale=wd_plane[:, b, t, :],
+                                rhs=codes[:, b, edges].bitcast(FP8X4),
+                                rhs_scale=h_plane[:, b, edges],
+                                start=(b == 0), stop=(b == PASSES - 1),
+                            )
+                nc.scalar.copy(msgs[:, 2 * pair : 2 * pair + 2, c * CHUNK : (c + 1) * CHUNK], y[:])
 
-        def clear_page(t, tag):
-            pages.append(keep.tile([P, T], F32, name="page%d" % t, tag=tag, align_bytes=64))
+        def clear_page(t, pool, **place):
+            pages[t] = pool.tile([P, T], F32, name="page%d" % t, align_bytes=64, **place)
             nc.gpsimd.memset(pages[t][:].bitcast(I32), 0)
 
-        def scatter(c, t, count):
-            gate, first = picked[c]
+        def scatter(t, c, count=1):
+            gate, first = picked[t, c]
             nc.vector.tensor_tensor(
                 pages[t][:].indirect(dst_list[:, c * LIST_COLS : (c + count) * LIST_COLS]),
-                msgs[c // 2][:, t, (c % 2) * CHUNK : (c % 2 + count) * CHUNK],
-                gate[:, t, first : first + count * CHUNK],
+                msgs[:, t, c * CHUNK : (c + count) * CHUNK],
+                gate[:, first : first + count * CHUNK],
                 MULT,
             )
 
-        sums(0)
-        hidden(0)
-        quantise(0)
-        gather_gates(0, 1, "picked0")
-        sums(1)
-        hidden(1)
-        quantise(1)
-        gather_gates(1, 1, "picked1")
-        gather_gates(2, 2, "h_words0")
-        messages(0)
-        clear_page(1, "h_words1")
-        clear_page(2, "page2")
-        for t in range(PACK - 1):
-            scatter(0, t, 1)
-        sums(2)
-        hidden(2)
-        clear_page(3, "page3")
-        scatter(0, PACK - 1, 1)
-        quantise(2)
-        messages(1)
-        for t in range(PACK):
-            scatter(1, t, 1)
-        last = CHUNKS - 1
-        sums(last)
-        hidden(last)
-        messages(last - 1)
-        quantise(last)
-        messages(last)
-        for c in (last - 1, last):
-            for t in range(PACK - 1):
-                scatter(c, t, 1)
-        scatter(last - 1, PACK - 1, 2)
+        def stage(c):
+            sums(c)
+            hidden(c)
+            quantise(c)
+            messages(c)
+
+        clear_page(0, keep, tag="wd_w")
+        clear_page(1, keep, tag="wd_rows")
+        gather_gates(None, [(0, 0, 4), (1, 0, 4)])
+        stage(0)
+        clear_page(2, laid, offset=ANCHOR[0])
+        clear_page(3, keep, tag="codes0")
+        gather_gates(0, [(2, 0, 1)])
+        scatter(0, 0)
+        scatter(1, 0)
+        scatter(2, 0)
+        stage(1)
+        gather_gates(1, [(3, 0, 1), (2, 1, 1)])
+        scatter(3, 0)
+        scatter(0, 1)
+        scatter(1, 1)
+        scatter(2, 1)
+        stage(2)
+        gather_gates(2, [(3, 1, 1), (2, 2, 1)])
+        scatter(3, 1)
+        scatter(0, 2)
+        scatter(1, 2)
+        scatter(2, 2)
+        stage(3)
+        gather_gates(3, [(3, 2, 2), (2, 3, 1)])
+        scatter(3, 2)
+        scatter(0, 3)
+        scatter(1, 3)
+        scatter(2, 3)
+        scatter(3, 3)
 
         out_rows = out_0.rearrange("(p t) c -> p t c", t=PACK)
         o_rows = keep.tile([P, PACK, T], BF16, name="o_rows", align_bytes=64)

@@ -25,12 +25,12 @@ CHUNK = 256
 CHUNKS = J // CHUNK
 EDGE_TILES = CHUNK // P
 LIST_COLS = CHUNK // 16
-HALF = J // 2
 SCALE_ROW = 48
 PIECE = 512
 VECTOR_COLS = 1152
 OVERLAP = 1024
 ANCHOR = (1024, 11264, 16384, 22528)
+ON_VECTOR = ()
 SUM_BANKS = 3
 TURN_BANKS = 3
 Y_BANKS = 2
@@ -65,11 +65,11 @@ def tile_list_msg_tanh_gateP_kernel(
         nc.vector.memset(ws_plane[:].rearrange("p a r -> p (a r)").bitcast(I32), 0)
         tab_rows = keep.tile([P, T // 4], I32, name="tab_rows", tag="tab_rows", align_bytes=64)
         for first, end in ((0, SCALE_ROW), (SCALE_ROW + 16, SCALE_ROW + 32), (SCALE_ROW + 48, P)):
-            nc.vector.memset(tab_rows[first:end, :], 0)
+            nc.gpsimd.memset(tab_rows[first:end, :], 0)
         wd_rows = keep.tile([P, PASSES, N], U8, name="wd_rows", tag="wd_rows", align_bytes=64)
         nc.vector.memset(wd_rows[:].rearrange("p a n -> p (a n)").bitcast(I32), 0)
         wt_plane = keep.tile([P, PASSES, R], U8, name="wt_plane", align_bytes=64)
-        nc.gpsimd.memset(wt_plane[:].rearrange("p a r -> p (a r)").bitcast(I32), 0)
+        nc.vector.memset(wt_plane[:].rearrange("p a r -> p (a r)").bitcast(I32), 0)
         nc.sync.dma_start(src_list[:], offs)
         nc.sync.dma_start(dst_list[:], offs2)
         tab_rows_src = tab_scales.rearrange("a (u x r) t -> x (a u) r t", x=2, r=4).bitcast(I32)
@@ -84,16 +84,16 @@ def tile_list_msg_tanh_gateP_kernel(
         wt_src = wt_words.rearrange("a p r i -> p a (r i)").bitcast(I32)
         nc.sync.dma_start(ws_w[0][:], ws_src[:, :, : BANK // 2])
         load_plane(ws_plane, ws_scales, nc.sync)
-        load_plane(wt_plane, wt_scales, nc.gpsimd)
+        load_plane(wt_plane, wt_scales, nc.scalar)
         nc.sync.dma_start(wt_w[0][:], wt_src[:, :, :BANK])
         nc.sync.dma_start(wt_w[1][:], wt_src[:, :, BANK:])
         nc.sync.dma_start(ws_w[1][:], ws_src[:, :, BANK // 2 :])
 
-        v_plane = [keep.tile([P, PASSES, 2, HALF], U8, name="v_plane%d" % h, align_bytes=64) for h in range(2)]
+        v_plane = {}
         ident = keep.tile([P, P], F32, name="ident")
         make_identity(nc, ident[:])
         sm_t = keep.tile([P, PASSES, PACK], F32, name="sm_t")
-        nc.gpsimd.dma_start(sm_t[:], sm.rearrange("(b p t) -> p b t", b=PASSES, t=PACK))
+        nc.sync.dma_start(sm_t[:], sm.rearrange("(b p t) -> p b t", b=PASSES, t=PACK))
         wd_w = keep.tile([P, PASSES, 2 * N], U8, name="wd_w", tag="wd_w", align_bytes=64)
         nc.sync.dma_start(wd_w[:].bitcast(I32), wd_words.rearrange("a p c -> p a c").bitcast(I32))
         load_plane(wd_rows, wd_scales, nc.sync)
@@ -102,18 +102,21 @@ def tile_list_msg_tanh_gateP_kernel(
 
         v_words = []
 
-        def gather_scales(h, tag, queue):
-            got = keep.tile([P, 2, HALF], U8, name="got%d" % h, tag=tag, align_bytes=64)
+        def gather_scales(c, count, tag, queue):
+            got = keep.tile([P, 2, count * CHUNK], U8, name="got%d" % c, tag=tag, align_bytes=64)
             for l in range(2):
-                offsets = lists[l][:, 2 * h * LIST_COLS : 2 * (h + 1) * LIST_COLS]
+                offsets = lists[l][:, c * LIST_COLS : (c + count) * LIST_COLS]
                 nc.vector.tensor_copy(got[:, l, :], tab_rows[:].bitcast(U8).indirect(offsets))
+            plane = keep.tile([P, PASSES, 2, count * CHUNK], U8, name="v_plane%d" % c, align_bytes=64)
             for a in range(PASSES):
                 for u in range(2):
                     first = SCALE_ROW + 8 * a + 4 * u
                     queue.dma_start(
-                        v_plane[h][64 * u : 64 * u + 64, a].rearrange("p l j -> p (l j)").bitcast(I32),
+                        plane[64 * u : 64 * u + 64, a].rearrange("p l j -> p (l j)").bitcast(I32),
                         got[first : first + 64].rearrange("p l j -> p (l j)").bitcast(I32),
                     )
+            for i in range(count):
+                v_plane[c + i] = (plane, i * CHUNK)
 
         def gather_words(c):
             both = keep.tile([P, 2, CHUNK], U32, name="both", tag="both%d" % c, align_bytes=64)
@@ -135,12 +138,12 @@ def tile_list_msg_tanh_gateP_kernel(
             gate_windows.append(keep.tile([P, T], F32, name="gates%d" % t, tag=tag, align_bytes=64))
             nc.sync.dma_start(gate_windows[t][:], gT_rows[:, t, :])
 
-        gather_scales(0, "got0", nc.scalar)
+        gather_scales(0, 2, "got0", nc.scalar)
         gather_words(0)
         load_gates("both0")
         load_gates("got0")
         gather_words(1)
-        gather_scales(1, "both1", nc.sync)
+        gather_scales(2, 2, "both1", nc.sync)
         gather_words(2)
         load_gates("both2")
         gather_words(3)
@@ -159,11 +162,11 @@ def tile_list_msg_tanh_gateP_kernel(
         msgs = keep.tile([P, PACK, J], F32, name="msgs", align_bytes=64)
 
         def sums(c):
-            plane = v_plane[c // 2]
+            plane, plane_first = v_plane[c]
             for b in range(PASSES):
                 for e in range(EDGE_TILES):
                     tanh = ring.tile([P, PACK, P], F32, name="tanh", bufs=2 * PASSES * EDGE_TILES)
-                    edge_scales = slice((c % 2) * CHUNK + e * P, (c % 2) * CHUNK + (e + 1) * P)
+                    edge_scales = slice(plane_first + e * P, plane_first + (e + 1) * P)
                     edge_bytes = slice(2 * e * P, 2 * (e + 1) * P)
                     acc = psum.tile([P, BANK], F32, name="acc", bufs=SUM_BANKS)
                     r_cols = slice(b * BANK, (b + 1) * BANK)
@@ -185,7 +188,7 @@ def tile_list_msg_tanh_gateP_kernel(
                             start=False, stop=(a == PASSES - 1),
                         )
                     nc.scalar.activation(
-                        tanh[:].rearrange("p t m -> p m t"), acc[:].rearrange("p (m t) -> p m t", t=PACK), ACT.Tanh
+                        tanh[:], acc[:].rearrange("p (m t) -> p t m", t=PACK), ACT.Tanh
                     )
                     tanhs[c, e, b] = tanh
 
@@ -195,6 +198,18 @@ def tile_list_msg_tanh_gateP_kernel(
                 [P, PASSES, CHUNK, PACK], BF16, name="h_words%d" % c, offset=ANCHOR[c] - OVERLAP, align_bytes=64
             )
             for b in range(PASSES):
+                if (c, b) in ON_VECTOR:
+                    for e in range(EDGE_TILES):
+                        turned = psum.tile([P, PACK, P], F32, name="turned", bufs=TURN_BANKS)
+                        for t in range(PACK):
+                            nc.tensor.transpose(turned[:, t, :], tanhs[c, e, b][:, t, :], ident[:])
+                        nc.vector.tensor_tensor(
+                            words[:, b, e * P : (e + 1) * P, :],
+                            turned[:].rearrange("p t j -> p j t"),
+                            sm_t[:, b : b + 1, :].to_broadcast([P, P, PACK]),
+                            MULT,
+                        )
+                    continue
                 for pair in range(2):
                     turned = psum.tile([P, 2, CHUNK], F32, name="turned", bufs=TURN_BANKS)
                     for s in range(2):
@@ -210,7 +225,7 @@ def tile_list_msg_tanh_gateP_kernel(
 
         def quantise(c):
             codes = keep.tile([P, PASSES, CHUNK], U32, name="codes", tag="codes%d" % c, align_bytes=64)
-            h_plane = ring.tile([P, PASSES, CHUNK], U8, name="h_plane", align_bytes=64)
+            h_plane = keep.tile([P, PASSES, CHUNK], U8, name="h_plane", tag="h_plane%d" % c, align_bytes=64)
             nc.vector.quantize_mx(
                 codes[:].rearrange("p b j -> p (b j)").bitcast(FP8X4),
                 h_plane[:].rearrange("p b j -> p (b j)"),

@@ -26,11 +26,10 @@ CHUNKS = J // CHUNK
 EDGE_TILES = CHUNK // P
 LIST_COLS = CHUNK // 16
 SCALE_ROW = 48
-PIECE = 512
+PIECES = ((0, 512), (512, 512), (1024, 512), (1536, 256), (1792, 256))
 VECTOR_COLS = 1152
 OVERLAP = 1024
 ANCHOR = (1024, 11264, 16384, 22528)
-ON_VECTOR = ()
 SUM_BANKS = 3
 TURN_BANKS = 3
 Y_BANKS = 2
@@ -193,23 +192,11 @@ def tile_list_msg_tanh_gateP_kernel(
                     tanhs[c, e, b] = tanh
 
         def hidden(c):
-            rows = ring.tile([P, PASSES, PACK, CHUNK], BF16, name="h_rows", align_bytes=64)
+            rows = ring.tile([P, PACK, PASSES * CHUNK], BF16, name="h_rows", align_bytes=64)
             words = laid.tile(
                 [P, PASSES, CHUNK, PACK], BF16, name="h_words%d" % c, offset=ANCHOR[c] - OVERLAP, align_bytes=64
             )
             for b in range(PASSES):
-                if (c, b) in ON_VECTOR:
-                    for e in range(EDGE_TILES):
-                        turned = psum.tile([P, PACK, P], F32, name="turned", bufs=TURN_BANKS)
-                        for t in range(PACK):
-                            nc.tensor.transpose(turned[:, t, :], tanhs[c, e, b][:, t, :], ident[:])
-                        nc.vector.tensor_tensor(
-                            words[:, b, e * P : (e + 1) * P, :],
-                            turned[:].rearrange("p t j -> p j t"),
-                            sm_t[:, b : b + 1, :].to_broadcast([P, P, PACK]),
-                            MULT,
-                        )
-                    continue
                 for pair in range(2):
                     turned = psum.tile([P, 2, CHUNK], F32, name="turned", bufs=TURN_BANKS)
                     for s in range(2):
@@ -219,8 +206,8 @@ def tile_list_msg_tanh_gateP_kernel(
                             )
                     for s in range(2):
                         t = 2 * pair + s
-                        nc.scalar.activation(rows[:, b, t, :], turned[:, s, :], ACT.Copy, scale=sm_t[:, b, t : t + 1])
-                interleave(nc.scalar.copy, words[:, b], rows[:, b])
+                        nc.scalar.activation(rows[:, t, b * CHUNK : (b + 1) * CHUNK], turned[:, s, :], ACT.Copy, scale=sm_t[:, b, t : t + 1])
+            interleave(nc.scalar.copy, words[:].rearrange("p b j t -> p (b j) t"), rows[:])
             h_words[c] = words
 
         def quantise(c):
@@ -316,11 +303,10 @@ def tile_list_msg_tanh_gateP_kernel(
         scatter(2, 2)
         stage(3)
         gather_gates(3, [(3, 2, 2), (2, 3, 1)])
-        scatter(3, 2)
         scatter(0, 3)
         scatter(1, 3)
         scatter(2, 3)
-        scatter(3, 3)
+        scatter(3, 2, 2)
 
         out_rows = out_0.rearrange("(p t) c -> p t c", t=PACK)
         o_rows = keep.tile([P, PACK, T], BF16, name="o_rows", align_bytes=64)
@@ -329,12 +315,12 @@ def tile_list_msg_tanh_gateP_kernel(
             if t < PACK - 1:
                 nc.scalar.copy(o_rows[:, t, :], pages[t][:])
             else:
-                nc.vector.tensor_copy(o_rows[:, t, : T // 2], pages[t][:, : T // 2])
-                nc.scalar.copy(o_rows[:, t, T // 2 :], pages[t][:, T // 2 :])
+                nc.vector.tensor_copy(o_rows[:, t, :VECTOR_COLS], pages[t][:, :VECTOR_COLS])
+                nc.scalar.copy(o_rows[:, t, VECTOR_COLS:], pages[t][:, VECTOR_COLS:])
 
         o_plane = keep.tile([P, T], U8, name="o_plane", align_bytes=64)
         out_words = out_1[0].rearrange("p t i -> p (t i)").bitcast(I32)
-        for first in range(0, T, PIECE):
+        for first, PIECE in PIECES:
             o_words = keep.tile([P, PIECE, PACK], BF16, name="o_words%d" % first, align_bytes=64)
             split = min(max(VECTOR_COLS - first, 0), PIECE)
             if split < PIECE:
@@ -347,6 +333,6 @@ def tile_list_msg_tanh_gateP_kernel(
             )
             nc.sync.dma_start(out_words[:, first : first + PIECE], o_codes[:])
         for quad in range(4):
-            nc.sync.dma_start(
+            (nc.sync, nc.scalar)[quad % 2].dma_start(
                 out_2[0, 4 * quad : 4 * quad + 4, :].bitcast(I32), o_plane[32 * quad : 32 * quad + 4, :].bitcast(I32)
             )

@@ -62,13 +62,15 @@ def tile_list_msg_tanh_gateP_kernel(
 
         ws_plane = keep.tile([P, PASSES, R], U8, name="ws_plane", align_bytes=64)
         nc.vector.memset(ws_plane[:].rearrange("p a r -> p (a r)").bitcast(I32), 0)
-        tab_rows = keep.tile([P, T // 4], I32, name="tab_rows", tag="tab_rows", align_bytes=64)
-        for first, end in ((0, SCALE_ROW), (SCALE_ROW + 16, SCALE_ROW + 32), (SCALE_ROW + 48, P)):
-            nc.gpsimd.memset(tab_rows[first:end, :], 0)
-        wd_rows = keep.tile([P, PASSES, N], U8, name="wd_rows", tag="wd_rows", align_bytes=64)
-        nc.vector.memset(wd_rows[:].rearrange("p a n -> p (a n)").bitcast(I32), 0)
         wt_plane = keep.tile([P, PASSES, R], U8, name="wt_plane", align_bytes=64)
         nc.vector.memset(wt_plane[:].rearrange("p a r -> p (a r)").bitcast(I32), 0)
+        tab_rows = keep.tile([P, T // 4], I32, name="tab_rows", tag="tab_rows", align_bytes=64)
+        for first, end in ((0, SCALE_ROW), (SCALE_ROW + 16, SCALE_ROW + 32), (SCALE_ROW + 48, P)):
+            nc.vector.memset(tab_rows[first:end, :], 0)
+        wd_rows = keep.tile([P, PASSES, N], U8, name="wd_rows", tag="wd_rows", align_bytes=64)
+        nc.vector.memset(wd_rows[:].rearrange("p a n -> p (a n)").bitcast(I32), 0)
+        pages = {0: keep.tile([P, T], F32, name="page0", align_bytes=64)}
+        nc.vector.memset(pages[0][:].bitcast(I32), 0)
         nc.sync.dma_start(src_list[:], offs)
         nc.sync.dma_start(dst_list[:], offs2)
         tab_rows_src = tab_scales.rearrange("a (u x r) t -> x (a u) r t", x=2, r=4).bitcast(I32)
@@ -153,7 +155,6 @@ def tile_list_msg_tanh_gateP_kernel(
         wd_plane = keep.tile([P, PASSES, PACK, P], U8, name="wd_plane", align_bytes=64)
         nc.vector.tensor_copy(wd_plane[:], wd_rows[:].rearrange("p a (m t) -> p a t m", t=PACK))
 
-        pages = {}
         tanhs = {}
         h_words = {}
         h_quantised = {}
@@ -279,7 +280,6 @@ def tile_list_msg_tanh_gateP_kernel(
             quantise(c)
             messages(c)
 
-        clear_page(0, keep, tag="wd_w")
         clear_page(1, keep, tag="wd_rows")
         gather_gates(None, [(0, 0, 4), (1, 0, 4)])
         stage(0)

@@ -26,13 +26,16 @@ CHUNKS = J // CHUNK
 EDGE_TILES = CHUNK // P
 LIST_COLS = CHUNK // 16
 SCALE_ROW = 48
-PIECES = ((0, 512), (512, 512), (1024, 512), (1536, 256), (1792, 256))
+LAST_PAGE = PACK - 1
+LAST_CHUNK = CHUNKS - 1
+PIECES = (512, 512, 512, 256, 256)
 VECTOR_COLS = 1152
-OVERLAP = 1024
-ANCHOR = (1024, 11264, 16384, 22528)
-SUM_BANKS = 3
-TURN_BANKS = 3
-Y_BANKS = 2
+PAGE_BYTES = 4 * T
+GATE_BYTES = 4 * CHUNK
+WORD_BYTES = 2 * 4 * CHUNK
+HIDDEN_BYTES = 2 * PASSES * CHUNK * PACK
+SUM_BANKS = 4
+TURN_BANKS = 4
 
 
 def tile_list_msg_tanh_gateP_kernel(
@@ -45,6 +48,19 @@ def tile_list_msg_tanh_gateP_kernel(
         ring = ctx.enter_context(tc.tile_pool(name="ring", bufs=2))
         laid = ctx.enter_context(tc.tile_pool(name="laid", bufs=1))
         psum = ctx.enter_context(tc.psum_pool(name="psum", bufs=1))
+
+        held_gates = [[(2, 0, 1)]]
+        for c in range(1, CHUNKS):
+            held_gates.append([(LAST_PAGE, c - 1, 2 if c == LAST_CHUNK else 1), (2, c, 1)])
+
+        gates_end = []
+        free_byte = 0
+        for c in range(CHUNKS):
+            gates_end.append(free_byte + GATE_BYTES * sum(count for t, first, count in held_gates[c]))
+            free_byte = gates_end[c] + (PAGE_BYTES if c == 0 else HIDDEN_BYTES - GATE_BYTES)
+        words_at = [free_byte, free_byte + PAGE_BYTES]
+        words_at.extend(words_at[1] + WORD_BYTES + i * PAGE_BYTES for i in range(2))
+        words_room = [3 * PAGE_BYTES + WORD_BYTES, WORD_BYTES, PAGE_BYTES, PAGE_BYTES]
 
         src_list = keep.tile([P, J // 16], U16, name="src_list")
         dst_list = keep.tile([P, J // 16], U16, name="dst_list")
@@ -64,7 +80,7 @@ def tile_list_msg_tanh_gateP_kernel(
         nc.vector.memset(ws_plane[:].rearrange("p a r -> p (a r)").bitcast(I32), 0)
         wt_plane = keep.tile([P, PASSES, R], U8, name="wt_plane", align_bytes=64)
         nc.vector.memset(wt_plane[:].rearrange("p a r -> p (a r)").bitcast(I32), 0)
-        tab_rows = keep.tile([P, T // 4], I32, name="tab_rows", tag="tab_rows", align_bytes=64)
+        tab_rows = keep.tile([P, T // 4], I32, name="tab_rows", align_bytes=64)
         for first, end in ((0, SCALE_ROW), (SCALE_ROW + 16, SCALE_ROW + 32), (SCALE_ROW + 48, P)):
             nc.vector.memset(tab_rows[first:end, :], 0)
         wd_rows = keep.tile([P, PASSES, N], U8, name="wd_rows", tag="wd_rows", align_bytes=64)
@@ -76,7 +92,7 @@ def tile_list_msg_tanh_gateP_kernel(
         tab_rows_src = tab_scales.rearrange("a (u x r) t -> x (a u) r t", x=2, r=4).bitcast(I32)
         for x in range(2):
             nc.sync.dma_start(tab_rows[SCALE_ROW + 32 * x : SCALE_ROW + 32 * x + 16, :], tab_rows_src[x])
-        tab_w = keep.tile([P, T], I32, name="tab_w", tag="tab_w", align_bytes=64)
+        tab_w = keep.tile([P, T], I32, name="tab_w", align_bytes=64)
         nc.sync.dma_start(tab_w[:], tab_words[0].rearrange("p t i -> p (t i)").bitcast(I32))
 
         ws_w = [keep.tile([P, PASSES, BANK // 2], I32, name="ws_w%d" % b, align_bytes=64) for b in range(PASSES)]
@@ -90,21 +106,21 @@ def tile_list_msg_tanh_gateP_kernel(
         nc.sync.dma_start(wt_w[1][:], wt_src[:, :, BANK:])
         nc.sync.dma_start(ws_w[1][:], ws_src[:, :, BANK // 2 :])
 
-        v_plane = {}
         ident = keep.tile([P, P], F32, name="ident")
         make_identity(nc, ident[:])
         sm_t = keep.tile([P, PASSES, PACK], F32, name="sm_t")
         nc.sync.dma_start(sm_t[:], sm.rearrange("(b p t) -> p b t", b=PASSES, t=PACK))
-        wd_w = keep.tile([P, PASSES, 2 * N], U8, name="wd_w", tag="wd_w", align_bytes=64)
+        wd_w = keep.tile([P, PASSES, 2 * N], U8, name="wd_w", align_bytes=64)
         nc.sync.dma_start(wd_w[:].bitcast(I32), wd_words.rearrange("a p c -> p a c").bitcast(I32))
         load_plane(wd_rows, wd_scales, nc.sync)
         edge_weight = keep.tile([P, J], F32, name="edge_weight", align_bytes=64)
         nc.sync.dma_start(edge_weight[:], wgo)
 
+        v_plane = {}
         v_words = []
 
-        def gather_scales(c, count, tag, queue):
-            got = keep.tile([P, 2, count * CHUNK], U8, name="got%d" % c, tag=tag, align_bytes=64)
+        def gather_scales(c, count, queue, pool, **place):
+            got = pool.tile([P, 2, count * CHUNK], U8, name="got%d" % c, align_bytes=64, **place)
             for l in range(2):
                 offsets = lists[l][:, c * LIST_COLS : (c + count) * LIST_COLS]
                 nc.vector.tensor_copy(got[:, l, :], tab_rows[:].bitcast(U8).indirect(offsets))
@@ -120,35 +136,35 @@ def tile_list_msg_tanh_gateP_kernel(
                 v_plane[c + i] = (plane, i * CHUNK)
 
         def gather_words(c):
-            both = keep.tile([P, 2, CHUNK], U32, name="both", tag="both%d" % c, align_bytes=64)
+            room = laid.tile([P, words_room[c] // 4], U32, name="both%d" % c, offset=words_at[c], align_bytes=64)
+            both = room[:, : 2 * CHUNK].rearrange("p (l j) -> p l j", l=2)
             for l in range(2):
                 offsets = lists[l][:, c * LIST_COLS : (c + 1) * LIST_COLS]
                 nc.vector.tensor_copy(both[:, l, :], tab_w[:].bitcast(U32).indirect(offsets))
             parted = keep.tile([P, 2, PASSES, 2 * CHUNK], U8, name="parted%d" % c, align_bytes=64)
             nc.vector.tensor_copy(
                 parted[:].bitcast(U16),
-                both[:].bitcast(U16).rearrange("p l (j a) -> p l a j", a=PASSES),
+                both.bitcast(U16).rearrange("p l (j a) -> p l a j", a=PASSES),
             )
             v_words.append(parted)
 
         gT_rows = gT.rearrange("(p t) c -> p t c", t=PACK)
         gate_windows = []
 
-        def load_gates(tag):
+        def load_gates(pool, **place):
             t = len(gate_windows)
-            gate_windows.append(keep.tile([P, T], F32, name="gates%d" % t, tag=tag, align_bytes=64))
+            gate_windows.append(pool.tile([P, T], F32, name="gates%d" % t, align_bytes=64, **place))
             nc.sync.dma_start(gate_windows[t][:], gT_rows[:, t, :])
 
-        gather_scales(0, 2, "got0", nc.scalar)
+        gather_scales(0, 2, nc.scalar, keep, tag="got0")
         gather_words(0)
-        load_gates("both0")
-        load_gates("got0")
+        load_gates(laid, offset=words_at[0])
+        load_gates(keep, tag="got0")
         gather_words(1)
-        gather_scales(2, 2, "both1", nc.sync)
-        gather_words(2)
-        load_gates("both2")
-        gather_words(3)
-        load_gates("both3")
+        gather_scales(2, 2, nc.sync, laid, offset=words_at[1])
+        for c in (2, 3):
+            gather_words(c)
+            load_gates(laid, offset=words_at[c])
 
         wd_dealt = keep.tile([P, PASSES, PACK, 2 * P], U8, name="wd_dealt", align_bytes=64)
         nc.vector.tensor_copy(wd_dealt[:].bitcast(U16), wd_w[:].bitcast(U16).rearrange("p a (m t) -> p a t m", t=PACK))
@@ -187,15 +203,13 @@ def tile_list_msg_tanh_gateP_kernel(
                             rhs_scale=wt_plane[:, a, r_cols],
                             start=False, stop=(a == PASSES - 1),
                         )
-                    nc.scalar.activation(
-                        tanh[:], acc[:].rearrange("p (m t) -> p t m", t=PACK), ACT.Tanh
-                    )
+                    nc.scalar.activation(tanh[:], acc[:].rearrange("p (m t) -> p t m", t=PACK), ACT.Tanh)
                     tanhs[c, e, b] = tanh
 
         def hidden(c):
             rows = ring.tile([P, PACK, PASSES * CHUNK], BF16, name="h_rows", align_bytes=64)
             words = laid.tile(
-                [P, PASSES, CHUNK, PACK], BF16, name="h_words%d" % c, offset=ANCHOR[c] - OVERLAP, align_bytes=64
+                [P, PASSES, CHUNK, PACK], BF16, name="h_words%d" % c, offset=gates_end[c] - GATE_BYTES, align_bytes=64
             )
             for b in range(PASSES):
                 for pair in range(2):
@@ -207,13 +221,16 @@ def tile_list_msg_tanh_gateP_kernel(
                             )
                     for s in range(2):
                         t = 2 * pair + s
-                        nc.scalar.activation(rows[:, t, b * CHUNK : (b + 1) * CHUNK], turned[:, s, :], ACT.Copy, scale=sm_t[:, b, t : t + 1])
+                        nc.scalar.activation(
+                            rows[:, t, b * CHUNK : (b + 1) * CHUNK], turned[:, s, :],
+                            ACT.Copy, scale=sm_t[:, b, t : t + 1],
+                        )
             interleave(nc.scalar.copy, words[:].rearrange("p b j t -> p (b j) t"), rows[:])
             h_words[c] = words
 
         def quantise(c):
             codes = keep.tile([P, PASSES, CHUNK], U32, name="codes", tag="codes%d" % c, align_bytes=64)
-            h_plane = keep.tile([P, PASSES, CHUNK], U8, name="h_plane", tag="h_plane%d" % c, align_bytes=64)
+            h_plane = keep.tile([P, PASSES, CHUNK], U8, name="h_plane%d" % c, align_bytes=64)
             nc.vector.quantize_mx(
                 codes[:].rearrange("p b j -> p (b j)").bitcast(FP8X4),
                 h_plane[:].rearrange("p b j -> p (b j)"),
@@ -221,14 +238,10 @@ def tile_list_msg_tanh_gateP_kernel(
             )
             h_quantised[c] = (codes, h_plane)
 
-        def gather_gates(after, units):
-            width = sum(count for t, c, count in units) * CHUNK
-            if after is None:
-                got = keep.tile([P, width], F32, name="picked_early", align_bytes=64)
-            else:
-                got = laid.tile(
-                    [P, width], F32, name="picked%d" % after, offset=ANCHOR[after] - 4 * width, align_bytes=64
-                )
+        def gate_columns(units):
+            return CHUNK * sum(count for t, c, count in units)
+
+        def gather_gates(got, units):
             first = 0
             for t, c, count in units:
                 offsets = src_list[:, c * LIST_COLS : (c + count) * LIST_COLS]
@@ -244,22 +257,20 @@ def tile_list_msg_tanh_gateP_kernel(
 
         def messages(c):
             codes, h_plane = h_quantised[c]
-            for pair in range(2):
-                y = psum.tile([P, 2, CHUNK], F32, name="y", bufs=Y_BANKS)
-                for s in range(2):
-                    t = 2 * pair + s
-                    for e in range(EDGE_TILES):
-                        edges = slice(e * P, (e + 1) * P)
-                        for b in range(PASSES):
-                            nc.tensor.matmul_mx(
-                                y[:, s, edges],
-                                lhsT=wd_dealt[:, b, t, :].bitcast(FP4X4),
-                                lhsT_scale=wd_plane[:, b, t, :],
-                                rhs=codes[:, b, edges].bitcast(FP8X4),
-                                rhs_scale=h_plane[:, b, edges],
-                                start=(b == 0), stop=(b == PASSES - 1),
-                            )
-                nc.scalar.copy(msgs[:, 2 * pair : 2 * pair + 2, c * CHUNK : (c + 1) * CHUNK], y[:])
+            for t in range(PACK):
+                y = psum.tile([P, CHUNK], F32, name="y", tag="turned", bufs=TURN_BANKS)
+                for e in range(EDGE_TILES):
+                    edges = slice(e * P, (e + 1) * P)
+                    for b in range(PASSES):
+                        nc.tensor.matmul_mx(
+                            y[:, edges],
+                            lhsT=wd_dealt[:, b, t, :].bitcast(FP4X4),
+                            lhsT_scale=wd_plane[:, b, t, :],
+                            rhs=codes[:, b, edges].bitcast(FP8X4),
+                            rhs_scale=h_plane[:, b, edges],
+                            start=(b == 0), stop=(b == PASSES - 1),
+                        )
+                nc.scalar.copy(msgs[:, t, c * CHUNK : (c + 1) * CHUNK], y[:])
 
         def clear_page(t, pool, **place):
             pages[t] = pool.tile([P, T], F32, name="page%d" % t, align_bytes=64, **place)
@@ -274,45 +285,33 @@ def tile_list_msg_tanh_gateP_kernel(
                 MULT,
             )
 
-        def stage(c):
+        clear_page(1, keep, tag="wd_rows")
+        early_gates = [(0, 0, CHUNKS), (1, 0, CHUNKS)]
+        gather_gates(keep.tile([P, gate_columns(early_gates)], F32, name="picked", align_bytes=64), early_gates)
+        for c in range(CHUNKS):
             sums(c)
             hidden(c)
             quantise(c)
             messages(c)
-
-        clear_page(1, keep, tag="wd_rows")
-        gather_gates(None, [(0, 0, 4), (1, 0, 4)])
-        stage(0)
-        clear_page(2, laid, offset=ANCHOR[0])
-        clear_page(3, keep, tag="codes0")
-        gather_gates(0, [(2, 0, 1)])
-        scatter(0, 0)
-        scatter(1, 0)
-        scatter(2, 0)
-        stage(1)
-        gather_gates(1, [(3, 0, 1), (2, 1, 1)])
-        scatter(3, 0)
-        scatter(0, 1)
-        scatter(1, 1)
-        scatter(2, 1)
-        stage(2)
-        gather_gates(2, [(3, 1, 1), (2, 2, 1)])
-        scatter(3, 1)
-        scatter(0, 2)
-        scatter(1, 2)
-        scatter(2, 2)
-        stage(3)
-        gather_gates(3, [(3, 2, 2), (2, 3, 1)])
-        scatter(0, 3)
-        scatter(1, 3)
-        scatter(2, 3)
-        scatter(3, 2, 2)
+            if c == 0:
+                clear_page(2, laid, offset=gates_end[0])
+                clear_page(LAST_PAGE, keep, tag="codes0")
+            columns = gate_columns(held_gates[c])
+            got = laid.tile(
+                [P, columns], F32, name="picked%d" % c, offset=gates_end[c] - 4 * columns, align_bytes=64
+            )
+            gather_gates(got, held_gates[c])
+            if 0 < c < LAST_CHUNK:
+                scatter(LAST_PAGE, c - 1)
+            for t in range(LAST_PAGE):
+                scatter(t, c)
+        scatter(LAST_PAGE, LAST_CHUNK - 1, 2)
 
         out_rows = out_0.rearrange("(p t) c -> p t c", t=PACK)
         o_rows = keep.tile([P, PACK, T], BF16, name="o_rows", align_bytes=64)
         for t in range(PACK):
             nc.sync.dma_start(out_rows[:, t, :], pages[t][:])
-            if t < PACK - 1:
+            if t < LAST_PAGE:
                 nc.scalar.copy(o_rows[:, t, :], pages[t][:])
             else:
                 nc.vector.tensor_copy(o_rows[:, t, :VECTOR_COLS], pages[t][:, :VECTOR_COLS])
@@ -320,18 +319,20 @@ def tile_list_msg_tanh_gateP_kernel(
 
         o_plane = keep.tile([P, T], U8, name="o_plane", align_bytes=64)
         out_words = out_1[0].rearrange("p t i -> p (t i)").bitcast(I32)
-        for first, PIECE in PIECES:
-            o_words = keep.tile([P, PIECE, PACK], BF16, name="o_words%d" % first, align_bytes=64)
-            split = min(max(VECTOR_COLS - first, 0), PIECE)
-            if split < PIECE:
-                interleave(nc.scalar.copy, o_words[:, split:, :], o_rows[:, :, first + split : first + PIECE])
+        first = 0
+        for width in PIECES:
+            o_words = keep.tile([P, width, PACK], BF16, name="o_words%d" % first, align_bytes=64)
+            split = min(max(VECTOR_COLS - first, 0), width)
+            if split < width:
+                interleave(nc.scalar.copy, o_words[:, split:, :], o_rows[:, :, first + split : first + width])
             if split > 0:
                 interleave(nc.vector.tensor_copy, o_words[:, :split, :], o_rows[:, :, first : first + split])
-            o_codes = keep.tile([P, PIECE], I32, name="o_codes%d" % first, align_bytes=64)
+            o_codes = keep.tile([P, width], I32, name="o_codes%d" % first, align_bytes=64)
             nc.vector.quantize_mx(
-                o_codes[:].bitcast(FP8X4), o_plane[:, first : first + PIECE], o_words[:].rearrange("p c t -> p (c t)")
+                o_codes[:].bitcast(FP8X4), o_plane[:, first : first + width], o_words[:].rearrange("p c t -> p (c t)")
             )
-            nc.sync.dma_start(out_words[:, first : first + PIECE], o_codes[:])
+            nc.sync.dma_start(out_words[:, first : first + width], o_codes[:])
+            first = first + width
         for quad in range(4):
             (nc.sync, nc.scalar)[quad % 2].dma_start(
                 out_2[0, 4 * quad : 4 * quad + 4, :].bitcast(I32), o_plane[32 * quad : 32 * quad + 4, :].bitcast(I32)

@@ -35,7 +35,6 @@ GATE_BYTES = 4 * CHUNK
 WORD_BYTES = 2 * 4 * CHUNK
 HIDDEN_BYTES = 2 * PASSES * CHUNK * PACK
 SUM_BANKS = 4
-TURN_BANKS = 4
 
 
 def tile_list_msg_tanh_gateP_kernel(
@@ -49,72 +48,74 @@ def tile_list_msg_tanh_gateP_kernel(
         laid = ctx.enter_context(tc.tile_pool(name="laid", bufs=1))
         psum = ctx.enter_context(tc.psum_pool(name="psum", bufs=1))
 
-        held_gates = [[(2, 0, 1)]]
-        for c in range(1, CHUNKS):
-            held_gates.append([(LAST_PAGE, c - 1, 2 if c == LAST_CHUNK else 1), (2, c, 1)])
+        held_gates = [[(2, 0, 3)], [(3, 0, 1)], [(3, 1, 1)], [(3, 2, 2), (2, 3, 1)]]
 
-        gates_end = []
+        rows_at = []
         free_byte = 0
         for c in range(CHUNKS):
-            gates_end.append(free_byte + GATE_BYTES * sum(count for t, first, count in held_gates[c]))
-            free_byte = gates_end[c] + (PAGE_BYTES if c == 0 else HIDDEN_BYTES - GATE_BYTES)
-        words_at = [free_byte, free_byte + PAGE_BYTES]
-        words_at.extend(words_at[1] + WORD_BYTES + i * PAGE_BYTES for i in range(2))
-        words_room = [3 * PAGE_BYTES + WORD_BYTES, WORD_BYTES, PAGE_BYTES, PAGE_BYTES]
+            rows_at.append(free_byte)
+            free_byte = free_byte + max(HIDDEN_BYTES, GATE_BYTES * sum(count for t, first, count in held_gates[c]))
+        page_at = {2: free_byte, 3: free_byte + PAGE_BYTES}
+        hidden_at = [page_at[3] - HIDDEN_BYTES // 2]
+        free_byte = free_byte + 2 * PAGE_BYTES
+        hidden_at.extend(free_byte + (i % 2) * HIDDEN_BYTES for i in range(LAST_CHUNK))
+        free_byte = free_byte + 2 * HIDDEN_BYTES
+        staged_at = rows_at[0]
+        rest_at = free_byte
+        late_at = rest_at
+        window0_at = late_at + 64 + 4 * PASSES * BANK + 2 * PASSES * BANK
+        words1_at = window0_at + PAGE_BYTES
+        edge_at = words1_at + WORD_BYTES
+        wd_plane_at = edge_at + 4 * J
+        words2_at = wd_plane_at + PASSES * N
+        page_at[0] = words2_at + 2 * PAGE_BYTES
+        page_at[1] = page_at[0] + PAGE_BYTES
+        wd_at = page_at[1] - PASSES * N
+        rest_end = page_at[1] + PAGE_BYTES
 
         src_list = keep.tile([P, J // 16], U16, name="src_list")
         dst_list = keep.tile([P, J // 16], U16, name="dst_list")
         lists = (src_list, dst_list)
 
-        def load_plane(plane, plane_src, queue):
-            for quad in range(4):
-                queue.dma_start(
-                    plane[32 * quad : 32 * quad + 4].bitcast(I32),
-                    plane_src[:, 4 * quad : 4 * quad + 4, :].rearrange("a q c -> q a c").bitcast(I32),
-                )
-
         def interleave(copy, words, rows):
             copy(words.rearrange("p (c i) t -> p c t i", i=4), rows.rearrange("p t (c i) -> p c t i", i=4))
 
-        ws_plane = keep.tile([P, PASSES, R], U8, name="ws_plane", align_bytes=64)
-        nc.vector.memset(ws_plane[:].rearrange("p a r -> p (a r)").bitcast(I32), 0)
-        wt_plane = keep.tile([P, PASSES, R], U8, name="wt_plane", align_bytes=64)
-        nc.vector.memset(wt_plane[:].rearrange("p a r -> p (a r)").bitcast(I32), 0)
+        planes = keep.tile([P, PASSES, 2 * R + N], U8, name="planes", align_bytes=64)
+        nc.vector.memset(planes[:].rearrange("p a r -> p (a r)").bitcast(I32), 0)
+        ws_plane = planes[:, :, :R]
+        wt_plane = planes[:, :, R : 2 * R]
+        wd_rows = planes[:, :, 2 * R :]
+        staged = laid.tile([16, PASSES, 2 * R + N], U8, name="staged", offset=staged_at, align_bytes=64)
+        for scales, first, width in ((ws_scales, 0, R), (wt_scales, R, R), (wd_scales, 2 * R, N)):
+            nc.scalar.dma_start(
+                staged[:, :, first : first + width].bitcast(I32), scales.rearrange("a q c -> q a c").bitcast(I32)
+            )
         tab_rows = keep.tile([P, T // 4], I32, name="tab_rows", align_bytes=64)
         for first, end in ((0, SCALE_ROW), (SCALE_ROW + 16, SCALE_ROW + 32), (SCALE_ROW + 48, P)):
             nc.vector.memset(tab_rows[first:end, :], 0)
-        wd_rows = keep.tile([P, PASSES, N], U8, name="wd_rows", tag="wd_rows", align_bytes=64)
-        nc.vector.memset(wd_rows[:].rearrange("p a n -> p (a n)").bitcast(I32), 0)
-        pages = {0: keep.tile([P, T], F32, name="page0", align_bytes=64)}
-        nc.vector.memset(pages[0][:].bitcast(I32), 0)
+        pages = {}
         nc.sync.dma_start(src_list[:], offs)
-        nc.sync.dma_start(dst_list[:], offs2)
         tab_rows_src = tab_scales.rearrange("a (u x r) t -> x (a u) r t", x=2, r=4).bitcast(I32)
         for x in range(2):
             nc.sync.dma_start(tab_rows[SCALE_ROW + 32 * x : SCALE_ROW + 32 * x + 16, :], tab_rows_src[x])
+        nc.sync.dma_start(dst_list[:], offs2)
         tab_w = keep.tile([P, T], I32, name="tab_w", align_bytes=64)
         nc.sync.dma_start(tab_w[:], tab_words[0].rearrange("p t i -> p (t i)").bitcast(I32))
 
-        ws_w = [keep.tile([P, PASSES, BANK // 2], I32, name="ws_w%d" % b, align_bytes=64) for b in range(PASSES)]
-        wt_w = [keep.tile([P, PASSES, BANK], I32, name="wt_w%d" % b, align_bytes=64) for b in range(PASSES)]
         ws_src = ws_words.rearrange("a p c -> p a c").bitcast(I32)
         wt_src = wt_words.rearrange("a p r i -> p a (r i)").bitcast(I32)
-        nc.sync.dma_start(ws_w[0][:], ws_src[:, :, : BANK // 2])
-        load_plane(ws_plane, ws_scales, nc.sync)
-        load_plane(wt_plane, wt_scales, nc.scalar)
+        wt_w = [keep.tile([P, PASSES, BANK], I32, name="wt_w0", align_bytes=64)]
         nc.sync.dma_start(wt_w[0][:], wt_src[:, :, :BANK])
-        nc.sync.dma_start(wt_w[1][:], wt_src[:, :, BANK:])
-        nc.sync.dma_start(ws_w[1][:], ws_src[:, :, BANK // 2 :])
+        ws_w = [keep.tile([P, PASSES, BANK // 2], I32, name="ws_w0", align_bytes=64)]
+        nc.sync.dma_start(ws_w[0][:], ws_src[:, :, : BANK // 2])
+        for quad in range(4):
+            nc.scalar.dma_start(
+                planes[32 * quad : 32 * quad + 4].rearrange("p a r -> p (a r)").bitcast(I32),
+                staged[4 * quad : 4 * quad + 4].rearrange("p a r -> p (a r)").bitcast(I32),
+            )
 
         ident = keep.tile([P, P], F32, name="ident")
         make_identity(nc, ident[:])
-        sm_t = keep.tile([P, PASSES, PACK], F32, name="sm_t")
-        nc.sync.dma_start(sm_t[:], sm.rearrange("(b p t) -> p b t", b=PASSES, t=PACK))
-        wd_w = keep.tile([P, PASSES, 2 * N], U8, name="wd_w", align_bytes=64)
-        nc.sync.dma_start(wd_w[:].bitcast(I32), wd_words.rearrange("a p c -> p a c").bitcast(I32))
-        load_plane(wd_rows, wd_scales, nc.sync)
-        edge_weight = keep.tile([P, J], F32, name="edge_weight", align_bytes=64)
-        nc.sync.dma_start(edge_weight[:], wgo)
 
         v_plane = {}
         v_words = []
@@ -135,18 +136,19 @@ def tile_list_msg_tanh_gateP_kernel(
             for i in range(count):
                 v_plane[c + i] = (plane, i * CHUNK)
 
-        def gather_words(c):
-            room = laid.tile([P, words_room[c] // 4], U32, name="both%d" % c, offset=words_at[c], align_bytes=64)
-            both = room[:, : 2 * CHUNK].rearrange("p (l j) -> p l j", l=2)
+        def gather_words(c, count, room_at, room_end):
+            room = laid.tile([P, (room_end - room_at) // 4], U32, name="both%d" % c, offset=room_at, align_bytes=64)
+            both = room[:, : 2 * count * CHUNK].rearrange("p (l j) -> p l j", l=2)
             for l in range(2):
-                offsets = lists[l][:, c * LIST_COLS : (c + 1) * LIST_COLS]
+                offsets = lists[l][:, c * LIST_COLS : (c + count) * LIST_COLS]
                 nc.vector.tensor_copy(both[:, l, :], tab_w[:].bitcast(U32).indirect(offsets))
-            parted = keep.tile([P, 2, PASSES, 2 * CHUNK], U8, name="parted%d" % c, align_bytes=64)
+            parted = keep.tile([P, 2, PASSES, count * 2 * CHUNK], U8, name="parted%d" % c, align_bytes=64)
             nc.vector.tensor_copy(
                 parted[:].bitcast(U16),
                 both.bitcast(U16).rearrange("p l (j a) -> p l a j", a=PASSES),
             )
-            v_words.append(parted)
+            for i in range(count):
+                v_words.append(parted[:, :, :, i * 2 * CHUNK : (i + 1) * 2 * CHUNK])
 
         gT_rows = gT.rearrange("(p t) c -> p t c", t=PACK)
         gate_windows = []
@@ -157,21 +159,35 @@ def tile_list_msg_tanh_gateP_kernel(
             nc.sync.dma_start(gate_windows[t][:], gT_rows[:, t, :])
 
         gather_scales(0, 2, nc.scalar, keep, tag="got0")
-        gather_words(0)
-        load_gates(laid, offset=words_at[0])
+        gather_words(0, 1, rest_at, rest_end)
+        wt_w.append(laid.tile([P, PASSES, BANK], I32, name="wt_w1", offset=late_at + 64, align_bytes=64))
+        nc.sync.dma_start(wt_w[1][:], wt_src[:, :, BANK:])
+        ws_w.append(
+            laid.tile([P, PASSES, BANK // 2], I32, name="ws_w1", offset=late_at + 64 + 4 * PASSES * BANK, align_bytes=64)
+        )
+        nc.sync.dma_start(ws_w[1][:], ws_src[:, :, BANK // 2 :])
+        sm_t = laid.tile([P, PASSES, PACK], F32, name="sm_t", offset=late_at, align_bytes=64)
+        nc.sync.dma_start(sm_t[:], sm.rearrange("(b p t) -> p b t", b=PASSES, t=PACK))
+
+        wd_w = laid.tile([P, PASSES, 2 * N], U8, name="wd_w", offset=wd_at, align_bytes=64)
+        nc.sync.dma_start(wd_w[:].bitcast(I32), wd_words.rearrange("a p c -> p a c").bitcast(I32))
+        edge_weight = laid.tile([P, J], F32, name="edge_weight", offset=edge_at, align_bytes=64)
+        nc.sync.dma_start(edge_weight[:], wgo)
+        load_gates(laid, offset=window0_at)
         load_gates(keep, tag="got0")
-        gather_words(1)
-        gather_scales(2, 2, nc.sync, laid, offset=words_at[1])
-        for c in (2, 3):
-            gather_words(c)
-            load_gates(laid, offset=words_at[c])
+        gather_words(1, 1, words1_at, edge_at)
+        gather_scales(2, 2, nc.sync, laid, offset=words1_at)
+        gather_words(2, 2, words2_at, wd_at)
+        for i in range(2):
+            load_gates(laid, offset=words2_at + i * PAGE_BYTES)
 
         wd_dealt = keep.tile([P, PASSES, PACK, 2 * P], U8, name="wd_dealt", align_bytes=64)
         nc.vector.tensor_copy(wd_dealt[:].bitcast(U16), wd_w[:].bitcast(U16).rearrange("p a (m t) -> p a t m", t=PACK))
-        wd_plane = keep.tile([P, PASSES, PACK, P], U8, name="wd_plane", align_bytes=64)
-        nc.vector.tensor_copy(wd_plane[:], wd_rows[:].rearrange("p a (m t) -> p a t m", t=PACK))
+        wd_plane = laid.tile([P, PASSES, PACK, P], U8, name="wd_plane", offset=wd_plane_at, align_bytes=64)
+        nc.vector.tensor_copy(wd_plane[:], wd_rows.rearrange("p a (m t) -> p a t m", t=PACK))
 
         tanhs = {}
+        h_rows = {}
         h_words = {}
         h_quantised = {}
         picked = {}
@@ -206,30 +222,34 @@ def tile_list_msg_tanh_gateP_kernel(
                     nc.scalar.activation(tanh[:], acc[:].rearrange("p (m t) -> p t m", t=PACK), ACT.Tanh)
                     tanhs[c, e, b] = tanh
 
-        def hidden(c):
-            rows = ring.tile([P, PACK, PASSES * CHUNK], BF16, name="h_rows", align_bytes=64)
-            words = laid.tile(
-                [P, PASSES, CHUNK, PACK], BF16, name="h_words%d" % c, offset=gates_end[c] - GATE_BYTES, align_bytes=64
-            )
-            for b in range(PASSES):
-                for pair in range(2):
-                    turned = psum.tile([P, 2, CHUNK], F32, name="turned", bufs=TURN_BANKS)
-                    for s in range(2):
-                        for e in range(EDGE_TILES):
-                            nc.tensor.transpose(
-                                turned[:, s, e * P : (e + 1) * P], tanhs[c, e, b][:, 2 * pair + s, :], ident[:]
-                            )
-                    for s in range(2):
-                        t = 2 * pair + s
-                        nc.scalar.activation(
-                            rows[:, t, b * CHUNK : (b + 1) * CHUNK], turned[:, s, :],
-                            ACT.Copy, scale=sm_t[:, b, t : t + 1],
+        def hidden(c, b):
+            if b == 0:
+                h_rows[c] = laid.tile(
+                    [P, PACK, PASSES * CHUNK], BF16, name="h_rows%d" % c, offset=rows_at[c], align_bytes=64
+                )
+            for pair in range(2):
+                turned = psum.tile([P, 2, CHUNK], F32, name="turned", tag="turn%d" % (2 * b + pair))
+                for s in range(2):
+                    for e in range(EDGE_TILES):
+                        nc.tensor.transpose(
+                            turned[:, s, e * P : (e + 1) * P], tanhs[c, e, b][:, 2 * pair + s, :], ident[:]
                         )
-            interleave(nc.scalar.copy, words[:].rearrange("p b j t -> p (b j) t"), rows[:])
+                for s in range(2):
+                    t = 2 * pair + s
+                    nc.scalar.activation(
+                        h_rows[c][:, t, b * CHUNK : (b + 1) * CHUNK], turned[:, s, :],
+                        ACT.Copy, scale=sm_t[:, b, t : t + 1],
+                    )
+
+        def weave(c):
+            words = laid.tile(
+                [P, PASSES, CHUNK, PACK], BF16, name="h_words%d" % c, offset=hidden_at[c], align_bytes=64
+            )
+            interleave(nc.scalar.copy, words[:].rearrange("p b j t -> p (b j) t"), h_rows[c][:])
             h_words[c] = words
 
         def quantise(c):
-            codes = keep.tile([P, PASSES, CHUNK], U32, name="codes", tag="codes%d" % c, align_bytes=64)
+            codes = keep.tile([P, PASSES, CHUNK], U32, name="codes%d" % c, align_bytes=64)
             h_plane = keep.tile([P, PASSES, CHUNK], U8, name="h_plane%d" % c, align_bytes=64)
             nc.vector.quantize_mx(
                 codes[:].rearrange("p b j -> p (b j)").bitcast(FP8X4),
@@ -255,22 +275,24 @@ def tile_list_msg_tanh_gateP_kernel(
                     picked[t, c + i] = (got, first + i * CHUNK)
                 first = first + count * CHUNK
 
-        def messages(c):
+        def messages(c, slots):
             codes, h_plane = h_quantised[c]
-            for t in range(PACK):
-                y = psum.tile([P, CHUNK], F32, name="y", tag="turned", bufs=TURN_BANKS)
-                for e in range(EDGE_TILES):
-                    edges = slice(e * P, (e + 1) * P)
-                    for b in range(PASSES):
-                        nc.tensor.matmul_mx(
-                            y[:, edges],
-                            lhsT=wd_dealt[:, b, t, :].bitcast(FP4X4),
-                            lhsT_scale=wd_plane[:, b, t, :],
-                            rhs=codes[:, b, edges].bitcast(FP8X4),
-                            rhs_scale=h_plane[:, b, edges],
-                            start=(b == 0), stop=(b == PASSES - 1),
-                        )
-                nc.scalar.copy(msgs[:, t, c * CHUNK : (c + 1) * CHUNK], y[:])
+            for bank in range(PACK // slots):
+                y = psum.tile([P, slots, CHUNK], F32, name="y", tag="turn%d" % (PACK - PACK // slots + bank))
+                for s in range(slots):
+                    t = bank * slots + s
+                    for e in range(EDGE_TILES):
+                        edges = slice(e * P, (e + 1) * P)
+                        for b in range(PASSES):
+                            nc.tensor.matmul_mx(
+                                y[:, s, edges],
+                                lhsT=wd_dealt[:, b, t, :].bitcast(FP4X4),
+                                lhsT_scale=wd_plane[:, b, t, :],
+                                rhs=codes[:, b, edges].bitcast(FP8X4),
+                                rhs_scale=h_plane[:, b, edges],
+                                start=(b == 0), stop=(b == PASSES - 1),
+                            )
+                nc.scalar.copy(msgs[:, bank * slots : (bank + 1) * slots, c * CHUNK : (c + 1) * CHUNK], y[:])
 
         def clear_page(t, pool, **place):
             pages[t] = pool.tile([P, T], F32, name="page%d" % t, align_bytes=64, **place)
@@ -285,20 +307,22 @@ def tile_list_msg_tanh_gateP_kernel(
                 MULT,
             )
 
-        clear_page(1, keep, tag="wd_rows")
+        clear_page(0, laid, offset=page_at[0])
+        clear_page(1, laid, offset=page_at[1])
         early_gates = [(0, 0, CHUNKS), (1, 0, CHUNKS)]
         gather_gates(keep.tile([P, gate_columns(early_gates)], F32, name="picked", align_bytes=64), early_gates)
         for c in range(CHUNKS):
             sums(c)
-            hidden(c)
+            for b in range(PASSES):
+                hidden(c, b)
+            weave(c)
             quantise(c)
-            messages(c)
+            messages(c, 1 if c == LAST_CHUNK else 2)
             if c == 0:
-                clear_page(2, laid, offset=gates_end[0])
-                clear_page(LAST_PAGE, keep, tag="codes0")
-            columns = gate_columns(held_gates[c])
+                clear_page(2, laid, offset=page_at[2])
+                clear_page(LAST_PAGE, laid, offset=page_at[LAST_PAGE])
             got = laid.tile(
-                [P, columns], F32, name="picked%d" % c, offset=gates_end[c] - 4 * columns, align_bytes=64
+                [P, gate_columns(held_gates[c])], F32, name="picked%d" % c, offset=rows_at[c], align_bytes=64
             )
             gather_gates(got, held_gates[c])
             if 0 < c < LAST_CHUNK:
@@ -314,25 +338,38 @@ def tile_list_msg_tanh_gateP_kernel(
             if t < LAST_PAGE:
                 nc.scalar.copy(o_rows[:, t, :], pages[t][:])
             else:
-                nc.vector.tensor_copy(o_rows[:, t, :VECTOR_COLS], pages[t][:, :VECTOR_COLS])
+                for first, end in ((0, PIECES[0]), (PIECES[0], VECTOR_COLS)):
+                    nc.vector.tensor_copy(o_rows[:, t, first:end], pages[t][:, first:end])
                 nc.scalar.copy(o_rows[:, t, VECTOR_COLS:], pages[t][:, VECTOR_COLS:])
 
         o_plane = keep.tile([P, T], U8, name="o_plane", align_bytes=64)
         out_words = out_1[0].rearrange("p t i -> p (t i)").bitcast(I32)
-        first = 0
-        for width in PIECES:
-            o_words = keep.tile([P, width, PACK], BF16, name="o_words%d" % first, align_bytes=64)
+        firsts = [sum(PIECES[:i]) for i in range(len(PIECES))]
+        o_words = []
+
+        def weave_piece(i):
+            first, width = firsts[i], PIECES[i]
+            words = keep.tile([P, width, PACK], BF16, name="o_words%d" % i, align_bytes=64)
             split = min(max(VECTOR_COLS - first, 0), width)
             if split < width:
-                interleave(nc.scalar.copy, o_words[:, split:, :], o_rows[:, :, first + split : first + width])
+                interleave(nc.scalar.copy, words[:, split:, :], o_rows[:, :, first + split : first + width])
             if split > 0:
-                interleave(nc.vector.tensor_copy, o_words[:, :split, :], o_rows[:, :, first : first + split])
-            o_codes = keep.tile([P, width], I32, name="o_codes%d" % first, align_bytes=64)
+                interleave(nc.vector.tensor_copy, words[:, :split, :], o_rows[:, :, first : first + split])
+            o_words.append(words)
+
+        def store_piece(i):
+            first, width = firsts[i], PIECES[i]
+            o_codes = keep.tile([P, width], I32, name="o_codes%d" % i, align_bytes=64)
             nc.vector.quantize_mx(
-                o_codes[:].bitcast(FP8X4), o_plane[:, first : first + width], o_words[:].rearrange("p c t -> p (c t)")
+                o_codes[:].bitcast(FP8X4), o_plane[:, first : first + width], o_words[i][:].rearrange("p c t -> p (c t)")
             )
             nc.sync.dma_start(out_words[:, first : first + width], o_codes[:])
-            first = first + width
+
+        weave_piece(0)
+        for i in range(1, len(PIECES)):
+            weave_piece(i)
+            store_piece(i - 1)
+        store_piece(len(PIECES) - 1)
         for quad in range(4):
             (nc.sync, nc.scalar)[quad % 2].dma_start(
                 out_2[0, 4 * quad : 4 * quad + 4, :].bitcast(I32), o_plane[32 * quad : 32 * quad + 4, :].bitcast(I32)

@@ -60,62 +60,63 @@ def tile_list_msg_tanh_gateP_kernel(
         free_byte = free_byte + 2 * PAGE_BYTES
         hidden_at.extend(free_byte + (i % 2) * HIDDEN_BYTES for i in range(LAST_CHUNK))
         free_byte = free_byte + 2 * HIDDEN_BYTES
-        staged_at = rows_at[0]
-        rest_at = free_byte
-        late_at = rest_at
-        window0_at = late_at + 64 + 4 * PASSES * BANK + 2 * PASSES * BANK
-        words1_at = window0_at + PAGE_BYTES
-        edge_at = words1_at + WORD_BYTES
-        wd_plane_at = edge_at + 4 * J
-        words2_at = wd_plane_at + PASSES * N
-        page_at[0] = words2_at + 2 * PAGE_BYTES
-        page_at[1] = page_at[0] + PAGE_BYTES
-        wd_at = page_at[1] - PASSES * N
-        rest_end = page_at[1] + PAGE_BYTES
+        words_at = [free_byte, free_byte + PAGE_BYTES]
+        words_at.extend(words_at[1] + WORD_BYTES + i * PAGE_BYTES for i in range(2))
+        words_room = [3 * PAGE_BYTES + WORD_BYTES, WORD_BYTES, PAGE_BYTES, PAGE_BYTES]
 
         src_list = keep.tile([P, J // 16], U16, name="src_list")
         dst_list = keep.tile([P, J // 16], U16, name="dst_list")
         lists = (src_list, dst_list)
 
+        def load_plane(plane, plane_src, queue):
+            for quad in range(4):
+                queue.dma_start(
+                    plane[32 * quad : 32 * quad + 4].bitcast(I32),
+                    plane_src[:, 4 * quad : 4 * quad + 4, :].rearrange("a q c -> q a c").bitcast(I32),
+                )
+
         def interleave(copy, words, rows):
             copy(words.rearrange("p (c i) t -> p c t i", i=4), rows.rearrange("p t (c i) -> p c t i", i=4))
 
-        planes = keep.tile([P, PASSES, 2 * R + N], U8, name="planes", align_bytes=64)
-        nc.vector.memset(planes[:].rearrange("p a r -> p (a r)").bitcast(I32), 0)
-        ws_plane = planes[:, :, :R]
-        wt_plane = planes[:, :, R : 2 * R]
-        wd_rows = planes[:, :, 2 * R :]
-        staged = laid.tile([16, PASSES, 2 * R + N], U8, name="staged", offset=staged_at, align_bytes=64)
-        for scales, first, width in ((ws_scales, 0, R), (wt_scales, R, R), (wd_scales, 2 * R, N)):
-            nc.scalar.dma_start(
-                staged[:, :, first : first + width].bitcast(I32), scales.rearrange("a q c -> q a c").bitcast(I32)
-            )
+        ws_plane = keep.tile([P, PASSES, R], U8, name="ws_plane", align_bytes=64)
+        nc.vector.memset(ws_plane[:].rearrange("p a r -> p (a r)").bitcast(I32), 0)
+        wt_plane = keep.tile([P, PASSES, R], U8, name="wt_plane", align_bytes=64)
+        nc.vector.memset(wt_plane[:].rearrange("p a r -> p (a r)").bitcast(I32), 0)
         tab_rows = keep.tile([P, T // 4], I32, name="tab_rows", align_bytes=64)
         for first, end in ((0, SCALE_ROW), (SCALE_ROW + 16, SCALE_ROW + 32), (SCALE_ROW + 48, P)):
             nc.vector.memset(tab_rows[first:end, :], 0)
-        pages = {}
+        wd_rows = keep.tile([P, PASSES, N], U8, name="wd_rows", tag="wd_rows", align_bytes=64)
+        nc.vector.memset(wd_rows[:].rearrange("p a n -> p (a n)").bitcast(I32), 0)
+        pages = {0: keep.tile([P, T], F32, name="page0", align_bytes=64)}
+        nc.vector.memset(pages[0][:].bitcast(I32), 0)
         nc.sync.dma_start(src_list[:], offs)
+        nc.sync.dma_start(dst_list[:], offs2)
         tab_rows_src = tab_scales.rearrange("a (u x r) t -> x (a u) r t", x=2, r=4).bitcast(I32)
         for x in range(2):
             nc.sync.dma_start(tab_rows[SCALE_ROW + 32 * x : SCALE_ROW + 32 * x + 16, :], tab_rows_src[x])
-        nc.sync.dma_start(dst_list[:], offs2)
         tab_w = keep.tile([P, T], I32, name="tab_w", align_bytes=64)
         nc.sync.dma_start(tab_w[:], tab_words[0].rearrange("p t i -> p (t i)").bitcast(I32))
 
+        ws_w = [keep.tile([P, PASSES, BANK // 2], I32, name="ws_w%d" % b, align_bytes=64) for b in range(PASSES)]
+        wt_w = [keep.tile([P, PASSES, BANK], I32, name="wt_w%d" % b, align_bytes=64) for b in range(PASSES)]
         ws_src = ws_words.rearrange("a p c -> p a c").bitcast(I32)
         wt_src = wt_words.rearrange("a p r i -> p a (r i)").bitcast(I32)
-        wt_w = [keep.tile([P, PASSES, BANK], I32, name="wt_w0", align_bytes=64)]
-        nc.sync.dma_start(wt_w[0][:], wt_src[:, :, :BANK])
-        ws_w = [keep.tile([P, PASSES, BANK // 2], I32, name="ws_w0", align_bytes=64)]
         nc.sync.dma_start(ws_w[0][:], ws_src[:, :, : BANK // 2])
-        for quad in range(4):
-            nc.scalar.dma_start(
-                planes[32 * quad : 32 * quad + 4].rearrange("p a r -> p (a r)").bitcast(I32),
-                staged[4 * quad : 4 * quad + 4].rearrange("p a r -> p (a r)").bitcast(I32),
-            )
+        load_plane(ws_plane, ws_scales, nc.sync)
+        load_plane(wt_plane, wt_scales, nc.scalar)
+        nc.sync.dma_start(wt_w[0][:], wt_src[:, :, :BANK])
+        nc.sync.dma_start(wt_w[1][:], wt_src[:, :, BANK:])
+        nc.sync.dma_start(ws_w[1][:], ws_src[:, :, BANK // 2 :])
 
         ident = keep.tile([P, P], F32, name="ident")
         make_identity(nc, ident[:])
+        sm_t = keep.tile([P, PASSES, PACK], F32, name="sm_t")
+        nc.sync.dma_start(sm_t[:], sm.rearrange("(b p t) -> p b t", b=PASSES, t=PACK))
+        wd_w = keep.tile([P, PASSES, 2 * N], U8, name="wd_w", align_bytes=64)
+        nc.sync.dma_start(wd_w[:].bitcast(I32), wd_words.rearrange("a p c -> p a c").bitcast(I32))
+        load_plane(wd_rows, wd_scales, nc.sync)
+        edge_weight = keep.tile([P, J], F32, name="edge_weight", align_bytes=64)
+        nc.sync.dma_start(edge_weight[:], wgo)
 
         v_plane = {}
         v_words = []
@@ -136,19 +137,18 @@ def tile_list_msg_tanh_gateP_kernel(
             for i in range(count):
                 v_plane[c + i] = (plane, i * CHUNK)
 
-        def gather_words(c, count, room_at, room_end):
-            room = laid.tile([P, (room_end - room_at) // 4], U32, name="both%d" % c, offset=room_at, align_bytes=64)
-            both = room[:, : 2 * count * CHUNK].rearrange("p (l j) -> p l j", l=2)
+        def gather_words(c):
+            room = laid.tile([P, words_room[c] // 4], U32, name="both%d" % c, offset=words_at[c], align_bytes=64)
+            both = room[:, : 2 * CHUNK].rearrange("p (l j) -> p l j", l=2)
             for l in range(2):
-                offsets = lists[l][:, c * LIST_COLS : (c + count) * LIST_COLS]
+                offsets = lists[l][:, c * LIST_COLS : (c + 1) * LIST_COLS]
                 nc.vector.tensor_copy(both[:, l, :], tab_w[:].bitcast(U32).indirect(offsets))
-            parted = keep.tile([P, 2, PASSES, count * 2 * CHUNK], U8, name="parted%d" % c, align_bytes=64)
+            parted = keep.tile([P, 2, PASSES, 2 * CHUNK], U8, name="parted%d" % c, align_bytes=64)
             nc.vector.tensor_copy(
                 parted[:].bitcast(U16),
                 both.bitcast(U16).rearrange("p l (j a) -> p l a j", a=PASSES),
             )
-            for i in range(count):
-                v_words.append(parted[:, :, :, i * 2 * CHUNK : (i + 1) * 2 * CHUNK])
+            v_words.append(parted)
 
         gT_rows = gT.rearrange("(p t) c -> p t c", t=PACK)
         gate_windows = []
@@ -159,32 +159,19 @@ def tile_list_msg_tanh_gateP_kernel(
             nc.sync.dma_start(gate_windows[t][:], gT_rows[:, t, :])
 
         gather_scales(0, 2, nc.scalar, keep, tag="got0")
-        gather_words(0, 1, rest_at, rest_end)
-        wt_w.append(laid.tile([P, PASSES, BANK], I32, name="wt_w1", offset=late_at + 64, align_bytes=64))
-        nc.sync.dma_start(wt_w[1][:], wt_src[:, :, BANK:])
-        ws_w.append(
-            laid.tile([P, PASSES, BANK // 2], I32, name="ws_w1", offset=late_at + 64 + 4 * PASSES * BANK, align_bytes=64)
-        )
-        nc.sync.dma_start(ws_w[1][:], ws_src[:, :, BANK // 2 :])
-        sm_t = laid.tile([P, PASSES, PACK], F32, name="sm_t", offset=late_at, align_bytes=64)
-        nc.sync.dma_start(sm_t[:], sm.rearrange("(b p t) -> p b t", b=PASSES, t=PACK))
-
-        wd_w = laid.tile([P, PASSES, 2 * N], U8, name="wd_w", offset=wd_at, align_bytes=64)
-        nc.sync.dma_start(wd_w[:].bitcast(I32), wd_words.rearrange("a p c -> p a c").bitcast(I32))
-        edge_weight = laid.tile([P, J], F32, name="edge_weight", offset=edge_at, align_bytes=64)
-        nc.sync.dma_start(edge_weight[:], wgo)
-        load_gates(laid, offset=window0_at)
+        gather_words(0)
+        load_gates(laid, offset=words_at[0])
         load_gates(keep, tag="got0")
-        gather_words(1, 1, words1_at, edge_at)
-        gather_scales(2, 2, nc.sync, laid, offset=words1_at)
-        gather_words(2, 2, words2_at, wd_at)
-        for i in range(2):
-            load_gates(laid, offset=words2_at + i * PAGE_BYTES)
+        gather_words(1)
+        gather_scales(2, 2, nc.sync, laid, offset=words_at[1])
+        for c in (2, 3):
+            gather_words(c)
+            load_gates(laid, offset=words_at[c])
 
         wd_dealt = keep.tile([P, PASSES, PACK, 2 * P], U8, name="wd_dealt", align_bytes=64)
         nc.vector.tensor_copy(wd_dealt[:].bitcast(U16), wd_w[:].bitcast(U16).rearrange("p a (m t) -> p a t m", t=PACK))
-        wd_plane = laid.tile([P, PASSES, PACK, P], U8, name="wd_plane", offset=wd_plane_at, align_bytes=64)
-        nc.vector.tensor_copy(wd_plane[:], wd_rows.rearrange("p a (m t) -> p a t m", t=PACK))
+        wd_plane = keep.tile([P, PASSES, PACK, P], U8, name="wd_plane", align_bytes=64)
+        nc.vector.tensor_copy(wd_plane[:], wd_rows[:].rearrange("p a (m t) -> p a t m", t=PACK))
 
         tanhs = {}
         h_rows = {}
@@ -307,8 +294,7 @@ def tile_list_msg_tanh_gateP_kernel(
                 MULT,
             )
 
-        clear_page(0, laid, offset=page_at[0])
-        clear_page(1, laid, offset=page_at[1])
+        clear_page(1, keep, tag="wd_rows")
         early_gates = [(0, 0, CHUNKS), (1, 0, CHUNKS)]
         gather_gates(keep.tile([P, gate_columns(early_gates)], F32, name="picked", align_bytes=64), early_gates)
         for c in range(CHUNKS):

@@ -85,10 +85,9 @@ def tile_list_msg_tanh_gateP_kernel(
         tab_rows = keep.tile([P, T // 4], I32, name="tab_rows", align_bytes=64)
         for first, end in ((0, SCALE_ROW), (SCALE_ROW + 16, SCALE_ROW + 32), (SCALE_ROW + 48, P)):
             nc.vector.memset(tab_rows[first:end, :], 0)
-        wd_rows = keep.tile([P, PASSES, N], U8, name="wd_rows", tag="wd_rows", align_bytes=64)
+        wd_rows = keep.tile([P, PASSES, N], U8, name="wd_rows", align_bytes=64)
         nc.vector.memset(wd_rows[:].rearrange("p a n -> p (a n)").bitcast(I32), 0)
-        pages = {0: keep.tile([P, T], F32, name="page0", align_bytes=64)}
-        nc.vector.memset(pages[0][:].bitcast(I32), 0)
+        pages = {}
         nc.sync.dma_start(src_list[:], offs)
         nc.sync.dma_start(dst_list[:], offs2)
         tab_rows_src = tab_scales.rearrange("a (u x r) t -> x (a u) r t", x=2, r=4).bitcast(I32)
@@ -97,16 +96,16 @@ def tile_list_msg_tanh_gateP_kernel(
         tab_w = keep.tile([P, T], I32, name="tab_w", align_bytes=64)
         nc.sync.dma_start(tab_w[:], tab_words[0].rearrange("p t i -> p (t i)").bitcast(I32))
 
-        ws_w = [keep.tile([P, PASSES, BANK // 2], I32, name="ws_w%d" % b, align_bytes=64) for b in range(PASSES)]
+        ws_all = keep.tile([P, PASSES, BANK], I32, name="ws_all", align_bytes=64)
+        ws_w = [ws_all[:, :, b * BANK // 2 : (b + 1) * BANK // 2] for b in range(PASSES)]
         wt_w = [keep.tile([P, PASSES, BANK], I32, name="wt_w%d" % b, align_bytes=64) for b in range(PASSES)]
         ws_src = ws_words.rearrange("a p c -> p a c").bitcast(I32)
         wt_src = wt_words.rearrange("a p r i -> p a (r i)").bitcast(I32)
-        nc.sync.dma_start(ws_w[0][:], ws_src[:, :, : BANK // 2])
+        nc.sync.dma_start(ws_all[:], ws_src)
         load_plane(ws_plane, ws_scales, nc.sync)
         load_plane(wt_plane, wt_scales, nc.scalar)
         nc.sync.dma_start(wt_w[0][:], wt_src[:, :, :BANK])
         nc.sync.dma_start(wt_w[1][:], wt_src[:, :, BANK:])
-        nc.sync.dma_start(ws_w[1][:], ws_src[:, :, BANK // 2 :])
 
         ident = keep.tile([P, P], F32, name="ident")
         make_identity(nc, ident[:])
@@ -116,7 +115,19 @@ def tile_list_msg_tanh_gateP_kernel(
         nc.sync.dma_start(wd_w[:].bitcast(I32), wd_words.rearrange("a p c -> p a c").bitcast(I32))
         load_plane(wd_rows, wd_scales, nc.sync)
         edge_weight = keep.tile([P, J], F32, name="edge_weight", align_bytes=64)
-        nc.sync.dma_start(edge_weight[:], wgo)
+        weight_rows = keep.tile([P, J // P], F32, name="weight_rows")
+        nc.gpsimd.dma_start(weight_rows[:], wgo[0].rearrange("(p i) -> p i", p=P))
+        for half in range(2):
+            spread = psum.tile([P, PACK, P], F32, name="spread", tag="turn%d" % half)
+            for i in range(PACK):
+                column = half * PACK + i
+                nc.tensor.transpose(
+                    spread[:, i, :], weight_rows[:, column : column + 1].to_broadcast([P, P]), ident[:]
+                )
+            nc.scalar.copy(
+                edge_weight[:].rearrange("m (p i) -> m p i", p=P)[:, :, half * PACK : (half + 1) * PACK],
+                spread[:].rearrange("m i p -> m p i"),
+            )
 
         v_plane = {}
         v_words = []
@@ -294,9 +305,10 @@ def tile_list_msg_tanh_gateP_kernel(
                 MULT,
             )
 
-        clear_page(1, keep, tag="wd_rows")
         early_gates = [(0, 0, CHUNKS), (1, 0, CHUNKS)]
         gather_gates(keep.tile([P, gate_columns(early_gates)], F32, name="picked", align_bytes=64), early_gates)
+        clear_page(0, laid, offset=words_at[0])
+        clear_page(1, keep, tag="got0")
         for c in range(CHUNKS):
             sums(c)
             for b in range(PASSES):

@@ -31,10 +31,10 @@ LAST_CHUNK = CHUNKS - 1
 PIECES = (512, 512, 512, 256, 256)
 VECTOR_COLS = 1152
 PAGE_BYTES = 4 * T
-GATE_BYTES = 4 * CHUNK
 WORD_BYTES = 2 * 4 * CHUNK
 HIDDEN_BYTES = 2 * PASSES * CHUNK * PACK
 SUM_BANKS = 4
+EARLY_PAGES = 2
 
 
 def tile_list_msg_tanh_gateP_kernel(
@@ -48,15 +48,14 @@ def tile_list_msg_tanh_gateP_kernel(
         laid = ctx.enter_context(tc.tile_pool(name="laid", bufs=1))
         psum = ctx.enter_context(tc.psum_pool(name="psum", bufs=1))
 
-        held_gates = [[(2, 0, 3)], [(3, 0, 1)], [(3, 1, 1)], [(3, 2, 2), (2, 3, 1)]]
+        held_gates = [[(2, 0, 1)]]
+        for c in range(1, CHUNKS):
+            held_gates.append([(LAST_PAGE, c - 1, 2 if c == LAST_CHUNK else 1), (2, c, 1)])
 
-        rows_at = []
-        free_byte = 0
-        for c in range(CHUNKS):
-            rows_at.append(free_byte)
-            free_byte = free_byte + max(HIDDEN_BYTES, GATE_BYTES * sum(count for t, first, count in held_gates[c]))
-        page_at = {2: free_byte, 3: free_byte + PAGE_BYTES}
-        hidden_at = [page_at[3] - HIDDEN_BYTES // 2]
+        rows_at = [c * HIDDEN_BYTES for c in range(CHUNKS)]
+        free_byte = CHUNKS * HIDDEN_BYTES
+        page_at = {1: free_byte, 2: free_byte + PAGE_BYTES}
+        hidden_at = [page_at[2] - HIDDEN_BYTES // 2]
         free_byte = free_byte + 2 * PAGE_BYTES
         hidden_at.extend(free_byte + (i % 2) * HIDDEN_BYTES for i in range(LAST_CHUNK))
         free_byte = free_byte + 2 * HIDDEN_BYTES
@@ -85,9 +84,8 @@ def tile_list_msg_tanh_gateP_kernel(
         tab_rows = keep.tile([P, T // 4], I32, name="tab_rows", align_bytes=64)
         for first, end in ((0, SCALE_ROW), (SCALE_ROW + 16, SCALE_ROW + 32), (SCALE_ROW + 48, P)):
             nc.vector.memset(tab_rows[first:end, :], 0)
-        wd_rows = keep.tile([P, PASSES, N], U8, name="wd_rows", align_bytes=64)
+        wd_rows = keep.tile([P, PASSES, N], U8, name="wd_rows", tag="wd_rows", align_bytes=64)
         nc.vector.memset(wd_rows[:].rearrange("p a n -> p (a n)").bitcast(I32), 0)
-        pages = {}
         nc.sync.dma_start(src_list[:], offs)
         nc.sync.dma_start(dst_list[:], offs2)
         tab_rows_src = tab_scales.rearrange("a (u x r) t -> x (a u) r t", x=2, r=4).bitcast(I32)
@@ -99,9 +97,8 @@ def tile_list_msg_tanh_gateP_kernel(
         ws_all = keep.tile([P, PASSES, BANK], I32, name="ws_all", align_bytes=64)
         ws_w = [ws_all[:, :, b * BANK // 2 : (b + 1) * BANK // 2] for b in range(PASSES)]
         wt_w = [keep.tile([P, PASSES, BANK], I32, name="wt_w%d" % b, align_bytes=64) for b in range(PASSES)]
-        ws_src = ws_words.rearrange("a p c -> p a c").bitcast(I32)
         wt_src = wt_words.rearrange("a p r i -> p a (r i)").bitcast(I32)
-        nc.sync.dma_start(ws_all[:], ws_src)
+        nc.sync.dma_start(ws_all[:], ws_words.rearrange("a p c -> p a c").bitcast(I32))
         load_plane(ws_plane, ws_scales, nc.sync)
         load_plane(wt_plane, wt_scales, nc.scalar)
         nc.sync.dma_start(wt_w[0][:], wt_src[:, :, :BANK])
@@ -189,6 +186,7 @@ def tile_list_msg_tanh_gateP_kernel(
         h_words = {}
         h_quantised = {}
         picked = {}
+        pages = {}
         msgs = keep.tile([P, PACK, J], F32, name="msgs", align_bytes=64)
 
         def sums(c):
@@ -247,7 +245,7 @@ def tile_list_msg_tanh_gateP_kernel(
             h_words[c] = words
 
         def quantise(c):
-            codes = keep.tile([P, PASSES, CHUNK], U32, name="codes%d" % c, align_bytes=64)
+            codes = keep.tile([P, PASSES, CHUNK], U32, name="codes", tag="codes%d" % c, align_bytes=64)
             h_plane = keep.tile([P, PASSES, CHUNK], U8, name="h_plane%d" % c, align_bytes=64)
             nc.vector.quantize_mx(
                 codes[:].rearrange("p b j -> p (b j)").bitcast(FP8X4),
@@ -305,10 +303,9 @@ def tile_list_msg_tanh_gateP_kernel(
                 MULT,
             )
 
-        early_gates = [(0, 0, CHUNKS), (1, 0, CHUNKS)]
+        clear_page(0, keep, tag="wd_rows")
+        early_gates = [(t, 0, CHUNKS) for t in range(EARLY_PAGES)]
         gather_gates(keep.tile([P, gate_columns(early_gates)], F32, name="picked", align_bytes=64), early_gates)
-        clear_page(0, laid, offset=words_at[0])
-        clear_page(1, keep, tag="got0")
         for c in range(CHUNKS):
             sums(c)
             for b in range(PASSES):
@@ -317,8 +314,9 @@ def tile_list_msg_tanh_gateP_kernel(
             quantise(c)
             messages(c, 1 if c == LAST_CHUNK else 2)
             if c == 0:
+                clear_page(1, laid, offset=page_at[1])
                 clear_page(2, laid, offset=page_at[2])
-                clear_page(LAST_PAGE, laid, offset=page_at[LAST_PAGE])
+                clear_page(LAST_PAGE, keep, tag="codes0")
             got = laid.tile(
                 [P, gate_columns(held_gates[c])], F32, name="picked%d" % c, offset=rows_at[c], align_bytes=64
             )

@@ -34,6 +34,7 @@ PAGE_BYTES = 4 * T
 WORD_BYTES = 2 * 4 * CHUNK
 HIDDEN_BYTES = 2 * PASSES * CHUNK * PACK
 SUM_BANKS = 4
+WARM_UPS = 4
 EARLY_PAGES = 2
 
 
@@ -48,12 +49,10 @@ def tile_list_msg_tanh_gateP_kernel(
         laid = ctx.enter_context(tc.tile_pool(name="laid", bufs=1))
         psum = ctx.enter_context(tc.psum_pool(name="psum", bufs=1))
 
-        held_gates = [[(2, 0, 1)]]
-        for c in range(1, CHUNKS):
-            held_gates.append([(LAST_PAGE, c - 1, 2 if c == LAST_CHUNK else 1), (2, c, 1)])
+        held_gates = [[(1, 0, 4), (2, 0, 1)], [(3, 0, 1), (2, 1, 1)], [(3, 1, 1), (2, 2, 1)], [(3, 2, 2), (2, 3, 1)]]
 
-        rows_at = [c * HIDDEN_BYTES for c in range(CHUNKS)]
-        free_byte = CHUNKS * HIDDEN_BYTES
+        rows_at = [c * 5120 for c in range(CHUNKS)]
+        free_byte = CHUNKS * 5120
         page_at = {1: free_byte, 2: free_byte + PAGE_BYTES}
         hidden_at = [page_at[2] - HIDDEN_BYTES // 2]
         free_byte = free_byte + 2 * PAGE_BYTES
@@ -61,7 +60,9 @@ def tile_list_msg_tanh_gateP_kernel(
         free_byte = free_byte + 2 * HIDDEN_BYTES
         words_at = [free_byte, free_byte + PAGE_BYTES]
         words_at.extend(words_at[1] + WORD_BYTES + i * PAGE_BYTES for i in range(2))
-        words_room = [3 * PAGE_BYTES + WORD_BYTES, WORD_BYTES, PAGE_BYTES, PAGE_BYTES]
+        page_at[0] = words_at[3] + PAGE_BYTES
+        wd_at = page_at[0] + PAGE_BYTES
+        words_room = [4 * PAGE_BYTES + WORD_BYTES + 4096, WORD_BYTES, PAGE_BYTES, 2 * PAGE_BYTES]
 
         src_list = keep.tile([P, J // 16], U16, name="src_list")
         dst_list = keep.tile([P, J // 16], U16, name="dst_list")
@@ -84,8 +85,6 @@ def tile_list_msg_tanh_gateP_kernel(
         tab_rows = keep.tile([P, T // 4], I32, name="tab_rows", align_bytes=64)
         for first, end in ((0, SCALE_ROW), (SCALE_ROW + 16, SCALE_ROW + 32), (SCALE_ROW + 48, P)):
             nc.vector.memset(tab_rows[first:end, :], 0)
-        wd_rows = keep.tile([P, PASSES, N], U8, name="wd_rows", tag="wd_rows", align_bytes=64)
-        nc.vector.memset(wd_rows[:].rearrange("p a n -> p (a n)").bitcast(I32), 0)
         nc.sync.dma_start(src_list[:], offs)
         nc.sync.dma_start(dst_list[:], offs2)
         tab_rows_src = tab_scales.rearrange("a (u x r) t -> x (a u) r t", x=2, r=4).bitcast(I32)
@@ -106,11 +105,6 @@ def tile_list_msg_tanh_gateP_kernel(
 
         ident = keep.tile([P, P], F32, name="ident")
         make_identity(nc, ident[:])
-        sm_t = keep.tile([P, PASSES, PACK], F32, name="sm_t")
-        nc.sync.dma_start(sm_t[:], sm.rearrange("(b p t) -> p b t", b=PASSES, t=PACK))
-        wd_w = keep.tile([P, PASSES, 2 * N], U8, name="wd_w", align_bytes=64)
-        nc.sync.dma_start(wd_w[:].bitcast(I32), wd_words.rearrange("a p c -> p a c").bitcast(I32))
-        load_plane(wd_rows, wd_scales, nc.sync)
         edge_weight = keep.tile([P, J], F32, name="edge_weight", align_bytes=64)
         weight_rows = keep.tile([P, J // P], F32, name="weight_rows")
         nc.gpsimd.dma_start(weight_rows[:], wgo[0].rearrange("(p i) -> p i", p=P))
@@ -124,6 +118,17 @@ def tile_list_msg_tanh_gateP_kernel(
             nc.scalar.copy(
                 edge_weight[:].rearrange("m (p i) -> m p i", p=P)[:, :, half * PACK : (half + 1) * PACK],
                 spread[:].rearrange("m i p -> m p i"),
+            )
+
+        idle = psum.tile([P, BANK], F32, name="idle", tag="turn3")
+        for i in range(WARM_UPS):
+            nc.tensor.matmul_mx(
+                idle[:],
+                lhsT=ws_w[0][:, 0, : P // 2].bitcast(FP4X4),
+                lhsT_scale=tab_rows[:].bitcast(U8)[:, :P],
+                rhs=ws_w[0][:, 0, :].bitcast(FP4X4),
+                rhs_scale=tab_rows[:].bitcast(U8)[:, :BANK],
+                start=True, stop=True,
             )
 
         v_plane = {}
@@ -147,15 +152,16 @@ def tile_list_msg_tanh_gateP_kernel(
 
         def gather_words(c):
             room = laid.tile([P, words_room[c] // 4], U32, name="both%d" % c, offset=words_at[c], align_bytes=64)
-            both = room[:, : 2 * CHUNK].rearrange("p (l j) -> p l j", l=2)
+            second = keep.tile([P, CHUNK], U32, name="second%d" % c, align_bytes=64)
+            both = (room[:, :CHUNK], second[:])
+            parted = keep.tile([P, 2, PASSES, 2 * CHUNK], U8, name="parted%d" % c, align_bytes=64)
             for l in range(2):
                 offsets = lists[l][:, c * LIST_COLS : (c + 1) * LIST_COLS]
-                nc.vector.tensor_copy(both[:, l, :], tab_w[:].bitcast(U32).indirect(offsets))
-            parted = keep.tile([P, 2, PASSES, 2 * CHUNK], U8, name="parted%d" % c, align_bytes=64)
-            nc.vector.tensor_copy(
-                parted[:].bitcast(U16),
-                both.bitcast(U16).rearrange("p l (j a) -> p l a j", a=PASSES),
-            )
+                nc.vector.tensor_copy(both[l], tab_w[:].bitcast(U32).indirect(offsets))
+            for l in range(2):
+                nc.vector.tensor_copy(
+                    parted[:, l].bitcast(U16), both[l].bitcast(U16).rearrange("p (j a) -> p a j", a=PASSES)
+                )
             v_words.append(parted)
 
         gT_rows = gT.rearrange("(p t) c -> p t c", t=PACK)
@@ -168,7 +174,14 @@ def tile_list_msg_tanh_gateP_kernel(
 
         gather_scales(0, 2, nc.scalar, keep, tag="got0")
         gather_words(0)
+        sm_t = laid.tile([P, PASSES, PACK], F32, name="sm_t", offset=wd_at + 3072)
+        nc.sync.dma_start(sm_t[:], sm.rearrange("(b p t) -> p b t", b=PASSES, t=PACK))
         load_gates(laid, offset=words_at[0])
+        wd_w = laid.tile([P, PASSES, 2 * N], U8, name="wd_w", offset=wd_at, align_bytes=64)
+        nc.sync.dma_start(wd_w[:].bitcast(I32), wd_words.rearrange("a p c -> p a c").bitcast(I32))
+        wd_rows = laid.tile([P, PASSES, N], U8, name="wd_rows", offset=wd_at + 2048, align_bytes=64)
+        nc.gpsimd.memset(wd_rows[:].rearrange("p a n -> p (a n)").bitcast(I32), 0)
+        load_plane(wd_rows, wd_scales, nc.sync)
         load_gates(keep, tag="got0")
         gather_words(1)
         gather_scales(2, 2, nc.sync, laid, offset=words_at[1])
@@ -303,8 +316,8 @@ def tile_list_msg_tanh_gateP_kernel(
                 MULT,
             )
 
-        clear_page(0, keep, tag="wd_rows")
-        early_gates = [(t, 0, CHUNKS) for t in range(EARLY_PAGES)]
+        clear_page(0, laid, offset=page_at[0])
+        early_gates = [(0, 0, CHUNKS)]
         gather_gates(keep.tile([P, gate_columns(early_gates)], F32, name="picked", align_bytes=64), early_gates)
         for c in range(CHUNKS):
             sums(c)
@@ -338,7 +351,7 @@ def tile_list_msg_tanh_gateP_kernel(
                     nc.vector.tensor_copy(o_rows[:, t, first:end], pages[t][:, first:end])
                 nc.scalar.copy(o_rows[:, t, VECTOR_COLS:], pages[t][:, VECTOR_COLS:])
 
-        o_plane = keep.tile([P, T], U8, name="o_plane", align_bytes=64)
+        o_plane = keep.tile([P, BANK], U8, name="o_plane", align_bytes=64)
         out_words = out_1[0].rearrange("p t i -> p (t i)").bitcast(I32)
         firsts = [sum(PIECES[:i]) for i in range(len(PIECES))]
         o_words = []
@@ -357,7 +370,7 @@ def tile_list_msg_tanh_gateP_kernel(
             first, width = firsts[i], PIECES[i]
             o_codes = keep.tile([P, width], I32, name="o_codes%d" % i, align_bytes=64)
             nc.vector.quantize_mx(
-                o_codes[:].bitcast(FP8X4), o_plane[:, first : first + width], o_words[i][:].rearrange("p c t -> p (c t)")
+                o_codes[:].bitcast(FP8X4), o_plane[4 * (first // BANK) :, first % BANK : first % BANK + width], o_words[i][:].rearrange("p c t -> p (c t)")
             )
             nc.sync.dma_start(out_words[:, first : first + width], o_codes[:])
 
@@ -366,7 +379,8 @@ def tile_list_msg_tanh_gateP_kernel(
             weave_piece(i)
             store_piece(i - 1)
         store_piece(len(PIECES) - 1)
+        out_scales = out_2[0].rearrange("(q r) (k j) -> q k r j", r=4, k=4).bitcast(I32)
         for quad in range(4):
             (nc.sync, nc.scalar)[quad % 2].dma_start(
-                out_2[0, 4 * quad : 4 * quad + 4, :].bitcast(I32), o_plane[32 * quad : 32 * quad + 4, :].bitcast(I32)
+                out_scales[quad], o_plane[32 * quad : 32 * quad + 16, :].bitcast(I32)
             )

@@ -34,7 +34,6 @@ PAGE_BYTES = 4 * T
 WORD_BYTES = 2 * 4 * CHUNK
 HIDDEN_BYTES = 2 * PASSES * CHUNK * PACK
 SUM_BANKS = 4
-WARM_UPS = 4
 EARLY_PAGES = 2
 
 
@@ -118,17 +117,6 @@ def tile_list_msg_tanh_gateP_kernel(
             nc.scalar.copy(
                 edge_weight[:].rearrange("m (p i) -> m p i", p=P)[:, :, half * PACK : (half + 1) * PACK],
                 spread[:].rearrange("m i p -> m p i"),
-            )
-
-        idle = psum.tile([P, BANK], F32, name="idle", tag="turn3")
-        for i in range(WARM_UPS):
-            nc.tensor.matmul_mx(
-                idle[:],
-                lhsT=ws_w[0][:, 0, : P // 2].bitcast(FP4X4),
-                lhsT_scale=tab_rows[:].bitcast(U8)[:, :P],
-                rhs=ws_w[0][:, 0, :].bitcast(FP4X4),
-                rhs_scale=tab_rows[:].bitcast(U8)[:, :BANK],
-                start=True, stop=True,
             )
 
         v_plane = {}

@@ -33,8 +33,6 @@ VECTOR_COLS = 1152
 PAGE_BYTES = 4 * T
 WORD_BYTES = 2 * 4 * CHUNK
 HIDDEN_BYTES = 2 * PASSES * CHUNK * PACK
-SUM_BANKS = 4
-EARLY_PAGES = 2
 
 
 def tile_list_msg_tanh_gateP_kernel(
@@ -48,7 +46,7 @@ def tile_list_msg_tanh_gateP_kernel(
         laid = ctx.enter_context(tc.tile_pool(name="laid", bufs=1))
         psum = ctx.enter_context(tc.psum_pool(name="psum", bufs=1))
 
-        held_gates = [[(1, 0, 4), (2, 0, 1)], [(3, 0, 1), (2, 1, 1)], [(3, 1, 1), (2, 2, 1)], [(3, 2, 2), (2, 3, 1)]]
+        held_gates = [[(2, 0, 3)], [(3, 0, 1)], [(3, 1, 1)], [(3, 2, 2), (2, 3, 1)]]
 
         rows_at = [c * 5120 for c in range(CHUNKS)]
         free_byte = CHUNKS * 5120
@@ -165,12 +163,12 @@ def tile_list_msg_tanh_gateP_kernel(
         sm_t = laid.tile([P, PASSES, PACK], F32, name="sm_t", offset=wd_at + 3072)
         nc.sync.dma_start(sm_t[:], sm.rearrange("(b p t) -> p b t", b=PASSES, t=PACK))
         load_gates(laid, offset=words_at[0])
+        load_gates(keep, tag="got0")
         wd_w = laid.tile([P, PASSES, 2 * N], U8, name="wd_w", offset=wd_at, align_bytes=64)
         nc.sync.dma_start(wd_w[:].bitcast(I32), wd_words.rearrange("a p c -> p a c").bitcast(I32))
         wd_rows = laid.tile([P, PASSES, N], U8, name="wd_rows", offset=wd_at + 2048, align_bytes=64)
         nc.gpsimd.memset(wd_rows[:].rearrange("p a n -> p (a n)").bitcast(I32), 0)
         load_plane(wd_rows, wd_scales, nc.sync)
-        load_gates(keep, tag="got0")
         gather_words(1)
         gather_scales(2, 2, nc.sync, laid, offset=words_at[1])
         for c in (2, 3):
@@ -190,34 +188,33 @@ def tile_list_msg_tanh_gateP_kernel(
         pages = {}
         msgs = keep.tile([P, PACK, J], F32, name="msgs", align_bytes=64)
 
-        def sums(c):
+        def sums(c, b):
             plane, plane_first = v_plane[c]
-            for b in range(PASSES):
-                for e in range(EDGE_TILES):
-                    tanh = ring.tile([P, PACK, P], F32, name="tanh", bufs=2 * PASSES * EDGE_TILES)
-                    edge_scales = slice(plane_first + e * P, plane_first + (e + 1) * P)
-                    edge_bytes = slice(2 * e * P, 2 * (e + 1) * P)
-                    acc = psum.tile([P, BANK], F32, name="acc", bufs=SUM_BANKS)
-                    r_cols = slice(b * BANK, (b + 1) * BANK)
-                    for a in range(PASSES):
-                        nc.tensor.matmul_mx(
-                            acc[:],
-                            lhsT=v_words[c][:, 0, a, edge_bytes].bitcast(FP4X4),
-                            lhsT_scale=plane[:, a, 0, edge_scales],
-                            rhs=ws_w[b][:, a, :].bitcast(FP4X4),
-                            rhs_scale=ws_plane[:, a, r_cols],
-                            start=(a == 0), stop=False,
-                        )
-                        nc.tensor.matmul_mx(
-                            acc[:],
-                            lhsT=v_words[c][:, 1, a, edge_bytes].bitcast(FP4X4),
-                            lhsT_scale=plane[:, a, 1, edge_scales],
-                            rhs=wt_w[b][:, a, :].bitcast(FP8X4),
-                            rhs_scale=wt_plane[:, a, r_cols],
-                            start=False, stop=(a == PASSES - 1),
-                        )
-                    nc.scalar.activation(tanh[:], acc[:].rearrange("p (m t) -> p t m", t=PACK), ACT.Tanh)
-                    tanhs[c, e, b] = tanh
+            for e in range(EDGE_TILES):
+                tanh = ring.tile([P, PACK, P], F32, name="tanh", bufs=2 * PASSES * EDGE_TILES)
+                edge_scales = slice(plane_first + e * P, plane_first + (e + 1) * P)
+                edge_bytes = slice(2 * e * P, 2 * (e + 1) * P)
+                acc = psum.tile([P, BANK], F32, name="acc", tag="sum%d" % (EDGE_TILES * b + e))
+                r_cols = slice(b * BANK, (b + 1) * BANK)
+                for a in range(PASSES):
+                    nc.tensor.matmul_mx(
+                        acc[:],
+                        lhsT=v_words[c][:, 0, a, edge_bytes].bitcast(FP4X4),
+                        lhsT_scale=plane[:, a, 0, edge_scales],
+                        rhs=ws_w[b][:, a, :].bitcast(FP4X4),
+                        rhs_scale=ws_plane[:, a, r_cols],
+                        start=(a == 0), stop=False,
+                    )
+                    nc.tensor.matmul_mx(
+                        acc[:],
+                        lhsT=v_words[c][:, 1, a, edge_bytes].bitcast(FP4X4),
+                        lhsT_scale=plane[:, a, 1, edge_scales],
+                        rhs=wt_w[b][:, a, :].bitcast(FP8X4),
+                        rhs_scale=wt_plane[:, a, r_cols],
+                        start=False, stop=(a == PASSES - 1),
+                    )
+                nc.scalar.activation(tanh[:], acc[:].rearrange("p (m t) -> p t m", t=PACK), ACT.Tanh)
+                tanhs[c, e, b] = tanh
 
         def hidden(c, b):
             if b == 0:
@@ -238,15 +235,16 @@ def tile_list_msg_tanh_gateP_kernel(
                         ACT.Copy, scale=sm_t[:, b, t : t + 1],
                     )
 
-        def weave(c):
-            words = laid.tile(
-                [P, PASSES, CHUNK, PACK], BF16, name="h_words%d" % c, offset=hidden_at[c], align_bytes=64
-            )
-            interleave(nc.scalar.copy, words[:].rearrange("p b j t -> p (b j) t"), h_rows[c][:])
-            h_words[c] = words
+        def weave(c, b):
+            if b == 0:
+                h_words[c] = laid.tile(
+                    [P, PASSES, CHUNK, PACK], BF16, name="h_words%d" % c, offset=hidden_at[c], align_bytes=64
+                )
+            interleave(nc.scalar.copy, h_words[c][:, b], h_rows[c][:, :, b * CHUNK : (b + 1) * CHUNK])
 
         def quantise(c):
-            codes = keep.tile([P, PASSES, CHUNK], U32, name="codes", tag="codes%d" % c, align_bytes=64)
+            tag = "got0" if c == 0 else "codes%d" % c
+            codes = keep.tile([P, PASSES, CHUNK], U32, name="codes", tag=tag, align_bytes=64)
             h_plane = keep.tile([P, PASSES, CHUNK], U8, name="h_plane%d" % c, align_bytes=64)
             nc.vector.quantize_mx(
                 codes[:].rearrange("p b j -> p (b j)").bitcast(FP8X4),
@@ -275,20 +273,18 @@ def tile_list_msg_tanh_gateP_kernel(
         def messages(c, slots):
             codes, h_plane = h_quantised[c]
             for bank in range(PACK // slots):
-                y = psum.tile([P, slots, CHUNK], F32, name="y", tag="turn%d" % (PACK - PACK // slots + bank))
+                y = psum.tile([P, slots, CHUNK], F32, name="y", tag="sum%d" % (PACK - PACK // slots + bank))
                 for s in range(slots):
                     t = bank * slots + s
-                    for e in range(EDGE_TILES):
-                        edges = slice(e * P, (e + 1) * P)
-                        for b in range(PASSES):
-                            nc.tensor.matmul_mx(
-                                y[:, s, edges],
-                                lhsT=wd_dealt[:, b, t, :].bitcast(FP4X4),
-                                lhsT_scale=wd_plane[:, b, t, :],
-                                rhs=codes[:, b, edges].bitcast(FP8X4),
-                                rhs_scale=h_plane[:, b, edges],
-                                start=(b == 0), stop=(b == PASSES - 1),
-                            )
+                    for b in range(PASSES):
+                        nc.tensor.matmul_mx(
+                            y[:, s, :],
+                            lhsT=wd_dealt[:, b, t, :].bitcast(FP4X4),
+                            lhsT_scale=wd_plane[:, b, t, :],
+                            rhs=codes[:, b, :].bitcast(FP8X4),
+                            rhs_scale=h_plane[:, b, :],
+                            start=(b == 0), stop=(b == PASSES - 1),
+                        )
                 nc.scalar.copy(msgs[:, bank * slots : (bank + 1) * slots, c * CHUNK : (c + 1) * CHUNK], y[:])
 
         def clear_page(t, pool, **place):
@@ -305,19 +301,28 @@ def tile_list_msg_tanh_gateP_kernel(
             )
 
         clear_page(0, laid, offset=page_at[0])
-        early_gates = [(0, 0, CHUNKS)]
+        early_gates = [(0, 0, CHUNKS), (1, 0, CHUNKS)]
         gather_gates(keep.tile([P, gate_columns(early_gates)], F32, name="picked", align_bytes=64), early_gates)
+        sums(0, 0)
+        sums(0, 1)
+        hidden(0, 0)
         for c in range(CHUNKS):
-            sums(c)
-            for b in range(PASSES):
-                hidden(c, b)
-            weave(c)
+            hidden(c, 1)
+            weave(c, 0)
+            if 0 < c < LAST_CHUNK:
+                sums(c + 1, 0)
+            weave(c, 1)
             quantise(c)
+            if c == 0:
+                sums(c + 1, 0)
+            if c < LAST_CHUNK:
+                sums(c + 1, 1)
+                hidden(c + 1, 0)
             messages(c, 1 if c == LAST_CHUNK else 2)
             if c == 0:
                 clear_page(1, laid, offset=page_at[1])
                 clear_page(2, laid, offset=page_at[2])
-                clear_page(LAST_PAGE, keep, tag="codes0")
+                clear_page(LAST_PAGE, keep, tag="got0")
             got = laid.tile(
                 [P, gate_columns(held_gates[c])], F32, name="picked%d" % c, offset=rows_at[c], align_bytes=64
             )

@@ -58,8 +58,8 @@ def tile_list_msg_tanh_gateP_kernel(
         words_at = [free_byte, free_byte + PAGE_BYTES]
         words_at.extend(words_at[1] + WORD_BYTES + i * PAGE_BYTES for i in range(2))
         page_at[0] = words_at[3] + PAGE_BYTES
-        wd_at = page_at[0] + PAGE_BYTES
-        words_room = [4 * PAGE_BYTES + WORD_BYTES + 4096, WORD_BYTES, PAGE_BYTES, 2 * PAGE_BYTES]
+        sm_at = page_at[0] + PAGE_BYTES
+        words_room = [4 * PAGE_BYTES + WORD_BYTES + 64, WORD_BYTES, PAGE_BYTES, 2 * PAGE_BYTES]
 
         src_list = keep.tile([P, J // 16], U16, name="src_list")
         dst_list = keep.tile([P, J // 16], U16, name="dst_list")
@@ -99,12 +99,17 @@ def tile_list_msg_tanh_gateP_kernel(
         load_plane(wt_plane, wt_scales, nc.scalar)
         nc.sync.dma_start(wt_w[0][:], wt_src[:, :, :BANK])
         nc.sync.dma_start(wt_w[1][:], wt_src[:, :, BANK:])
+        wd_w = keep.tile([P, PASSES, 2 * N], U8, name="wd_w", align_bytes=64)
+        nc.sync.dma_start(wd_w[:].bitcast(I32), wd_words.rearrange("a p c -> p a c").bitcast(I32))
 
         ident = keep.tile([P, P], F32, name="ident")
         make_identity(nc, ident[:])
         edge_weight = keep.tile([P, J], F32, name="edge_weight", align_bytes=64)
         weight_rows = keep.tile([P, J // P], F32, name="weight_rows")
         nc.gpsimd.dma_start(weight_rows[:], wgo[0].rearrange("(p i) -> p i", p=P))
+        wd_rows = keep.tile([P, PASSES, N], U8, name="wd_rows", align_bytes=64)
+        nc.gpsimd.memset(wd_rows[:].rearrange("p a n -> p (a n)").bitcast(I32), 0)
+        load_plane(wd_rows, wd_scales, nc.gpsimd)
         for half in range(2):
             spread = psum.tile([P, PACK, P], F32, name="spread", tag="turn%d" % half)
             for i in range(PACK):
@@ -160,15 +165,10 @@ def tile_list_msg_tanh_gateP_kernel(
 
         gather_scales(0, 2, nc.scalar, keep, tag="got0")
         gather_words(0)
-        sm_t = laid.tile([P, PASSES, PACK], F32, name="sm_t", offset=wd_at + 3072)
+        sm_t = laid.tile([P, PASSES, PACK], F32, name="sm_t", offset=sm_at)
         nc.sync.dma_start(sm_t[:], sm.rearrange("(b p t) -> p b t", b=PASSES, t=PACK))
         load_gates(laid, offset=words_at[0])
         load_gates(keep, tag="got0")
-        wd_w = laid.tile([P, PASSES, 2 * N], U8, name="wd_w", offset=wd_at, align_bytes=64)
-        nc.sync.dma_start(wd_w[:].bitcast(I32), wd_words.rearrange("a p c -> p a c").bitcast(I32))
-        wd_rows = laid.tile([P, PASSES, N], U8, name="wd_rows", offset=wd_at + 2048, align_bytes=64)
-        nc.gpsimd.memset(wd_rows[:].rearrange("p a n -> p (a n)").bitcast(I32), 0)
-        load_plane(wd_rows, wd_scales, nc.sync)
         gather_words(1)
         gather_scales(2, 2, nc.sync, laid, offset=words_at[1])
         for c in (2, 3):
@@ -176,9 +176,12 @@ def tile_list_msg_tanh_gateP_kernel(
             load_gates(laid, offset=words_at[c])
 
         wd_dealt = keep.tile([P, PASSES, PACK, 2 * P], U8, name="wd_dealt", align_bytes=64)
-        nc.vector.tensor_copy(wd_dealt[:].bitcast(U16), wd_w[:].bitcast(U16).rearrange("p a (m t) -> p a t m", t=PACK))
-        wd_plane = keep.tile([P, PASSES, PACK, P], U8, name="wd_plane", align_bytes=64)
-        nc.vector.tensor_copy(wd_plane[:], wd_rows[:].rearrange("p a (m t) -> p a t m", t=PACK))
+        nc.scalar.copy(
+            wd_dealt[:].bitcast(U16).rearrange("p a t m -> p a m t"),
+            wd_w[:].bitcast(U16).rearrange("p a (m t) -> p a m t", t=PACK),
+        )
+        wd_plane = keep.tile([P, PASSES, PACK, P], U8, name="wd_plane", tag="second1", align_bytes=64)
+        nc.gpsimd.tensor_copy(wd_plane[:], wd_rows[:].rearrange("p a (m t) -> p a t m", t=PACK))
 
         tanhs = {}
         h_rows = {}

@@ -59,7 +59,7 @@ def tile_list_msg_tanh_gateP_kernel(
         words_at.extend(words_at[1] + WORD_BYTES + i * PAGE_BYTES for i in range(2))
         page_at[0] = words_at[3] + PAGE_BYTES
         sm_at = page_at[0] + PAGE_BYTES
-        words_room = [4 * PAGE_BYTES + WORD_BYTES + 64, WORD_BYTES, PAGE_BYTES, 2 * PAGE_BYTES]
+        words_room = [4 * PAGE_BYTES + WORD_BYTES + 64, WORD_BYTES, PAGE_BYTES, PAGE_BYTES + PAGE_BYTES // 2]
 
         src_list = keep.tile([P, J // 16], U16, name="src_list")
         dst_list = keep.tile([P, J // 16], U16, name="dst_list")
@@ -99,8 +99,6 @@ def tile_list_msg_tanh_gateP_kernel(
         load_plane(wt_plane, wt_scales, nc.scalar)
         nc.sync.dma_start(wt_w[0][:], wt_src[:, :, :BANK])
         nc.sync.dma_start(wt_w[1][:], wt_src[:, :, BANK:])
-        wd_w = keep.tile([P, PASSES, 2 * N], U8, name="wd_w", align_bytes=64)
-        nc.sync.dma_start(wd_w[:].bitcast(I32), wd_words.rearrange("a p c -> p a c").bitcast(I32))
 
         ident = keep.tile([P, P], F32, name="ident")
         make_identity(nc, ident[:])
@@ -167,6 +165,8 @@ def tile_list_msg_tanh_gateP_kernel(
         gather_words(0)
         sm_t = laid.tile([P, PASSES, PACK], F32, name="sm_t", offset=sm_at)
         nc.sync.dma_start(sm_t[:], sm.rearrange("(b p t) -> p b t", b=PASSES, t=PACK))
+        wd_w = laid.tile([P, PASSES, 2 * N], U8, name="wd_w", offset=page_at[0] + PAGE_BYTES // 2, align_bytes=64)
+        nc.sync.dma_start(wd_w[:].bitcast(I32), wd_words.rearrange("a p c -> p a c").bitcast(I32))
         load_gates(laid, offset=words_at[0])
         load_gates(keep, tag="got0")
         gather_words(1)
@@ -176,10 +176,7 @@ def tile_list_msg_tanh_gateP_kernel(
             load_gates(laid, offset=words_at[c])
 
         wd_dealt = keep.tile([P, PASSES, PACK, 2 * P], U8, name="wd_dealt", align_bytes=64)
-        nc.scalar.copy(
-            wd_dealt[:].bitcast(U16).rearrange("p a t m -> p a m t"),
-            wd_w[:].bitcast(U16).rearrange("p a (m t) -> p a m t", t=PACK),
-        )
+        nc.vector.tensor_copy(wd_dealt[:].bitcast(U16), wd_w[:].bitcast(U16).rearrange("p a (m t) -> p a t m", t=PACK))
         wd_plane = keep.tile([P, PASSES, PACK, P], U8, name="wd_plane", tag="second1", align_bytes=64)
         nc.gpsimd.tensor_copy(wd_plane[:], wd_rows[:].rearrange("p a (m t) -> p a t m", t=PACK))
 

@@ -46,7 +46,7 @@ def tile_list_msg_tanh_gateP_kernel(
         laid = ctx.enter_context(tc.tile_pool(name="laid", bufs=1))
         psum = ctx.enter_context(tc.psum_pool(name="psum", bufs=1))
 
-        held_gates = [[(2, 0, 3)], [(3, 0, 1)], [(3, 1, 1)], [(3, 2, 2), (2, 3, 1)]]
+        held_gates = [[(2, 0, 4)], [(3, 0, 1)], [(3, 1, 3)]]
 
         rows_at = [c * 5120 for c in range(CHUNKS)]
         free_byte = CHUNKS * 5120
@@ -270,32 +270,32 @@ def tile_list_msg_tanh_gateP_kernel(
                     picked[t, c + i] = (got, first + i * CHUNK)
                 first = first + count * CHUNK
 
-        def messages(c, slots):
+        def messages(c, first_slot, slots, bank):
             codes, h_plane = h_quantised[c]
-            for bank in range(PACK // slots):
-                y = psum.tile([P, slots, CHUNK], F32, name="y", tag="sum%d" % (PACK - PACK // slots + bank))
-                for s in range(slots):
-                    t = bank * slots + s
-                    for b in range(PASSES):
-                        nc.tensor.matmul_mx(
-                            y[:, s, :],
-                            lhsT=wd_dealt[:, b, t, :].bitcast(FP4X4),
-                            lhsT_scale=wd_plane[:, b, t, :],
-                            rhs=codes[:, b, :].bitcast(FP8X4),
-                            rhs_scale=h_plane[:, b, :],
-                            start=(b == 0), stop=(b == PASSES - 1),
-                        )
-                nc.scalar.copy(msgs[:, bank * slots : (bank + 1) * slots, c * CHUNK : (c + 1) * CHUNK], y[:])
+            y = psum.tile([P, slots, CHUNK], F32, name="y", tag="sum%d" % bank)
+            for s in range(slots):
+                t = first_slot + s
+                for b in range(PASSES):
+                    nc.tensor.matmul_mx(
+                        y[:, s, :],
+                        lhsT=wd_dealt[:, b, t, :].bitcast(FP4X4),
+                        lhsT_scale=wd_plane[:, b, t, :],
+                        rhs=codes[:, b, :].bitcast(FP8X4),
+                        rhs_scale=h_plane[:, b, :],
+                        start=(b == 0), stop=(b == PASSES - 1),
+                    )
+            return y
 
         def clear_page(t, pool, **place):
             pages[t] = pool.tile([P, T], F32, name="page%d" % t, align_bytes=64, **place)
             nc.gpsimd.memset(pages[t][:].bitcast(I32), 0)
 
-        def scatter(t, c, count=1):
+        def scatter(t, c, values):
+            count = values.shape[1] // CHUNK
             gate, first = picked[t, c]
             nc.vector.tensor_tensor(
                 pages[t][:].indirect(dst_list[:, c * LIST_COLS : (c + count) * LIST_COLS]),
-                msgs[:, t, c * CHUNK : (c + count) * CHUNK],
+                values,
                 gate[:, first : first + count * CHUNK],
                 MULT,
             )
@@ -306,19 +306,22 @@ def tile_list_msg_tanh_gateP_kernel(
         sums(0, 0)
         sums(0, 1)
         hidden(0, 0)
-        for c in range(CHUNKS):
+        for c in range(LAST_CHUNK):
+            edges = slice(c * CHUNK, (c + 1) * CHUNK)
             hidden(c, 1)
             weave(c, 0)
-            if 0 < c < LAST_CHUNK:
+            if c > 0:
                 sums(c + 1, 0)
             weave(c, 1)
             quantise(c)
             if c == 0:
                 sums(c + 1, 0)
-            if c < LAST_CHUNK:
-                sums(c + 1, 1)
-                hidden(c + 1, 0)
-            messages(c, 1 if c == LAST_CHUNK else 2)
+            sums(c + 1, 1)
+            hidden(c + 1, 0)
+            nc.scalar.copy(msgs[:, :2, edges], messages(c, 0, 2, 2)[:])
+            waiting = messages(c, 2, 2, 3)
+            if c < LAST_CHUNK - 1:
+                nc.scalar.copy(msgs[:, 2:, edges], waiting[:])
             if c == 0:
                 clear_page(1, laid, offset=page_at[1])
                 clear_page(2, laid, offset=page_at[2])
@@ -327,11 +330,25 @@ def tile_list_msg_tanh_gateP_kernel(
                 [P, gate_columns(held_gates[c])], F32, name="picked%d" % c, offset=rows_at[c], align_bytes=64
             )
             gather_gates(got, held_gates[c])
-            if 0 < c < LAST_CHUNK:
-                scatter(LAST_PAGE, c - 1)
-            for t in range(LAST_PAGE):
-                scatter(t, c)
-        scatter(LAST_PAGE, LAST_CHUNK - 1, 2)
+            if c > 0:
+                scatter(LAST_PAGE, c - 1, msgs[:, LAST_PAGE, (c - 1) * CHUNK : c * CHUNK])
+            for t in range(LAST_PAGE if c < LAST_CHUNK - 1 else 2):
+                scatter(t, c, msgs[:, t, edges])
+
+        c = LAST_CHUNK
+        hidden(c, 1)
+        for b in range(PASSES):
+            weave(c, b)
+        quantise(c)
+        late = laid.tile([P, 2, 2 * CHUNK], F32, name="late", offset=rows_at[c], align_bytes=64)
+        nc.scalar.copy(late[:, :, :CHUNK], waiting[:])
+        scatter(2, c - 1, late[:, 0, :CHUNK])
+        for t in range(PACK):
+            into = msgs[:, t, c * CHUNK :] if t < 2 else late[:, t - 2, CHUNK:]
+            nc.scalar.copy(into, messages(c, t, 1, t)[:, 0, :])
+            if t < LAST_PAGE:
+                scatter(t, c, into)
+        scatter(LAST_PAGE, c - 1, late[:, 1, :])
 
         out_rows = out_0.rearrange("(p t) c -> p t c", t=PACK)
         o_rows = keep.tile([P, PACK, T], BF16, name="o_rows", align_bytes=64)

from contextlib import ExitStack

import concourse.mybir as mybir
from concourse.masks import make_identity

K, R, N, T, J = 1024, 1024, 512, 2048, 1024
FLOPS = 2 * J * (2 * K * R + R * N)

F32 = mybir.dt.float32
BF16 = mybir.dt.bfloat16
I32 = mybir.dt.int32
U32 = mybir.dt.uint32
U16 = mybir.dt.uint16
U8 = mybir.dt.uint8
FP8X4 = mybir.dt.float8_e4m3fn_x4
FP4X4 = mybir.dt.float4_e2m1fn_x4
ACT = mybir.ActivationFunctionType
MULT = mybir.AluOpType.mult

P = 128
PACK = 4
PASSES = 2
BANK = 512
CHUNK = 256
CHUNKS = J // CHUNK
EDGE_TILES = CHUNK // P
LIST_COLS = CHUNK // 16
SCALE_ROW = 48
LAST_PAGE = PACK - 1
LAST_CHUNK = CHUNKS - 1
PIECES = (512, 512, 512, 256, 256)
VECTOR_COLS = 1152
PAGE_BYTES = 4 * T
WORD_BYTES = 2 * 4 * CHUNK
HIDDEN_BYTES = 2 * PASSES * CHUNK * PACK


def tile_list_msg_tanh_gateP_kernel(
    tc, tab_words, tab_scales, ws_words, ws_scales, wt_words, wt_scales, sm,
    wd_words, wd_scales, gT, wgo, offs, offs2, out_0, out_1, out_2,
):
    nc = tc.nc
    with ExitStack() as ctx:
        keep = ctx.enter_context(tc.tile_pool(name="keep", bufs=1))
        ring = ctx.enter_context(tc.tile_pool(name="ring", bufs=2))
        laid = ctx.enter_context(tc.tile_pool(name="laid", bufs=1))
        psum = ctx.enter_context(tc.psum_pool(name="psum", bufs=1))

        held_gates = [[(2, 0, 4)], [(3, 0, 1)], [(3, 1, 3)]]

        rows_at = [c * 5120 for c in range(CHUNKS)]
        free_byte = CHUNKS * 5120
        page_at = {1: free_byte, 2: free_byte + PAGE_BYTES}
        hidden_at = [page_at[2] - HIDDEN_BYTES // 2]
        free_byte = free_byte + 2 * PAGE_BYTES
        hidden_at.extend(free_byte + (i % 2) * HIDDEN_BYTES for i in range(LAST_CHUNK))
        free_byte = free_byte + 2 * HIDDEN_BYTES
        words_at = [free_byte, free_byte + PAGE_BYTES]
        words_at.extend(words_at[1] + WORD_BYTES + i * PAGE_BYTES for i in range(2))
        page_at[0] = words_at[3] + PAGE_BYTES
        sm_at = page_at[0] + PAGE_BYTES
        words_room = [4 * PAGE_BYTES + WORD_BYTES + 64, WORD_BYTES, PAGE_BYTES, PAGE_BYTES + PAGE_BYTES // 2]

        src_list = keep.tile([P, J // 16], U16, name="src_list")
        dst_list = keep.tile([P, J // 16], U16, name="dst_list")
        lists = (src_list, dst_list)

        def load_plane(plane, plane_src, queue):
            for quad in range(4):
                queue.dma_start(
                    plane[32 * quad : 32 * quad + 4].bitcast(I32),
                    plane_src[:, 4 * quad : 4 * quad + 4, :].rearrange("a q c -> q a c").bitcast(I32),
                )

        def interleave(copy, words, rows):
            copy(words.rearrange("p (c i) t -> p c t i", i=4), rows.rearrange("p t (c i) -> p c t i", i=4))

        ws_plane = keep.tile([P, PASSES, R], U8, name="ws_plane", align_bytes=64)
        nc.vector.memset(ws_plane[:].rearrange("p a r -> p (a r)").bitcast(I32), 0)
        wt_plane = keep.tile([P, PASSES, R], U8, name="wt_plane", align_bytes=64)
        nc.vector.memset(wt_plane[:].rearrange("p a r -> p (a r)").bitcast(I32), 0)
        tab_rows = keep.tile([P, T // 4], I32, name="tab_rows", align_bytes=64)
        for first, end in ((0, SCALE_ROW), (SCALE_ROW + 16, SCALE_ROW + 32), (SCALE_ROW + 48, P)):
            nc.vector.memset(tab_rows[first:end, :], 0)
        nc.sync.dma_start(src_list[:], offs)
        nc.sync.dma_start(dst_list[:], offs2)
        tab_rows_src = tab_scales.rearrange("a (u x r) t -> x (a u) r t", x=2, r=4).bitcast(I32)
        for x in range(2):
            nc.sync.dma_start(tab_rows[SCALE_ROW + 32 * x : SCALE_ROW + 32 * x + 16, :], tab_rows_src[x])
        tab_w = keep.tile([P, T], I32, name="tab_w", align_bytes=64)
        nc.sync.dma_start(tab_w[:], tab_words[0].rearrange("p t i -> p (t i)").bitcast(I32))

        ws_all = keep.tile([P, PASSES, BANK], I32, name="ws_all", align_bytes=64)
        ws_w = [ws_all[:, :, b * BANK // 2 : (b + 1) * BANK // 2] for b in range(PASSES)]
        wt_w = [keep.tile([P, PASSES, BANK], I32, name="wt_w%d" % b, align_bytes=64) for b in range(PASSES)]
        wt_src = wt_words.rearrange("a p r i -> p a (r i)").bitcast(I32)
        nc.sync.dma_start(ws_all[:], ws_words.rearrange("a p c -> p a c").bitcast(I32))
        load_plane(ws_plane, ws_scales, nc.sync)
        load_plane(wt_plane, wt_scales, nc.scalar)
        nc.sync.dma_start(wt_w[0][:], wt_src[:, :, :BANK])
        nc.sync.dma_start(wt_w[1][:], wt_src[:, :, BANK:])

        ident = keep.tile([P, P], F32, name="ident")
        make_identity(nc, ident[:])
        edge_weight = keep.tile([P, J], F32, name="edge_weight", align_bytes=64)
        weight_rows = keep.tile([P, J // P], F32, name="weight_rows")
        nc.gpsimd.dma_start(weight_rows[:], wgo[0].rearrange("(p i) -> p i", p=P))
        wd_rows = keep.tile([P, PASSES, N], U8, name="wd_rows", align_bytes=64)
        nc.gpsimd.memset(wd_rows[:].rearrange("p a n -> p (a n)").bitcast(I32), 0)
        load_plane(wd_rows, wd_scales, nc.gpsimd)
        for half in range(2):
            spread = psum.tile([P, PACK, P], F32, name="spread", tag="turn%d" % half)
            for i in range(PACK):
                column = half * PACK + i
                nc.tensor.transpose(
                    spread[:, i, :], weight_rows[:, column : column + 1].to_broadcast([P, P]), ident[:]
                )
            nc.scalar.copy(
                edge_weight[:].rearrange("m (p i) -> m p i", p=P)[:, :, half * PACK : (half + 1) * PACK],
                spread[:].rearrange("m i p -> m p i"),
            )

        v_plane = {}
        v_words = []

        def gather_scales(c, count, queue, pool, **place):
            got = pool.tile([P, 2, count * CHUNK], U8, name="got%d" % c, align_bytes=64, **place)
            for l in range(2):
                offsets = lists[l][:, c * LIST_COLS : (c + count) * LIST_COLS]
                nc.vector.tensor_copy(got[:, l, :], tab_rows[:].bitcast(U8).indirect(offsets))
            plane = keep.tile([P, PASSES, 2, count * CHUNK], U8, name="v_plane%d" % c, align_bytes=64)
            for a in range(PASSES):
                for u in range(2):
                    first = SCALE_ROW + 8 * a + 4 * u
                    queue.dma_start(
                        plane[64 * u : 64 * u + 64, a].rearrange("p l j -> p (l j)").bitcast(I32),
                        got[first : first + 64].rearrange("p l j -> p (l j)").bitcast(I32),
                    )
            for i in range(count):
                v_plane[c + i] = (plane, i * CHUNK)

        def gather_words(c):
            room = laid.tile([P, words_room[c] // 4], U32, name="both%d" % c, offset=words_at[c], align_bytes=64)
            second = keep.tile([P, CHUNK], U32, name="second%d" % c, align_bytes=64)
            both = (room[:, :CHUNK], second[:])
            parted = keep.tile([P, 2, PASSES, 2 * CHUNK], U8, name="parted%d" % c, align_bytes=64)
            for l in range(2):
                offsets = lists[l][:, c * LIST_COLS : (c + 1) * LIST_COLS]
                nc.vector.tensor_copy(both[l], tab_w[:].bitcast(U32).indirect(offsets))
            for l in range(2):
                nc.vector.tensor_copy(
                    parted[:, l].bitcast(U16), both[l].bitcast(U16).rearrange("p (j a) -> p a j", a=PASSES)
                )
            v_words.append(parted)

        gT_rows = gT.rearrange("(p t) c -> p t c", t=PACK)
        gate_windows = []

        def load_gates(pool, **place):
            t = len(gate_windows)
            gate_windows.append(pool.tile([P, T], F32, name="gates%d" % t, align_bytes=64, **place))
            nc.sync.dma_start(gate_windows[t][:], gT_rows[:, t, :])

        gather_scales(0, 2, nc.scalar, keep, tag="got0")
        gather_words(0)
        sm_t = laid.tile([P, PASSES, PACK], F32, name="sm_t", offset=sm_at)
        nc.sync.dma_start(sm_t[:], sm.rearrange("(b p t) -> p b t", b=PASSES, t=PACK))
        wd_w = laid.tile([P, PASSES, 2 * N], U8, name="wd_w", offset=page_at[0] + PAGE_BYTES // 2, align_bytes=64)
        nc.sync.dma_start(wd_w[:].bitcast(I32), wd_words.rearrange("a p c -> p a c").bitcast(I32))
        load_gates(laid, offset=words_at[0])
        load_gates(keep, tag="got0")
        gather_words(1)
        gather_scales(2, 2, nc.sync, laid, offset=words_at[1])
        for c in (2, 3):
            gather_words(c)
            load_gates(laid, offset=words_at[c])

        wd_dealt = keep.tile([P, PASSES, PACK, 2 * P], U8, name="wd_dealt", align_bytes=64)
        nc.vector.tensor_copy(wd_dealt[:].bitcast(U16), wd_w[:].bitcast(U16).rearrange("p a (m t) -> p a t m", t=PACK))
        wd_plane = keep.tile([P, PASSES, PACK, P], U8, name="wd_plane", tag="second1", align_bytes=64)
        nc.gpsimd.tensor_copy(wd_plane[:], wd_rows[:].rearrange("p a (m t) -> p a t m", t=PACK))

        tanhs = {}
        h_rows = {}
        h_words = {}
        h_quantised = {}
        picked = {}
        pages = {}
        msgs = keep.tile([P, PACK, J], F32, name="msgs", align_bytes=64)

        def sums(c, b):
            plane, plane_first = v_plane[c]
            for e in range(EDGE_TILES):
                tanh = ring.tile([P, PACK, P], F32, name="tanh", bufs=2 * PASSES * EDGE_TILES)
                edge_scales = slice(plane_first + e * P, plane_first + (e + 1) * P)
                edge_bytes = slice(2 * e * P, 2 * (e + 1) * P)
                acc = psum.tile([P, BANK], F32, name="acc", tag="sum%d" % (EDGE_TILES * b + e))
                r_cols = slice(b * BANK, (b + 1) * BANK)
                for a in range(PASSES):
                    nc.tensor.matmul_mx(
                        acc[:],
                        lhsT=v_words[c][:, 0, a, edge_bytes].bitcast(FP4X4),
                        lhsT_scale=plane[:, a, 0, edge_scales],
                        rhs=ws_w[b][:, a, :].bitcast(FP4X4),
                        rhs_scale=ws_plane[:, a, r_cols],
                        start=(a == 0), stop=False,
                    )
                    nc.tensor.matmul_mx(
                        acc[:],
                        lhsT=v_words[c][:, 1, a, edge_bytes].bitcast(FP4X4),
                        lhsT_scale=plane[:, a, 1, edge_scales],
                        rhs=wt_w[b][:, a, :].bitcast(FP8X4),
                        rhs_scale=wt_plane[:, a, r_cols],
                        start=False, stop=(a == PASSES - 1),
                    )
                nc.scalar.activation(tanh[:], acc[:].rearrange("p (m t) -> p t m", t=PACK), ACT.Tanh)
                tanhs[c, e, b] = tanh

        def hidden(c, b):
            if b == 0:
                h_rows[c] = laid.tile(
                    [P, PACK, PASSES * CHUNK], BF16, name="h_rows%d" % c, offset=rows_at[c], align_bytes=64
                )
            for pair in range(2):
                turned = psum.tile([P, 2, CHUNK], F32, name="turned", tag="turn%d" % (2 * b + pair))
                for s in range(2):
                    for e in range(EDGE_TILES):
                        nc.tensor.transpose(
                            turned[:, s, e * P : (e + 1) * P], tanhs[c, e, b][:, 2 * pair + s, :], ident[:]
                        )
                for s in range(2):
                    t = 2 * pair + s
                    nc.scalar.activation(
                        h_rows[c][:, t, b * CHUNK : (b + 1) * CHUNK], turned[:, s, :],
                        ACT.Copy, scale=sm_t[:, b, t : t + 1],
                    )

        def weave(c, b):
            if b == 0:
                h_words[c] = laid.tile(
                    [P, PASSES, CHUNK, PACK], BF16, name="h_words%d" % c, offset=hidden_at[c], align_bytes=64
                )
            interleave(nc.scalar.copy, h_words[c][:, b], h_rows[c][:, :, b * CHUNK : (b + 1) * CHUNK])

        def quantise(c):
            tag = "got0" if c == 0 else "codes%d" % c
            codes = keep.tile([P, PASSES, CHUNK], U32, name="codes", tag=tag, align_bytes=64)
            h_plane = keep.tile([P, PASSES, CHUNK], U8, name="h_plane%d" % c, align_bytes=64)
            nc.vector.quantize_mx(
                codes[:].rearrange("p b j -> p (b j)").bitcast(FP8X4),
                h_plane[:].rearrange("p b j -> p (b j)"),
                h_words[c][:].rearrange("p b j t -> p (b j t)"),
            )
            h_quantised[c] = (codes, h_plane)

        def gate_columns(units):
            return CHUNK * sum(count for t, c, count in units)

        def gather_gates(got, units):
            first = 0
            for t, c, count in units:
                offsets = src_list[:, c * LIST_COLS : (c + count) * LIST_COLS]
                nc.vector.tensor_tensor(
                    got[:, first : first + count * CHUNK],
                    gate_windows[t][:].indirect(offsets),
                    edge_weight[:, c * CHUNK : (c + count) * CHUNK],
                    MULT,
                )
                for i in range(count):
                    picked[t, c + i] = (got, first + i * CHUNK)
                first = first + count * CHUNK

        def messages(c, first_slot, slots, bank):
            codes, h_plane = h_quantised[c]
            y = psum.tile([P, slots, CHUNK], F32, name="y", tag="sum%d" % bank)
            for s in range(slots):
                t = first_slot + s
                for b in range(PASSES):
                    nc.tensor.matmul_mx(
                        y[:, s, :],
                        lhsT=wd_dealt[:, b, t, :].bitcast(FP4X4),
                        lhsT_scale=wd_plane[:, b, t, :],
                        rhs=codes[:, b, :].bitcast(FP8X4),
                        rhs_scale=h_plane[:, b, :],
                        start=(b == 0), stop=(b == PASSES - 1),
                    )
            return y

        def clear_page(t, pool, **place):
            pages[t] = pool.tile([P, T], F32, name="page%d" % t, align_bytes=64, **place)
            nc.gpsimd.memset(pages[t][:].bitcast(I32), 0)

        def scatter(t, c, values):
            count = values.shape[1] // CHUNK
            gate, first = picked[t, c]
            nc.vector.tensor_tensor(
                pages[t][:].indirect(dst_list[:, c * LIST_COLS : (c + count) * LIST_COLS]),
                values,
                gate[:, first : first + count * CHUNK],
                MULT,
            )

        clear_page(0, laid, offset=page_at[0])
        early_gates = [(0, 0, CHUNKS), (1, 0, CHUNKS)]
        gather_gates(keep.tile([P, gate_columns(early_gates)], F32, name="picked", align_bytes=64), early_gates)
        sums(0, 0)
        sums(0, 1)
        hidden(0, 0)
        for c in range(LAST_CHUNK):
            edges = slice(c * CHUNK, (c + 1) * CHUNK)
            hidden(c, 1)
            weave(c, 0)
            if c > 0:
                sums(c + 1, 0)
            weave(c, 1)
            quantise(c)
            if c == 0:
                sums(c + 1, 0)
            sums(c + 1, 1)
            hidden(c + 1, 0)
            nc.scalar.copy(msgs[:, :2, edges], messages(c, 0, 2, 2)[:])
            waiting = messages(c, 2, 2, 3)
            if c < LAST_CHUNK - 1:
                nc.scalar.copy(msgs[:, 2:, edges], waiting[:])
            if c == 0:
                clear_page(1, laid, offset=page_at[1])
                clear_page(2, laid, offset=page_at[2])
                clear_page(LAST_PAGE, keep, tag="got0")
            got = laid.tile(
                [P, gate_columns(held_gates[c])], F32, name="picked%d" % c, offset=rows_at[c], align_bytes=64
            )
            gather_gates(got, held_gates[c])
            if c > 0:
                scatter(LAST_PAGE, c - 1, msgs[:, LAST_PAGE, (c - 1) * CHUNK : c * CHUNK])
            for t in range(LAST_PAGE if c < LAST_CHUNK - 1 else 2):
                scatter(t, c, msgs[:, t, edges])

        c = LAST_CHUNK
        hidden(c, 1)
        for b in range(PASSES):
            weave(c, b)
        quantise(c)
        late = laid.tile([P, 2, 2 * CHUNK], F32, name="late", offset=rows_at[c], align_bytes=64)
        nc.scalar.copy(late[:, :, :CHUNK], waiting[:])
        scatter(2, c - 1, late[:, 0, :CHUNK])
        for t in range(PACK):
            into = msgs[:, t, c * CHUNK :] if t < 2 else late[:, t - 2, CHUNK:]
            nc.scalar.copy(into, messages(c, t, 1, t)[:, 0, :])
            if t < LAST_PAGE:
                scatter(t, c, into)
        scatter(LAST_PAGE, c - 1, late[:, 1, :])

        out_rows = out_0.rearrange("(p t) c -> p t c", t=PACK)
        o_rows = keep.tile([P, PACK, T], BF16, name="o_rows", align_bytes=64)
        for t in range(PACK):
            nc.sync.dma_start(out_rows[:, t, :], pages[t][:])
            if t < LAST_PAGE:
                nc.scalar.copy(o_rows[:, t, :], pages[t][:])
            else:
                for first, end in ((0, PIECES[0]), (PIECES[0], VECTOR_COLS)):
                    nc.vector.tensor_copy(o_rows[:, t, first:end], pages[t][:, first:end])
                nc.scalar.copy(o_rows[:, t, VECTOR_COLS:], pages[t][:, VECTOR_COLS:])

        o_plane = keep.tile([P, BANK], U8, name="o_plane", align_bytes=64)
        out_words = out_1[0].rearrange("p t i -> p (t i)").bitcast(I32)
        firsts = [sum(PIECES[:i]) for i in range(len(PIECES))]
        o_words = []

        def weave_piece(i):
            first, width = firsts[i], PIECES[i]
            words = keep.tile([P, width, PACK], BF16, name="o_words%d" % i, align_bytes=64)
            split = min(max(VECTOR_COLS - first, 0), width)
            if split < width:
                interleave(nc.scalar.copy, words[:, split:, :], o_rows[:, :, first + split : first + width])
            if split > 0:
                interleave(nc.vector.tensor_copy, words[:, :split, :], o_rows[:, :, first : first + split])
            o_words.append(words)

        def store_piece(i):
            first, width = firsts[i], PIECES[i]
            o_codes = keep.tile([P, width], I32, name="o_codes%d" % i, align_bytes=64)
            nc.vector.quantize_mx(
                o_codes[:].bitcast(FP8X4), o_plane[4 * (first // BANK) :, first % BANK : first % BANK + width], o_words[i][:].rearrange("p c t -> p (c t)")
            )
            nc.sync.dma_start(out_words[:, first : first + width], o_codes[:])

        weave_piece(0)
        for i in range(1, len(PIECES)):
            weave_piece(i)
            store_piece(i - 1)
        store_piece(len(PIECES) - 1)
        out_scales = out_2[0].rearrange("(q r) (k j) -> q k r j", r=4, k=4).bitcast(I32)
        for quad in range(4):
            (nc.sync, nc.scalar)[quad % 2].dma_start(
                out_scales[quad], o_plane[32 * quad : 32 * quad + 16, :].bitcast(I32)
            )
